import numpy as np, ml_dtypes
CORES = [13,21,141,149]
N = 4
BF = ml_dtypes.bfloat16
def gentries(a):
    return np.ascontiguousarray(a.reshape(8, 16, -1).transpose(0, 2, 1)).reshape(8, -1)
def gtable(e):
    e = np.asarray(e); return np.ascontiguousarray(e.reshape(8, -1, 16).transpose(0, 2, 1)).reshape(128, -1).astype(np.int32)
V, XW, L, RO, CAP, TH, EPS, LIM = 1008, 2048, 64, 5, 128, 88, 20, 14
def of(rng, lev, want):
    out = np.zeros(want.shape, np.int64)
    for q in range(N):
        for g in range(8):
            o = np.argsort(lev[q, g], kind="stable"); st = np.searchsorted(lev[q, g][o], np.arange(7))
            a, b = st[want[q, g]], st[want[q, g] + 1]
            out[q, g] = o[a + ((b - a) * rng.random(want[q, g].shape)).astype(np.int64)]
    return out
def parts(rng):
    lev = rng.integers(0, 5, (N, 8, XW)); lev = np.where(rng.random((N, 8, XW)) < rng.choice(np.array([0.1, 0.2, 0.35]), (N, 8, 1)), 5, lev)
    like = np.minimum(3 * lev[:, :, None, :] + rng.integers(0, 3, (N, 8, 16, 1)) + (rng.random((N, 8, 16, XW)) * rng.integers(1, 5, (N, 8, 1, XW))).astype(np.int64), 15)
    x = np.where(lev[:, :, None, :] == 5, rng.integers(0, 16, (N, 8, 16, XW)), like)
    own = lev[:, :, :V]; keep = rng.random((N, 8, V, 8)) < rng.choice(np.array([0.4, 0.75, 0.95]), (N, 8, V, 1))
    s = of(rng, own, np.where(keep, own[..., None], rng.integers(0, 6, (N, 8, V, 8))))
    p = np.where(rng.random((N, 8, V, 1)) < 0.12, of(rng, lev, np.zeros((N, 8, V, 8), np.int64)), rng.integers(0, XW, (N, 8, V, 8)))
    e = np.ascontiguousarray(np.concatenate([p, s], axis=3).transpose(0, 1, 3, 2))
    v = rng.integers(0, V, (N, 8, L)); v = np.where(rng.random((N, 8, L)) < 0.2, np.take_along_axis(v, rng.integers(0, L, (N, 8, L)), 2), v)
    return e, x, v, rng.integers(0, 256, (N, 8, 16))
def pack(e, x, v, w):
    return {"e0": np.ascontiguousarray(e).reshape(N, 128, V).astype(np.int32), "x0": np.ascontiguousarray(x).reshape(N, 128, XW).astype(np.float32).astype(BF),
            "v0": np.stack([gtable(a) for a in v]), "wt": np.ascontiguousarray(w).reshape(N, 128, 1).astype(np.int32)}
def node(e, v, p, s):
    e[:8, v] = p; e[8:, v] = s
def place(w, c):
    u = int(np.add.reduce(w * c)) & (XW - 1)
    return ((u * u >> 5) + u) & (XW - 1)
def total(rng, s):
    o = np.full(16, s >> 4); o[rng.permutation(16)[:s & 15]] += 1; a = rng.permutation(16)
    for i in range(8):
        m = int(rng.integers(0, min(int(o[a[2 * i]]), 15 - int(o[a[2 * i + 1]])) + 1)); o[a[2 * i]] -= m; o[a[2 * i + 1]] += m
    return o
def away(rng, c, d):
    o = c.copy()
    for r in rng.permutation(16):
        k = int(c[r]); s = min(d, max(k, 15 - k)); o[r] = k + s if 15 - k >= k else k - s; d -= s
    return o
def fan(rng, e, nd, n, pr, far, fit):
    for i in range(7):
        s = np.full(8, fit); s[rng.permutation(8)[:n // 7 + int(i < n % 7)]] = far; node(e, nd[i], pr, s)
def setup_inputs(rng):
    return pack(*parts(rng))
def setup_inputs_corners(rng):
    e, x, v, w = parts(rng); w = np.maximum(w, 1); goal = (CAP, CAP + 1, CAP - 1, 0, 8 * L, 1, CAP, 8)
    for q in range(N):
        for g in range(8):
            eg, xg, wg = e[q, g], x[q, g], w[q, g]
            a1, a0 = total(rng, TH), total(rng, TH - 1); ha = place(wg, a1)
            for i in range(64):
                m1 = total(rng, TH + 40); hm = place(wg, m1)
                if hm != ha: break
            c = rng.permutation(V); c = c[(c != ha) & (c != hm)]
            cb, ca, cz, cm, cp, cf, cx = c[:7]
            xg[:, ha] = away(rng, a1, EPS + 1); xg[:, hm] = away(rng, m1, EPS)
            xg[:, cb] = 15; xg[:, ca] = a1; xg[:, cz] = a0; xg[:, cm] = m1
            xg[:, cp] = total(rng, 120); xg[:, cf] = away(rng, xg[:, cp], EPS); xg[:, cx] = away(rng, xg[:, cp], EPS + 1)
            nd = rng.permutation(V)
            for k in range(9):
                node(eg, nd[k], np.where(rng.permutation(8) < k, ca, rng.choice(np.array([cm, cz]), 8)), rng.integers(0, V, 8))
            node(eg, nd[9], cz, rng.integers(0, V, 8)); node(eg, nd[10], cm, cp)
            fan(rng, eg, nd[11:18], LIM, cm, cx, cf); fan(rng, eg, nd[18:25], LIM + 1, cm, cx, cf)
            at = nd[25:25 + L]; n = goal[(q + g) % 8]
            kind = rng.choice(np.array([0, 9, 10, 11]), L); kind[:n // 8] = 8
            if n % 8: kind[n // 8] = n % 8
            kind = rng.permutation(kind)
            for l in range(L):
                k = int(kind[l])
                s = np.full(8, nd[k]) if k < 10 else np.concatenate([nd[10:11], nd[11:18] if k == 10 else nd[18:25]])
                node(eg, at[l], cb, s)
            v[q, g] = at
    return pack(e, x, v, w)
def setup_inputs_crowd(rng):
    e, x, v, w = parts(rng); w = np.maximum(w, 1); w[2, 4] = 0
    for q in range(N):
        for g in range(8):
            eg, xg, wg = e[q, g], x[q, g], w[q, g]
            h = place(wg, np.full(16, 15)); c = XW // 4 + rng.permutation(V - XW // 4); c = c[c != h]
            cb, cp, cq = c[:3]; dd = c[3:11]; na, nb, nc, turn, hold = c[11:16]; lo = rng.integers(0, 4, 16)
            xg[:, h] = 0; xg[:, cb] = 15; xg[:, cp] = lo; xg[:, dd] = lo[:, None]; xg[:, cq] = rng.integers(12, 16, 16)
            node(eg, na, cb, dd); node(eg, nb, cb, cq); node(eg, nc, cb, c[16:24])
            node(eg, turn, cb, np.array([na] + 7 * [nb])); node(eg, hold, cb, nc)
            node(eg, dd[0], cb, cp); fan(rng, eg, dd[1:], LIM + 7, cb, cq, cp)
            o = np.full(L, hold); any2 = rng.integers(0, V, 2); k = (q + g) % 6
            if q < 2:
                o[:] = turn
                if q == 1 and g == 7: o[L - 1] = hold
            elif k == 1: o[L - 1] = turn
            elif k == 2: o[rng.integers(0, L)] = any2[0]
            elif k == 3: o = rng.choice(np.array([turn, hold, any2[0], any2[1]]), L)
            elif k == 4: o[:] = any2[0]
            elif k == 5: o[:] = any2[0]; o[0] = any2[1]
            v[q, g] = o
    return pack(e, x, v, w)
def tips(rng, n, shape, a, b):
    r = rng.random(shape)
    return np.where(r < a, 0, np.where(r < a + b, n - 1, rng.integers(0, n, shape)))
def setup_inputs_ends(rng):
    pops = np.array([0, 4, 7, 10, 13, 16]); lev = rng.integers(0, 6, (N, 8, XW)); row = np.argsort(rng.random((N, 8, 16)), axis=-1)
    lev[..., 0] = np.where(np.arange(8) % 2 == 0, 4, 1); lev[..., V - 1] = 2; lev[..., XW - 1] = 5
    flip = (rng.random((N, 8, 1, XW)) < 0.5) & (np.arange(16)[:, None] == rng.integers(0, 16, (N, 8, 1, XW))); flip[..., [0, V - 1, XW - 1]] = False
    x = 15 * ((row[..., None] < pops[lev][:, :, None, :]) ^ flip).astype(np.int64)
    e = np.concatenate([tips(rng, XW, (N, 8, 8, V), 0.45, 0.45), tips(rng, V, (N, 8, 8, V), 0.45, 0.35)], axis=2)
    v = tips(rng, V, (N, 8, L), 0.35, 0.45); w = 255 * rng.integers(0, 2, (N, 8, 16)); w[:, 7] = 255
    for q in range(N):
        node(e[q, 7], V - 1, XW - 1, 0); node(e[q, 7], 0, XW - 1, np.array([V - 1, 0] * 4)); v[q, 7] = V - 1
        x[q, 7, :, place(w[q, 7], np.full(16, 15))] = 0
        node(e[q, 6], V - 2, XW - 1, np.array([V - 3] + [V - 4] * 7)); node(e[q, 6], V - 3, XW - 1, 0); node(e[q, 6], V - 4, XW - 1, V - 1)
        v[q, 6, 0] = V - 2; v[q, 6, L - 2:] = V - 2
    return pack(e, x, v, w)
def setup_inputs_quiet(rng):
    e, x, v, w = parts(rng); w = np.maximum(w, 1)
    for q in range(N):
        few = rng.permutation(8 * L).reshape(8, L) < 7 + 8 * int(rng.integers(0, L))
        for g in range(8):
            eg, xg = e[q, g], x[q, g]
            for i in range(64):
                h = place(w[q, g], np.full(16, 15))
                if h >= XW // 4: break
                w[q, g] = rng.integers(1, 256, 16)
            c = XW // 4 + rng.permutation(V - XW // 4); c = c[c != h]
            cb, cz = c[:2]; xg[:, h] = 0; xg[:, cb] = 15; xg[:, cz] = 0
            if q % 2 == 0:
                z, asks, mids = c[2:10], c[10:18], c[18:26]; y1, y2, y3, ask0, mid0, ask4 = c[26:32]
                for k in range(8):
                    node(eg, z[k], cz, rng.choice(z, 8)); node(eg, asks[k], cb, mids[k]); node(eg, mids[k], cb, np.roll(z, k))
                node(eg, ask0, cb, mid0); node(eg, mid0, cb, y1); node(eg, y1, cz, y2); node(eg, y2, cz, y3); node(eg, y3, cz, ask4); node(eg, ask4, cb, mids[0])
                v[q, g] = asks[rng.integers(0, 8, L)]; v[q, g, int(rng.integers(1, CAP // 8))] = ask0
            else:
                cp, cq, na, nb, turn, first, idle = c[2:9]; dd = c[9:17]; lo = rng.integers(0, 4, 16)
                xg[:, cp] = lo; xg[:, dd] = lo[:, None]; xg[:, na] = lo; xg[:, nb] = lo; xg[:, cq] = rng.integers(12, 16, 16)
                node(eg, na, cb, dd); node(eg, nb, cb, cq); node(eg, dd[0], cb, cp); fan(rng, eg, dd[1:], LIM + 7, cb, cq, cp)
                node(eg, turn, cb, np.array([nb] + 7 * [na])); node(eg, first, cb, np.array([turn] + 7 * [nb])); node(eg, idle, cz, turn)
                v[q, g] = np.where(few[g], first, idle)
    return pack(e, x, v, w)
def setup_inputs_spread(rng):
    full = rng.random((N, 8, 1, XW)) < rng.choice(np.array([0.3, 0.6, 1.0]), (N, 8, 1, 1))
    x = np.minimum((rng.random((N, 8, 16, XW)) * np.where(full, 16, rng.integers(1, 17, (N, 8, 1, XW)))).astype(np.int64), 15)
    s = np.minimum((V * rng.random((N, 8, 8, V)) ** rng.choice(np.array([1.0, 2.0]), (N, 8, 1, 1))).astype(np.int64), V - 1)
    e = np.concatenate([rng.integers(0, XW, (N, 8, 8, V)), s], axis=2)
    v = np.minimum((V * rng.random((N, 8, L)) ** rng.choice(np.array([1.0, 3.0]), (N, 8, 1))).astype(np.int64), V - 1)
    w = np.minimum(np.exp2(8 * rng.random((N, 8, 16))).astype(np.int64) - 1, 255)
    return pack(e, x, v, w)
def check_inputs(d):
    bad = []
    for k, lo, hi in (("e0", 0, XW - 1), ("x0", 0, 15), ("v0", 0, V - 1), ("wt", 0, 255)):
        a = np.asarray(d[k]).astype(np.float64)
        if not np.all((a >= lo) & (a <= hi)): bad.append("range of " + k)
    if np.max(np.asarray(d["e0"]).reshape(-1, 16, V)[:, 8:]) >= V: bad.append("range of the subs in e0")
    a = np.asarray(d["x0"]).astype(np.float32)
    if np.any(a != np.floor(a)): bad.append("whole numbers in x0")
    return bad
def reference(e0, x0, v0, wt):
    M = 8 * N
    E = np.ascontiguousarray(e0.reshape(M, 16, V).transpose(0, 2, 1)).astype(np.int64)
    X = np.ascontiguousarray(x0.astype(np.float32).reshape(M, 16, XW).transpose(0, 2, 1)).astype(np.int32)
    v = np.stack([gentries(a) for a in v0]).reshape(M, L).astype(np.int64); w = wt.reshape(M, 1, 1, 16).astype(np.int32)
    k = np.arange(M); k1, k2, k3 = k[:, None], k[:, None, None], k[:, None, None, None]
    A = np.zeros((M, 1), np.int64); lower = np.arange(L)[None, :] < np.arange(L)[:, None]
    for t in range(RO):
        c = E[k1, v]; p, s = c[..., :8], c[..., 8:]
        c = E[k2, s]; pp, ss = c[..., :8], c[..., 8:]
        m = np.minimum(X[k2, p][:, :, :, None, :], X[k3, pp])
        alive = np.add.reduce(m, axis=4) >= TH
        full = np.any(alive, axis=2); first = np.argmax(alive, axis=2)
        sub = np.take_along_axis(ss, first[:, :, None, :], 2)[:, :, 0]
        far = np.add.reduce(np.abs(X[k3, ss] - X[k2, sub][:, :, None]), axis=4) > EPS
        pi = np.max(np.where((alive & ~far)[..., None], m, 0), axis=2)
        stand = np.add.reduce((alive & far).astype(np.int64), axis=(2, 3)) <= LIM + (A & 7)
        u = np.add.reduce(w * pi, axis=3).astype(np.int64) & (XW - 1); h = ((u * u >> 5) + u) & (XW - 1)
        known = np.add.reduce(np.abs(X[k2, h] - pi), axis=3) <= EPS
        new = XW // 4 * (t & 3) + np.arange(8 * L).reshape(L, 8); name = np.where(known, h, new)
        ask = stand[:, :, None] & full & ~known
        one = ask.reshape(M, 8 * L).astype(np.int64); before = (np.add.accumulate(one, axis=1) - one).reshape(M, L, 8)
        k4 = (k // 8 + 1 + t % (N - 1)) % N * 8 + k % 8
        got = X[k4[:, None, None], h]
        val = np.where((ask & (before < CAP))[..., None], (pi + got) >> 1, pi)
        best = np.argmax(np.where(full, np.add.reduce(pi, axis=3), -1), axis=2)
        go = np.where(stand & np.any(full, axis=2), np.take_along_axis(sub, best[..., None], 2)[..., 0], s[:, :, t])
        lead = stand & ~np.any((v[:, :, None] == v[:, None, :]) & stand[:, None, :] & lower, axis=2)
        pair = np.concatenate([np.where(full, name, p), np.where(full, sub, s)], axis=2)
        a, l = np.nonzero(lead); E[a, v[a, l]] = pair[a, l]
        a, l, j = np.nonzero(ask); X[a, new[l, j]] = val[a, l, j]
        A = np.repeat(np.add.reduce((~stand).reshape(N, 8 * L).astype(np.int64), axis=1), 8)[:, None]; v = go
    return {"ye": np.ascontiguousarray(E.transpose(0, 2, 1)).reshape(N, 128, V).astype(np.float32),
            "yx": np.ascontiguousarray(X.transpose(0, 2, 1)).reshape(N, 128, XW).astype(np.float32).astype(BF),
            "yv": np.stack([gtable(a) for a in v.reshape(N, 8, L)]).astype(np.float32)}

@@ -1,0 +1,642 @@
+import numpy as np
+from concourse.mybir import dt, AluOpType, AxisListType, ActivationFunctionType
+
+A = AluOpType
+F = ActivationFunctionType
+V, XW, RO = 1008, 2048, 5
+SC = 8192.0
+KA = 87.5 * SC
+KD = 20.0 * SC
+BIG = float(2 ** 30)
+
+CFG = {
+    "ch": (8, 8, 8, 8),
+    "bc": ("vvvvvvv", "vvvvvvg", "vvvvggg", "vvvgggg"),
+    "fb": (),
+    "tp": (32,),
+    "hd": (8, 24), "n2": "vs", "xp": "ssss", "fin": 12, "av": ("ssv", "ssv"), "tries": 5000, "seed": 2, "heat": 600.0, "xs": 4, "fv": (2, 4), "xe": "ssssssss",
+    "lat": 70.0, "pe": 0.55, "ga": 1.56, "so": 30.0,
+}
+
+
+def _sb(n, d):
+    return ("sbuf", [128] + (n if isinstance(n, list) else [n]), d)
+
+
+F32, B16, F16, I32, U16 = "float32", "bfloat16", "float16", "int32", "uint16"
+SCRATCH = {
+    "ei": _sb(V, I32), "ef": _sb(V + 64, F32), "X": _sb(XW, B16),
+    "vi": _sb(4, I32), "wi": _sb(1, I32), "vu": _sb(4, U16), "vF": _sb(4, F32),
+    "N1": _sb(64, F16), "L": _sb(64, U16), "pcsc": _sb(64, F32), "XpB": _sb(4096, B16), "N2": _sb(512, F16),
+    "pU": _sb(256, U16), "sU": _sb(224, U16), "sK": _sb(256, F32), "m": _sb(4096, B16), "Xs": _sb(3584, B16),
+    "Y": _sb(256, F32), "dead": _sb(256, B16), "sc1": _sb(256, F32), "subU": _sb(32, U16), "Xsub": _sb(512, B16),
+    "absd": _sb(3584, B16), "pen": _sb(256, B16), "SO": _sb([256, 16], B16), "FS": _sb(1024, B16),
+    "hI": _sb(128, I32), "hU": _sb(32, U16), "dk": _sb(512, B16), "ak": _sb(512, B16),
+    "ask": _sb(32, B16), "cum": _sb(32, B16), "ad": _sb(32, F16), "bp": _sb(64, F16),
+    "sm": _sb(512, F32), "stT": _sb(32, B16), "aU": _sb(32, U16), "bU": _sb(32, U16),
+    "ga": _sb(512, B16), "gb": _sb(512, B16), "gc2": _sb(512, B16), "pair": _sb(64, F32),
+    "key": _sb(96, F32), "goI": _sb(8, I32), "goF": _sb(4, F32), "goH": _sb(16, F16),
+    "z": _sb(64, F32), "zj": _sb(544, F32), "fs": _sb(32, F32), "soff": _sb(4, U16), "aI": _sb(2, I32), "thr": _sb(2, F32),
+    "val": _sb(128 * 5, B16), "ix": _sb(160, B16), "ci": _sb(8, I32), "cc": _sb(32, F32),
+    "PM": _sb(128 * 8, F16), "ID": _sb(128 * 4, B16), "ST": _sb(128 * 16, B16), "BK": _sb(128 * 7, B16),
+    "B8": _sb(144, B16), "Bw": _sb(144, B16), "G": _sb(160, F16), "rst": _sb(256, B16), "one": _sb(32, B16),
+    "nn": _sb(96, F32), "i64": _sb(V, F32), "lrow": _sb(64, F32),
+    "pa": ("psum", [128, 512], F32), "pb": ("psum", [128, 512], F32),
+    "pc0": ("psum", [128, 2, 32, 8], F32), "pc1": ("psum", [128, 2, 32, 8], F32),
+    "pd0": ("psum", [128, 4, 8, 16], F32), "pd1": ("psum", [128, 4, 8, 16], F32),
+    "pf0": ("psum", [128, 512], F32), "pf1": ("psum", [128, 512], F32),
+}
+for _t in range(RO):
+    SCRATCH["W%d" % _t] = _sb(3584, B16)
+
+
+def messages():
+    out = [(0, 1024 * w, 1024 * w + 1024, -1) for w in range(2)]
+    out.append((1, 512, 2048, -1))
+    for t in range(1, RO):
+        out.append((t, 512 * t - 512, 512 * t, t - 1))
+        if t + 1 < RO:
+            out.append((t + 1, 0, 512 * t, t - 1))
+            if t < 3:
+                out.append((t + 1, 512 * t + 512, 2048, t - 1))
+    return out
+
+
+MSG = messages()
+SEMAPHORES = (["cv", "cs", "cp", "cg"] + ["d%d" % k for k in range(16)] + ["arr%d" % t for t in range(RO)]
+              + ["hop%d" % k for k in range(len(MSG))] + ["ls%d" % k for k in range(len(MSG))])
+
+
+def bits(x):
+    return bin(x).count("1")
+
+
+def route(T, topo, rank, t):
+    n = len(T.cores)
+    src, dst = T.cores[rank], T.cores[(rank - 1 - t % (n - 1)) % n]
+    if topo.may_write(src, dst):
+        return dst, None
+    can = [c for c in topo.cores_of(src) if T.rank_of(c) is None and topo.may_write(c, dst)]
+    near = [c for c in can if topo.die(c) == topo.die(src)]
+    return dst, (near or can)[0]
+
+
+def helper_program(g, core, T, topo):
+    for rank in range(len(T.cores)):
+        mine = [(k, x, route(T, topo, rank, x[0])[0]) for k, x in enumerate(MSG) if route(T, topo, rank, x[0])[1] == core]
+        for k, (t, a, b, _), dst in mine:
+            g.wait_ge(T.sem["hop%d" % k], bits(topo.mask(T.cores[rank], core)))
+            rid, pid = topo.addr(dst, core)
+            w = T["W%d" % t]
+            g.remote_dma(w[:, a:b], w[:, a:b], T.sem["arr%d" % t], T.sem["ls%d" % k], pid, rid, topo.mask(core, dst))
+        for k, _, dst in mine:
+            g.wait_ge(T.sem["ls%d" % k], bits(topo.mask(core, dst)))
+
+
+def plan_once(ops, succ, pr, look):
+    eng, cost, left = ops
+    n = len(eng)
+    left = list(left)
+    ready = {e: [] for e in eng}
+    for i in range(n):
+        if not left[i]:
+            ready[eng[i]].append(i)
+    est = [0.0] * n
+    at = [0.0] * n
+    free = {e: 0.0 for e in ready}
+    soon = {e: 0.0 for e in ready if ready[e]}
+    order = []
+    while soon:
+        e = min(soon, key=soon.get)
+        now, q = soon[e], ready[e]
+        i = q[0]
+        if len(q) > 1:
+            i = max([k for k in q if est[k] <= now], key=pr.get)
+            by = now + min(0.5 * cost[i], look[i])
+            i = max([k for k in q if est[k] <= by], key=pr.get)
+        q.remove(i)
+        at[i] = max(now, est[i])
+        f = free[e] = at[i] + cost[i]
+        order.append(i)
+        if q:
+            soon[e] = max(f, min([est[k] for k in q]))
+        else:
+            del soon[e]
+        for s, lag in succ[i]:
+            if f + lag > est[s]:
+                est[s] = f + lag
+            left[s] -= 1
+            if not left[s]:
+                x = eng[s]
+                ready[x].append(s)
+                soon[x] = min(soon.get(x, 1e18), max(est[s], free[x]))
+    return order, at
+
+
+def plan(ops):
+    n = len(ops)
+    succ = [[] for _ in ops]
+    for i, o in enumerate(ops):
+        for d, wait in o["dep"].items():
+            near = ops[d]["eng"] == o["eng"] and not wait
+            succ[d].append((i, 0.0 if near else ops[d]["lag"] + (0.0 if ops[d]["eng"] == "n" else CFG["lat"])))
+    pr = [0.0] * n
+    for i in range(n - 1, -1, -1):
+        pr[i] = ops[i]["cost"] + max([pr[s] + lag for s, lag in succ[i]] + [ops[i]["lag"]])
+    names = sorted(set(o["kind"] for o in ops))
+    cls = [names.index(o["kind"]) for o in ops]
+    flat = ([o["eng"] for o in ops], [o["cost"] for o in ops], [len(o["dep"]) for o in ops])
+
+    def run(off, look):
+        order, at = plan_once(flat, succ, {i: pr[i] + off[cls[i]] for i in range(n)}, [look[c] for c in cls])
+        return max(at[i] + o["cost"] + o["lag"] for i, o in enumerate(ops)), order, at
+    rng = np.random.default_rng(CFG["seed"])
+    off, look = [0.0] * len(names), [250.0] * len(names)
+    best = cur = run(off, look)
+    for it in range(CFG["tries"]):
+        o2, l2 = list(off), list(look)
+        for _ in range(int(rng.integers(1, 9))):
+            k = int(rng.integers(0, len(names)))
+            o2[k] += float(rng.normal(0.0, 1500.0))
+            l2[k] = float(rng.choice([0.0, 150.0, 400.0, 900.0]))
+        got = run(o2, l2)
+        if got[0] <= cur[0] + CFG["heat"] * (1.0 - it / CFG["tries"]) * float(rng.random()):
+            cur, off, look = got, o2, l2
+            best = min(best, got)
+    for o, x in zip(ops, best[2]):
+        o["at"] = x
+    return best[1], best[0]
+
+
+def build(T, topo, core, rank):
+    ops = []
+    lastw, readers, bank, seen = {}, {}, {}, {}
+    nd = [0]
+    PE, GA, SO = CFG["pe"], CFG["ga"], CFG["so"]
+
+    def add(eng, cost, fn, r=(), w=(), pk=(), lag=0.0, sem=None):
+        i = len(ops)
+        dep = {}
+        w = list(w) + (["pe" + k for k in pk] if eng == "p" else [])
+        for k in r:
+            if k in lastw:
+                dep[lastw[k]] = True
+        for k in w:
+            for d in readers.get(k, []) + ([lastw[k]] if k in lastw else []):
+                dep[d] = dep.get(d, False) or not (eng == "p" or k in ("sendq", "ldq"))
+        for k in pk:
+            who, cur, prev = bank.get(k, (None, [], []))
+            if who != eng:
+                cur, prev = [], cur
+            for d in prev:
+                dep.setdefault(d, False)
+            bank[k] = (eng, cur + [i], prev)
+        for k in r:
+            readers.setdefault(k, []).append(i)
+        for k in w:
+            lastw[k] = i
+            readers[k] = []
+        dep.pop(i, None)
+        seen[w[0]] = seen.get(w[0], 0) + 1
+        ops.append({"eng": eng, "cost": float(cost), "fn": fn, "dep": dep, "lag": float(lag), "sem": sem, "w": w,
+                    "kind": "%s.%d" % (w[0], seen[w[0]])})
+
+    def vc(n, half=False):
+        return max(64.0, n * (0.5 if half else 1.0))
+
+    def ts(out, a, s1, s2, o0, o1, n, r, w, pk=(), half=False):
+        if o1 is None:
+            add("v", vc(n, half), lambda e: e.tensor_scalar(out, a, s1, None, o0), r, w, pk)
+        else:
+            add("v", vc(n, half), lambda e: e.tensor_scalar(out, a, s1, s2, o0, o1), r, w, pk)
+
+    def tt(out, a, b, o, n, r, w, pk=()):
+        add("v", vc(n * (1 if pk else 2)), lambda e: e.tensor_tensor(out, a, b, o), r, w, pk)
+
+    def act(out, a, f, n, r, w, pk=(), **kw):
+        add("s", SO + vc(n), lambda e: e.activation(out, a, f, **kw), r, w, pk)
+
+    def cp(eng, out, a, n, r, w, pk=(), half=False):
+        if eng == "v":
+            add("v", vc(n, half), lambda e: e.tensor_copy(out, a), r, w, pk)
+        elif eng == "s":
+            act(out, a, F.Copy, n, r, w, pk)
+        else:
+            add("g", 205 + 2 * n, lambda e: e.affine_select(out, a, [[0, n]], A.is_ge, 0.0, 0, 0), r, w, pk)
+
+    def aff(eng, out, a, scale, bias, n, r, w, half=False, pk=()):
+        if eng == "v":
+            ts(out, a, scale, bias, A.mult, A.add, n, r, w, pk, half=half)
+        else:
+            act(out, a, F.Identity, n, r, w, pk, bias=bias, scale=scale)
+
+    def scan(out, d0, d1, ini, op1, cost, r, w, pk=()):
+        add("v", max(64, cost), lambda e: e.tensor_tensor_scan(out, d0, d1, ini, A.mult, op1), r, w, pk)
+
+    def gat(eng, out, win, off, n, r, w, in1=None, o=None):
+        if in1 is not None:
+            add("v", 60 + GA * n, lambda e: e.tensor_tensor(out, win.indirect(off), in1, o), r, w)
+        elif eng == "v":
+            add("v", 60 + GA * n, lambda e: e.tensor_copy(out, win.indirect(off)), r, w)
+        else:
+            add("s", 80 + GA * n, lambda e: e.activation(out, win.indirect(off), F.Copy), r, w)
+
+    def mm(groups, r, w, pk, first=True, last=True):
+        def fn(e):
+            ins = None
+            for grp in groups:
+                for k, (o, l, x, _) in enumerate(grp):
+                    ins = e.matmul(o, l, x, first and k == 0, last and k == len(grp) - 1)
+            return ins
+        add("p", PE * sum(max(64, x[3]) for grp in groups for x in grp), fn, r, w, pk, lag=60)
+
+    def dma(eng, out, a, nbytes, r, w):
+        s = "d%d" % nd[0]
+        nd[0] += 1
+        add(eng, 80, lambda e: e.dma_start(out, a), r, w, lag=2000 + nbytes / 200.0, sem=(s, 16))
+
+    def iota(out, pat, cm, n, w):
+        add("g", 160 + 2 * n, lambda e: e.iota(out, pat, 0, cm, allow_small_or_imprecise_dtypes=True), (), w)
+
+    def fill(ap, x, w):
+        add("v", 64, lambda e: e.memset(ap, x), (), w)
+
+    XK = ["X0", "X1", "X2", "X3"]
+    Xw = T.X[:, 0:XW]
+    cc = T.cc
+
+    def col(k):
+        return cc[:, k:k + 1]
+
+    def mat(buf, k):
+        return buf[:, 128 * k:128 * k + 128]
+
+    dma("s", T.vi[:], T.v0[:], 2048, (), ["vi"])
+    dma("y", T.ei[:], T.e0[:], 516096, (), ["ei", "ldq"])
+    dma("y", T.X[:], T.x0[:], 2 * 524288, (), XK + ["ldq"])
+    dma("s", T.wi[:], T.wt[:], 512, (), ["wi"])
+
+    add("g", 162, lambda e: e.iota(T.ci[:, 0:1], [[0, 1]], 0, 1), (), ["p"])
+    iota(mat(T.val, 0), [[16, 8], [-1, 8], [128, 2]], -1, 128, ["val0"])
+    iota(mat(T.val, 1), [[16, 8], [128, 2], [1, 8]], -1, 128, ["val1"])
+    iota(T.ix[:], [[1, 160]], 0, 160, ["ix"])
+    iota(mat(T.val, 2), [[1, 128]], -1, 128, ["val2"])
+    iota(mat(T.val, 3), [[16, 8], [0, 16]], -1, 128, ["val3"])
+    iota(mat(T.val, 4), [[8, 16], [0, 8]], 0, 128, ["val4"])
+    iota(T.lrow[:], [[1, 64]], 0, 64, ["lrow"])
+    iota(T.i64[:], [[64, V]], 0, V, ["i64"])
+    for b in range(2):
+        for k, (x, off) in enumerate(((0, 7), (0, 15), (1, 0), (1, 8))):
+            ts(mat(T.PM, 2 * k + b), mat(T.val, x), 128.0 * b - off, None, A.is_equal, None, 128, ["val%d" % x], ["PM%d%d" % (k, b)], half=True)
+    LP, LS, PC, SB = [[mat(T.PM, 2 * k + b) for b in range(2)] for k in range(4)]
+    KL, KC = ["PM00", "PM01", "PM10", "PM11"], ["PM20", "PM21", "PM30", "PM31"]
+    for k, mask in enumerate((112, 120, 15, 7, 96)):
+        ts(T.ci[:, k + 1:k + 2], T.ci[:, 0:1], mask, None, A.bitwise_and, None, 1, ["p"], ["ci%d" % k])
+    ts(T.ci[:, 6:7], T.ci[:, 0:1], 3, 3, A.arith_shift_right, A.bitwise_and, 1, ["p"], ["ci5"])
+    cp("v", cc[:, 0:7], T.ci[:, 0:7], 7, ["p"] + ["ci%d" % k for k in range(6)], ["cc"])
+    aff("s", col(7), col(1), 1.0, 15.0, 1, ["cc"], ["c7"])
+    aff("s", col(11), col(5), 1.0, 17.0, 1, ["cc"], ["c11"])
+    aff("s", col(8), col(4), 2.0, col(11), 1, ["cc", "c11"], ["c8"])
+    aff("s", col(9), col(4), -1024.0, 8192.0 - KA + KD, 1, ["cc"], ["c9"])
+    cp("v", col(10), T.wi[:], 1, ["wi"], ["c10"])
+    ts(cc[:, 12:16], T.ix[:, 0:4], col(6), None, A.is_equal, None, 4, ["cc", "ix"], ["qm"])
+    ts(cc[:, 16:24], T.ix[:, 0:8], col(4), None, A.is_equal, None, 8, ["cc", "ix"], ["jm"])
+    ts(T.B8[:], T.ix[:, 0:144], col(7), SC, A.is_equal, A.mult, 144, ["c7", "ix"], ["B8"], half=True)
+    ts(T.Bw[:], T.ix[:, 0:144], col(7), col(10), A.is_equal, A.mult, 144, ["c7", "c10", "ix"], ["Bw"], half=True)
+    ts(T.G[:], T.ix[:], col(8), None, A.is_equal, None, 160, ["c8", "ix"], ["G"], half=True)
+    for k, x in enumerate((1.0, -1.0, 2.0 ** 22, -2.0 ** 22)):
+        ts(mat(T.ID, k), mat(T.val, 2), 0.0, x, A.is_equal, A.mult, 128, ["val2"], ["ID%d" % k], half=True)
+    IDp, IDn, I22, N22 = [mat(T.ID, k) for k in range(4)]
+    for r in range(16):
+        ts(mat(T.ST, r), mat(T.val, 3), float(-r), None, A.is_equal, None, 128, ["val3"], ["ST%d" % r], half=True)
+    ts(mat(T.BK, 0), mat(T.val, 4), col(2), -1.0 / 16, A.is_equal, A.mult, 128, ["val4", "cc"], ["BK0"], half=True)
+    ts(mat(T.BK, 1), mat(T.val, 4), col(2), -1.0, A.is_equal, A.mult, 128, ["val4", "cc"], ["BK1"], half=True)
+    ts(mat(T.BK, 5), mat(T.val, 3), col(0), col(1), A.add, A.is_equal, 128, ["val3", "cc"], ["BK5"], half=True)
+    aff("s", mat(T.BK, 2), mat(T.BK, 5), 4096.0, 0.0, 128, ["BK5"], ["BK2"])
+    ts(mat(T.BK, 6), mat(T.val, 2), 0.0, -4096.0, A.is_lt, A.mult, 128, ["val2"], ["BK6"], half=True)
+    tt(mat(T.BK, 3), mat(T.BK, 6), mat(T.BK, 5), A.mult, 128, ["BK6", "BK5"], ["BK3"])
+    fill(mat(T.BK, 4), 2.0 ** -33, ["BK4"])
+    fill(T.one[:], 1.0, ["one"])
+    fill(T.thr[:, 0:1], 14.0, ["thr"])
+    fill(T.ef[:, V:V + 64], 0.0, ["efd"])
+    fill(T.rst[:], 1.0, ["rst1"])
+    aff("s", T.rst[:, 0:256:8], T.one[:], 0.0, 0.0, 32, ["one", "rst1"], ["rst"])
+    aff("s", T.nn[:, 0:32], T.ix[:, 0:32], 16.0, col(3), 32, ["ix", "cc"], ["nn"])
+    aff("s", T.nn[:, 32:36], T.nn[:, 0:4], 1.0, float(V), 4, ["nn"], ["dump"])
+    cp("v", T.vu[:], T.vi[:], 4, ["vi"], ["vu"])
+    cp("v", T.vF[:], T.vi[:], 4, ["vi"], ["vF"])
+    for k in range(2):
+        cp("v", T.ef[:, 504 * k:504 * k + 504], T.ei[:, 504 * k:504 * k + 504], 504, ["ei"], ["ef%d" % k])
+
+    def send(after, urgent, behind=()):
+        for k, (t, a, b, aft) in enumerate(MSG):
+            if aft != after or (t == after + 1) != urgent:
+                continue
+            dst, via = route(T, topo, rank, t)
+            to = dst if via is None else via
+            rid, pid = topo.addr(to, core)
+            mask = topo.mask(core, to)
+            rs = T.sem["arr%d" % t] if via is None else T.sem["hop%d" % k]
+
+            def fn(e, k=k, t=t, a=a, b=b, rs=rs, pid=pid, rid=rid, mask=mask):
+                e.remote_dma(T["W%d" % t][:, a:b], T.X[:, a:b], rs, T.sem["ls%d" % k], pid, rid, mask)
+                return None
+            add("g", 1000, fn, XK[a // 512:b // 512] + list(behind), ["sendq", "msg%d" % k], lag=(3000 + (b - a) * 4.0) * (2 - (t % 3 == 1)),
+                sem=("ls%d" % k, bits(mask)))
+
+    def arrivals(t):
+        n = len(T.cores)
+        src = (rank + 1 + t % (n - 1)) % n
+        via = route(T, topo, src, t)[1]
+        return bits(topo.mask(T.cores[src] if via is None else via, core)) * sum(1 for x in MSG if x[0] == t)
+
+    def bview(buf, r):
+        return buf[:, 15 - r:143 - r]
+
+    def pieces(sizes):
+        out, c = [], 0
+        for k, n in enumerate(sizes):
+            out.append((k, c, n))
+            c += n
+        return out
+
+    CH, TP = pieces(CFG["ch"]), pieces(CFG["tp"])
+
+    def keys(name, c0, nc):
+        return [name + str(h) for h, a, n in CH if a < c0 + nc and c0 < a + n]
+
+    send(-1, True)
+    sm, hI = T.sm, T.hI
+    for t in range(RO):
+        W = T["W%d" % t]
+        wk = t % 4
+        EK = ["ei"] if t == 0 else ["ef0", "ef1", "efd"]
+        Ew = T.ei[:, 0:V] if t == 0 else T.ef[:, 0:V]
+        XR, OLD = "XR%d" % t, "old%d" % t
+        seen.clear()
+        add("x%d" % t, 0, None, ["msg%d" % k for k, x in enumerate(MSG) if x[0] == t], [XR], sem=("arr%d" % t, arrivals(t)))
+        dma("y", W[:, 2048:2560], T.X[:, 512 * wk:512 * wk + 512], 131072, [XK[wk]], [OLD])
+        gat("v", T.N1[:], Ew, T.vu[:, 0:4], 64, EK + ["vu"], ["N1"])
+        mm([[(T.pa[:, 32:64], LS[b], T.N1[:, b:64:2], 32) for b in range(2)],
+            [(T.pa[:, 0:32], LP[b], T.N1[:, b:64:2], 32) for b in range(2)]], ["N1"] + KL, ["paL"], ["pa"])
+        cp("v", T.L[:], T.pa[:, 0:64], 64, ["paL"], ["L"], ["pa"])
+        mm([[(T.pb[:, 128:160], PC[b], T.N1[:, b:64:2], 32) for b in range(2)],
+            [(T.pb[:, 160:192], SB[b], T.N1[:, b:64:2], 32) for b in range(2)]], ["N1"] + KC, ["pbC"], ["pb"])
+        cp("s", T.pcsc[:], T.pb[:, 128:192], 64, ["pbC"], ["pcsc"], ["pb"])
+        gat("v", T.z[:], T.i64[:, 0:V], T.vu[:, 0:4], 64, ["i64", "vu", "lrow"], ["z"], T.lrow[:], A.add)
+        aff("s", T.fs[:, 0:4], T.vF[:], -64.0, 0.5, 4, ["vF"], ["nlo"])
+        tt(T.fs[:, 4:8], T.fs[:, 0:4], T.nn[:, 0:4], A.subtract, 4, ["nlo", "nn"], ["nhi"])
+        for q in range(8):
+            act(T.zj[:, 64 * q:64 * q + 64], T.z[:], F.Sign, 90, ["z", "nlo", "nhi"], ["cn%d" % q], bias=T.fs[:, q:q + 1], accum_out=T.fs[:, 8 + q:9 + q])
+        tt(T.fs[:, 16:20], T.fs[:, 8:12], T.fs[:, 12:16], A.subtract, 4, ["cn%d" % q for q in range(8)], ["f1"])
+        aff("s", T.fs[:, 20:24], T.fs[:, 16:20], 1024.0, 0.0, 4, ["f1"], ["f2"])
+        tt(T.fs[:, 24:28], T.fs[:, 20:24], T.vF[:], A.add, 4, ["f2", "vF"], ["f3"])
+        tt(T.fs[:, 28:32], T.fs[:, 24:28], T.nn[:, 32:36], A.min, 4, ["f3", "dump"], ["f4"])
+        cp("v", T.soff[:], T.fs[:, 28:32], 4, ["f4"], ["soff"])
+        aff("s", sm[:, 0:32], T.pcsc[:, 32:64], col(16 + t), 0.0, 32, ["pcsc", "jm"], ["fb"])
+        aff("s", T.nn[:, 64:96], T.nn[:, 0:32], 1.0, 512.0 * wk, 32, ["nn"], ["nw"])
+        nf = 0
+        for h, c0, nc in CH:
+            H = str(h)
+            e0, e1 = 128 * c0, 128 * (c0 + nc)
+            gat(CFG["xp"][h], T.XpB[:, e0:e1:8], Xw, T.L[:, c0:c0 + nc], 16 * nc, XK + ["L"], ["XpB0" + H])
+            for j in range(1, 8):
+                cp(CFG["bc"][h][j - 1], T.XpB[:, e0 + j:e1:8], T.XpB[:, e0:e1:8], 16 * nc, ["XpB0" + H], ["XpB%d" % j + H], half=True)
+        send(t - 1, False, ["XpB%d%d" % (j, h) for h, _, _ in CH for j in range(1, 8) if CFG["bc"][h][j - 1] == "g"])
+        for h, c0, nc in pieces(CFG["hd"]):
+            H = str(h)
+            sc, s8 = slice(c0, c0 + nc), slice(8 * c0, 8 * (c0 + nc))
+            gat("v" if t == 0 else CFG["n2"][h], T.N2[:, 16 * c0:16 * (c0 + nc)], Ew, T.L[:, 32 + c0:32 + c0 + nc], 16 * nc, EK + ["L"], ["N2" + H])
+            n2 = [T.N2[:, 16 * c0 + b:16 * (c0 + nc):2] for b in range(2)]
+            mm([[(T.pc1[:, 1, sc], SB[b], n2[b], 8 * nc) for b in range(2)]], ["N2" + H] + KC, ["ps" + H], ["pc1"])
+            mm([[(T.pf1[:, s8], PC[b], n2[b], 8 * nc) for b in range(2)]], ["N2" + H] + KC, ["pp" + H, "pf1"], ["pf1"])
+            cp("v", T.sU[:, 7 * c0:7 * (c0 + nc)], T.pc1[:, 1, sc, 0:7], 7 * nc, ["ps" + H], keys("sU", c0, nc), ["pc1"])
+            cp("v", T.pU[:, s8], T.pf1[:, s8], 8 * nc, ["pp" + H, "pf1"], keys("pU", c0, nc), ["pf1"])
+            act(T.sK[:, s8], T.pc1[:, 1, sc], F.Identity, 8 * nc, ["ps" + H], keys("sK", c0, nc), ["pc1"], bias=KA)
+        for h, c0, nc in CH:
+            H = str(h)
+            e0, e1 = 128 * c0, 128 * (c0 + nc)
+            sc = slice(c0, c0 + nc)
+            s8 = slice(8 * c0, 8 * (c0 + nc))
+            s16 = slice(16 * c0, 16 * (c0 + nc))
+            pS, pD = T.pc0[:, 0, sc], T.pc1[:, 0, sc]
+            gat("v", T.m[:, e0:e1], Xw, T.pU[:, s8], 128 * nc, XK + ["pU" + H] + ["XpB%d" % j + H for j in range(8)],
+                ["m" + H], T.XpB[:, e0:e1], A.min)
+            for a in range(c0, c0 + nc, CFG["xs"]):
+                n = min(CFG["xs"], c0 + nc - a)
+                gat(CFG["xe"][a // 4], T.Xs[:, 112 * a:112 * (a + n)], Xw, T.sU[:, 7 * a:7 * (a + n)], 112 * n, XK + ["sU" + H],
+                    ["Xs%d" % k for k in range(a // 4, (a + n) // 4)])
+            mm([[(pS, bview(T.B8, r), T.m[:, e0 + r:e1:16], 8 * nc) for r in range(16)]], ["m" + H, "B8"], ["S" + H], ["pc0"])
+            tt(T.Y[:, s8], T.sK[:, s8], pS, A.min, 8 * nc, ["sK" + H, "S" + H], ["Y" + H], ["pc0"])
+            ts(T.dead[:, s8], pS, KA, None, A.is_lt, None, 8 * nc, ["S" + H], ["dead" + H], ["pc0"])
+            scan(T.sc1[:, s8], T.dead[:, s8], T.Y[:, s8], 0.0, A.max, 8 * nc, ["Y" + H, "dead" + H], ["sc1" + H])
+            ts(T.subU[:, c0:c0 + nc], T.sc1[:, 8 * c0 + 7:8 * (c0 + nc):8], -KA, 0.0, A.add, A.max, nc, ["sc1" + H], ["subU" + H])
+            gat("s", T.Xsub[:, s16], Xw, T.subU[:, c0:c0 + nc], 16 * nc, XK + ["subU" + H], ["Xsub" + H])
+            for k in range(c0 // 4, (c0 + nc) // 4):
+                pd, dk_ = T["pd%d" % (k % 2)], ["pd%d" % (k % 2)]
+                mm([[(pd[:, :, 0:7, :], IDp, T.Xs[:, 448 * k:448 * k + 448], 448)]
+                    + [(pd[:, :, i, :], IDn, T.Xsub[:, 64 * k:64 * k + 64], 64) for i in range(7)]],
+                   ["Xs%d" % k, "Xsub" + H, "ID0", "ID1"], dk_, dk_)
+                act(T.absd[:, 448 * k:448 * k + 448], pd[:, :, 0:7, :], F.Abs, 448, dk_, ["absd%d" % k], dk_)
+            mm([[(pD, I22, T.dead[:, s8], 8 * nc)]
+                + [(T.pc1[:, 0, sc, 0:7], bview(T.B8, r), T.absd[:, 112 * c0 + r:112 * (c0 + nc):16], 7 * nc) for r in range(16)]],
+               ["dead" + H, "ID2", "B8"] + ["absd%d" % k for k in range(c0 // 4, (c0 + nc) // 4)], ["D" + H], ["pc1"])
+            ts(T.pen[:, s8], pD, KD, -16.0, A.is_gt, A.mult, 8 * nc, ["D" + H], ["pen" + H], ["pc1"])
+            per, w8 = 64 // nc, 8 * nc
+            for r0 in range(0, 16, per):
+                pf, fk = T["pf%d" % (nf % 2)], ["pf%d" % (nf % 2)]
+                rs = list(range(r0, min(16, r0 + per)))
+                fv = nf in CFG["fv"]
+                mm([[(pf[:, w8 * (r - r0):w8 * (r - r0 + 1)], IDp, T.m[:, e0 + r:e1:16], w8)][:0 if fv else 1]
+                    + [(pf[:, w8 * (r - r0):w8 * (r - r0 + 1)], mat(T.ST, r), T.pen[:, s8], w8)] for r in rs],
+                   ["m" + H, "pen" + H, "ID0"] + ["ST%d" % r for r in rs], fk, fk)
+                if fv:
+                    for r in rs:
+                        a = w8 * (r - r0)
+                        b = 512 * (CFG["fv"].index(nf) % 2) + a
+                        tt(T.FS[:, b:b + w8], T.m[:, e0 + r:e1:16], pf[:, a:a + w8], A.add, w8, ["m" + H] + fk, ["FV%d" % b], fk)
+                        scan(T.SO[:, s8, r], T.rst[:, 0:w8], T.FS[:, b:b + w8], 0.0, A.max, w8 / 2, ["rst", "FV%d" % b], ["SO%d_" % r + H])
+                    nf += 1
+                    continue
+                via = nf in CFG["fb"]
+                if via:
+                    f0 = 512 * (CFG["fb"].index(nf) % 2)
+                    fkey = ["FS%d" % f0]
+                    cp("s", T.FS[:, f0:f0 + w8 * len(rs)], pf[:, 0:w8 * len(rs)], w8 * len(rs), fk, fkey, fk)
+                for r in rs:
+                    a = w8 * (r - r0)
+                    if via:
+                        scan(T.SO[:, s8, r], T.rst[:, 0:w8], T.FS[:, f0 + a:f0 + a + w8], 0.0, A.max, w8 / 2, ["rst"] + fkey, ["SO%d_" % r + H])
+                    else:
+                        scan(T.SO[:, s8, r], T.rst[:, 0:w8], pf[:, a:a + w8], 0.0, A.max, w8, ["rst"] + fk, ["SO%d_" % r + H], fk)
+                nf += 1
+            cp("s", W[:, 2560 + 16 * c0:2560 + 16 * (c0 + nc)], T.SO[:, 8 * c0 + 7:8 * (c0 + nc):8, :], 16 * nc,
+               ["SO%d_" % r + H for r in range(16)], ["pi" + H])
+        SCK = keys("sc1", 0, 32)
+        aff("s", sm[:, 32:64], T.sc1[:, 7:256:8], 1.0, col(9), 32, SCK + ["c9"], ["base0"])
+        act(sm[:, 64:96], T.sc1[:, 7:256:8], F.Relu, 32, SCK, ["subF"], bias=-KA)
+        tt(sm[:, 96:128], sm[:, 64:96], T.pcsc[:, 32:64], A.subtract, 32, ["subF", "pcsc"], ["ds"])
+        PIK = keys("pi", 0, 32)
+        for u, c0, nc in TP:
+            U = str(u)
+
+            def cs(a):
+                return slice(a + c0, a + c0 + nc)
+            sub = [(c0, nc // 2), (c0 + nc // 2, nc // 2)] if nc >= 16 else [(c0, nc)]
+            so = T.SO
+            pn = T.pc0[:, 1, c0 // 8:(c0 + nc) // 8]
+            mm([[(pn, mat(T.BK, 1), T.dead[:, 8 * c0 + i:8 * (c0 + nc):8], nc) for i in range(8)]],
+               keys("dead", c0, nc) + ["BK1"], ["cnt" + U], ["pc0"], True, False)
+            mm([[(pn, mat(T.BK, 0), T.pen[:, 8 * c0 + i:8 * (c0 + nc):8], nc) for i in range(8)]],
+               keys("pen", c0, nc) + ["BK0"], ["cnu" + U, "cnt" + U], ["pc0"], False, True)
+            ts(T.stT[:, cs(0)], pn, T.thr[:, 0:1], BIG, A.is_gt, A.mult, nc, ["cnt" + U, "thr"], ["stT" + U], ["pc0"])
+            for q in range(4):
+                rs = range(4 * q, 4 * q + 4)
+                kk = [x for r in rs for x in keys("SO%d_" % r, c0, nc)]
+                mm([[(T.pa[:, cs(128)], bview(T.Bw, r), so[:, 8 * c0 + 7:8 * (c0 + nc):8, r], nc) for r in rs]],
+                   kk + ["Bw"], ["U" + U], ["pa"], q == 0, q == 3)
+                mm([[(T.pb[:, cs(32)], bview(T.B8, r), so[:, 8 * c0 + 7:8 * (c0 + nc):8, r], nc) for r in rs]],
+                   kk + ["B8"], ["sum" + U], ["pb"], q == 0, q == 3)
+            cp("v", hI[:, cs(0)], T.pa[:, cs(128)], nc, ["U" + U], ["h0" + U], ["pa"])
+            ts(hI[:, cs(32)], hI[:, cs(0)], 2047, None, A.bitwise_and, None, nc, ["h0" + U], ["h1" + U])
+            ts(hI[:, cs(64)], hI[:, cs(32)], 32.0, None, A.add, None, nc, ["h1" + U], ["h2" + U])
+            tt(hI[:, cs(0)], hI[:, cs(32)], hI[:, cs(64)], A.mult, nc, ["h1" + U, "h2" + U], ["h0" + U])
+            ts(hI[:, cs(96)], hI[:, cs(0)], 5, 2047, A.arith_shift_right, A.bitwise_and, nc, ["h0" + U], ["h3" + U])
+            cp("v", T.hU[:, cs(0)], hI[:, cs(96)], nc, ["h3" + U], ["hU" + U])
+            tt(sm[:, cs(128)], T.pb[:, cs(32)], T.stT[:, cs(0)], A.is_gt, nc, ["sum" + U, "stT" + U], ["sf" + U], ["pb"])
+            aff("s", sm[:, cs(160)], sm[:, cs(128)], -BIG, BIG + KD, nc, ["sf" + U], ["thrK" + U])
+            tt(sm[:, cs(192)], sm[:, cs(32)], sm[:, cs(160)], A.subtract, nc, ["base0", "thrK" + U], ["bm" + U])
+            tt(T.key[:, cs(0)], T.pb[:, cs(32)], sm[:, cs(192)], A.add, nc, ["sum" + U, "bm" + U], ["k0" + U], ["pb"])
+            for a, n in sub:
+                s16 = slice(16 * a, 16 * (a + n))
+                gat("v", T.dk[:, s16], Xw, T.hU[:, a:a + n], 16 * n, XK + ["hU" + U] + keys("pi", a, n), ["dk%d" % a],
+                    W[:, 2560 + 16 * a:2560 + 16 * (a + n)], A.subtract)
+                act(T.ak[:, s16], T.dk[:, s16], F.Abs, 16 * n, ["dk%d" % a], ["ak%d" % a])
+            mm([[(T.pb[:, cs(224)], bview(T.B8, r), T.ak[:, 16 * c0 + r:16 * (c0 + nc):16], nc) for r in range(16)]],
+               ["ak%d" % a for a, n in sub] + ["B8"], ["KD" + U], ["pb"])
+            tt(T.ask[:, cs(0)], T.pb[:, cs(224)], sm[:, cs(160)], A.is_gt, nc, ["KD" + U, "thrK" + U], ["ask" + U], ["pb"])
+            ts(sm[:, cs(416)], T.ask[:, cs(0)], 512.0, None, A.mult, None, nc, ["ask" + U], ["a5" + U])
+            scan(T.cum[:, cs(0)], T.one[:, 0:nc], T.ask[:, cs(0)], T.cum[:, c0 - 1:c0] if c0 else 56.0, A.add, nc,
+                 ["ask" + U, "one"] + (["cum%d" % (u - 1)] if c0 else []), ["cum" + U])
+            tt(sm[:, cs(448)], sm[:, cs(416)], T.nn[:, cs(0)], A.add, nc, ["a5" + U, "nn"], ["oa" + U])
+            mm([[(T.pb[:, cs(192)], mat(T.BK, 2), T.cum[:, cs(0)], nc), (T.pb[:, cs(192)], mat(T.BK, 3), T.ask[:, cs(0)], nc),
+                 (T.pb[:, cs(192)], N22, T.ask[:, cs(0)], nc)]], ["cum" + U, "ask" + U, "BK2", "BK3", "ID3"], ["pz" + U], ["pb"])
+            ts(sm[:, cs(480)], T.pb[:, cs(192)], 0.0, 512.0, A.is_le, A.mult, nc, ["pz" + U], ["b1" + U], ["pb"])
+            tt(sm[:, cs(384)], sm[:, cs(480)], sm[:, cs(448)], A.add, nc, ["b1" + U, "oa" + U], ["b2" + U])
+            cp("v", T.bU[:, cs(0)], sm[:, cs(384)], nc, ["b2" + U], ["bU" + U])
+            for x, (a, n) in enumerate(sub):
+                s16 = slice(16 * a, 16 * (a + n))
+                pi, av = W[:, 2560 + 16 * a:2560 + 16 * (a + n)], W[:, 3072 + 16 * a:3072 + 16 * (a + n)]
+                e1, e2, e3 = CFG["av"][x]
+                if e1 == "v":
+                    gat("v", T.gb[:, s16], W[:, 0:XW], T.hU[:, a:a + n], 16 * n, ["hU" + U, XR] + keys("pi", a, n), ["gb%d" % a], pi, A.add)
+                    aff(e2, T.gc2[:, s16], T.gb[:, s16], 0.5, 191.75, 16 * n, ["gb%d" % a], ["gc%d" % a], half=True)
+                else:
+                    gat("s", T.gb[:, s16], W[:, 0:XW], T.hU[:, a:a + n], 16 * n, ["hU" + U, XR], ["gb%d" % a])
+                    pf, fk = T["pf%d" % x][:, 0:16 * n], ["pf%d" % x]
+                    mm([[(pf, IDp, pi, 16 * n), (pf, IDp, T.gb[:, s16], 16 * n)]], ["gb%d" % a, "ID0"] + keys("pi", a, n), fk, fk)
+                    aff(e2, T.gc2[:, s16], pf, 0.5, 191.75, 16 * n, fk, ["gc%d" % a], pk=fk)
+                aff(e3, av, T.gc2[:, s16], 1.0, -192.0, 16 * n, ["gc%d" % a], ["av%d" % a], half=True)
+
+        def allp(name):
+            return [name + str(u) for u, _, _ in TP]
+        if t + 1 < RO:
+            mm([[(T.pa[:, 64:96], mat(T.BK, 4), T.stT[:], 32)]], allp("stT") + ["BK4"], ["pA"], ["pa"])
+            act(T.zj[:, 512:544], T.pa[:, 64:96], F.Identity, 40, ["pA"], ["A0"], ["pa"], accum_out=T.thr[:, 1:2])
+            cp("v", T.aI[:, 0:1], T.thr[:, 1:2], 1, ["A0"], ["A1"])
+            ts(T.aI[:, 1:2], T.aI[:, 0:1], 7, None, A.bitwise_and, None, 1, ["A1"], ["A2"])
+            ts(T.thr[:, 0:1], T.aI[:, 1:2], 14.0, None, A.add, None, 1, ["A2"], ["thr"])
+        tt(T.key[:, 32:64], T.key[:, 0:32], sm[:, 0:32], A.max, 32, allp("k0") + ["fb"], ["k1"])
+        add("v", 64, lambda e: e.transpose(T.key[:, 64:96], T.key[:, 32:64]), ["k1"], ["k2"])
+        scan(T.key[:, 32:64], T.rst[:, 0:32], T.key[:, 64:96], 0.0, A.max, 32, ["k2", "rst"], ["k1"])
+        cp("v", T.goI[:, 0:4], T.key[:, 39:64:8], 4, ["k1"], ["g0"])
+        ts(T.goI[:, 4:8], T.goI[:, 0:4], 1023, None, A.bitwise_and, None, 4, ["g0"], ["g1"])
+        cp("v", T.goF[:], T.goI[:, 4:8], 4, ["g1"], ["g2"])
+        for q in range(4):
+            aff("s", T.goH[:, q:16:4], T.goF[:], col(12 + q), 0.0, 4, ["g2", "qm"], ["gh%d" % q])
+        mm([[(T.pa[:, 96:100], T.G[:, 17 - (16 * (x // 2) + x % 2):145 - (16 * (x // 2) + x % 2)], T.goH[:, 4 * x:4 * x + 4], 4) for x in range(4)]],
+           ["G"] + ["gh%d" % q for q in range(4)], ["pgo"], ["pa"])
+        if t + 1 < RO:
+            cp("v", T.vu[:], T.pa[:, 96:100], 4, ["pgo"], ["vu"], ["pa"])
+        cp("v", T.vF[:], T.pa[:, 96:100], 4, ["pgo"], ["vF"], ["pa"])
+        tt(sm[:, 224:256], hI[:, 96:128], T.pcsc[:, 0:32], A.subtract, 32, allp("h3") + ["pcsc"], ["dp"])
+        tt(T.bp[:, 0:32], sm[:, 224:256], sm[:, 128:160], A.mult, 32, ["dp"] + allp("sf"), ["bp0"])
+        tt(T.bp[:, 32:64], sm[:, 96:128], sm[:, 128:160], A.mult, 32, ["ds"] + allp("sf"), ["bp1"])
+        tt(sm[:, 352:384], T.nn[:, 64:96], hI[:, 96:128], A.subtract, 32, allp("h3") + ["nw"], ["dl"])
+        tt(T.ad[:], T.ask[:], sm[:, 352:384], A.mult, 32, allp("ask") + ["dl"], ["ad"])
+        toP, toS = [PC[0], SB[0]], [PC[1], SB[1]]
+        mm([[(T.pa[:, 224:288], PC[0], T.N1[:], 64), (T.pa[:, 224:288], SB[1], T.N1[:], 64)]
+            + [(T.pa[:, 224 + b:288:2], toP[b], T.bp[:, 0:32], 32) for b in range(2)]
+            + [(T.pa[:, 224 + b:288:2], toS[b], T.bp[:, 32:64], 32) for b in range(2)]], ["N1", "bp0", "bp1"] + KC, ["ppair"], ["pa"], True, False)
+        mm([[(T.pa[:, 224 + b:288:2], toP[b], T.ad[:], 32) for b in range(2)]], ["ad"] + KC, ["ppair"], ["pa"], False, True)
+        cp("s", T.pair[:], T.pa[:, 224:288], 64, ["ppair"], ["pair"], ["pa"])
+        add("v", 60 + 64 * 3.5, lambda e: e.tensor_copy(T.ef[:, 0:V + 64].indirect(T.soff[:, 0:4]), T.pair[:]),
+            ["pair", "soff", "ef0", "ef1", "efd"], ["ef0", "ef1", "efd"])
+        kk = [k for k in lastw if k.startswith("av")] + PIK + allp("bU") + [OLD, XK[wk]]
+        add("n", 0, None, (), [XK[wk]])
+        f = CFG["fin"]
+        gat("v", T.X[:, 512 * wk:512 * wk + 16 * f], W[:, 2048:3584], T.bU[:, 0:f], 16 * f, kk, ["Xa"])
+        gat("s", T.X[:, 512 * wk + 16 * f:512 * wk + 512], W[:, 2048:3584], T.bU[:, f:32], 512 - 16 * f, kk, ["Xb"])
+        add("n", 0, None, ["Xa", "Xb"], [XK[wk]])
+        send(t, True)
+        if t == 3:
+            dma("y", T.yx[:, 512:2048], T.X[:, 512:2048], 393216, XK[1:], ["yx1"])
+    dma("y", T.yv[:], T.vF[:], 2048, ["vF"], ["yv"])
+    dma("y", T.ye[:], T.ef[:, 0:V], 516096, ["ef0", "ef1"], ["ye"])
+    dma("s", T.yx[:, 0:512], T.X[:, 0:512], 131072, ["X0"], ["yx0"])
+    return ops
+
+
+PLAN = {}
+
+
+def rank_program(g, core, T, topo):
+    rank = T.rank_of(core)
+    if rank is None:
+        helper_program(g, core, T, topo)
+        return
+    ops = build(T, topo, core, rank)
+    if "order" not in PLAN:
+        PLAN["order"] = plan(ops)[0]
+    eng = {"v": g.vector, "s": g.scalar, "p": g.tensor, "g": g, "y": g.sync}
+    cnt = {"v": 0, "s": 0, "p": 0, "g": 0}
+    seen = {e: {} for e in eng}
+    done = {}
+
+    def needs(o, e, need):
+        for d, raw in o["dep"].items():
+            p = ops[d]
+            if p["eng"] == "n":
+                needs({"dep": {x: True for x in p["dep"]}, "sem": o["sem"]}, e, need)
+            elif p["eng"] == e and p["sem"] is None and (not raw or e == "p"):
+                continue
+            elif p["eng"] == e and not raw and ("sendq" in o.get("w", ()) or "ldq" in o.get("w", ())):
+                continue
+            else:
+                s, n = done[d]
+                need[s] = max(need.get(s, 0), n)
+        return need
+
+    for i in PLAN["order"]:
+        o = ops[i]
+        e = o["eng"]
+        if o["fn"] is not None:
+            for s, n in needs(o, e, {}).items():
+                if seen[e].get(s, 0) < n:
+                    eng[e].wait_ge(T.sem[s], n)
+                    seen[e][s] = n
+            ins = o["fn"](eng[e])
+            if o["sem"] is None:
+                cnt[e] += 1
+                ins.then_inc(T.sem["c" + e], 1)
+            elif ins is not None:
+                ins.then_inc(T.sem[o["sem"][0]], o["sem"][1])
+        if e != "n":
+            done[i] = o["sem"] if o["sem"] is not None else ("c" + e, cnt[e])
+    last = {"c" + e: n for e, n in cnt.items()}
+    for o in ops:
+        if o["sem"] is not None:
+            last[o["sem"][0]] = o["sem"][1]
+    for s, n in last.items():
+        if n and not any(seen[e].get(s, 0) >= n for e in eng):
+            g.sync.wait_ge(T.sem[s], n)

@@ -14,8 +14,12 @@ CFG = {
     "bc": ("vvvvvvv", "vvvvvvg", "vvvvggg", "vvvgggg"),
     "fb": (),
     "tp": (32,),
-    "hd": (8, 24), "n2": "vs", "xp": "ssss", "fin": 12, "av": ("ssv", "ssv"), "tries": 5000, "seed": 2, "heat": 600.0, "xs": 4, "fv": (2, 4), "xe": "ssssssss",
-    "lat": 70.0, "pe": 0.55, "ga": 1.56, "so": 30.0,
+    "hd": (8, 24), "n2": "vs", "xp": "ssss", "fin": 12, "av": ("ssv", "ssv"), "tries": 7000, "seed": 2, "heat": 600.0, "xs": 4, "fv": (2, 4), "xe": "ssssssss",
+    "np": (2, 3), "dk": 22, "p1": (1, 2, 2, 2),
+    "off": {"cnt0": -1500.0, "cnu0": -1500.0, "sum0": -1000.0, "Y0": 3000.0, "dead0": 3000.0, "sc10": 3000.0, "subU0": 3000.0,
+            "Xsub0": 3000.0, "Y1": 2000.0, "dead1": 2000.0, "sc11": 2000.0, "subU1": 2000.0, "Xsub1": 2000.0, "Xs0": 2000.0, "Xs1": 2000.0,
+            "pd0": 1000.0, "pd1": 1000.0, "absd0": 2000.0, "absd1": 2000.0, "D0": 2000.0, "pen0": 2000.0},
+    "lat": 230.0, "pe": 0.55, "ga": 1.56, "so": 80.0,
 }
 
 
@@ -41,7 +45,7 @@ SCRATCH = {
     "PM": _sb(128 * 8, F16), "ID": _sb(128 * 4, B16), "ST": _sb(128 * 16, B16), "BK": _sb(128 * 7, B16),
     "B8": _sb(144, B16), "Bw": _sb(144, B16), "G": _sb(160, F16), "rst": _sb(256, B16), "one": _sb(32, B16),
     "nn": _sb(96, F32), "i64": _sb(V, F32), "lrow": _sb(64, F32),
-    "pa": ("psum", [128, 512], F32), "pb": ("psum", [128, 512], F32),
+    "pa": ("psum", [128, 512], F32), "pf2": ("psum", [128, 512], F32),
     "pc0": ("psum", [128, 2, 32, 8], F32), "pc1": ("psum", [128, 2, 32, 8], F32),
     "pd0": ("psum", [128, 4, 8, 16], F32), "pd1": ("psum", [128, 4, 8, 16], F32),
     "pf0": ("psum", [128, 512], F32), "pf1": ("psum", [128, 512], F32),
@@ -151,7 +155,7 @@ def plan(ops):
         order, at = plan_once(flat, succ, {i: pr[i] + off[cls[i]] for i in range(n)}, [look[c] for c in cls])
         return max(at[i] + o["cost"] + o["lag"] for i, o in enumerate(ops)), order, at
     rng = np.random.default_rng(CFG["seed"])
-    off, look = [0.0] * len(names), [250.0] * len(names)
+    off, look = [CFG["off"].get(x.split(".")[0], 0.0) for x in names], [250.0] * len(names)
     best = cur = run(off, look)
     for it in range(CFG["tries"]):
         o2, l2 = list(off), list(look)
@@ -173,6 +177,7 @@ def build(T, topo, core, rank):
     lastw, readers, bank, seen = {}, {}, {}, {}
     nd = [0]
     PE, GA, SO = CFG["pe"], CFG["ga"], CFG["so"]
+    NPD, NPF = CFG["np"]
 
     def add(eng, cost, fn, r=(), w=(), pk=(), lag=0.0, sem=None):
         i = len(ops)
@@ -380,9 +385,9 @@ def build(T, topo, core, rank):
         mm([[(T.pa[:, 32:64], LS[b], T.N1[:, b:64:2], 32) for b in range(2)],
             [(T.pa[:, 0:32], LP[b], T.N1[:, b:64:2], 32) for b in range(2)]], ["N1"] + KL, ["paL"], ["pa"])
         cp("v", T.L[:], T.pa[:, 0:64], 64, ["paL"], ["L"], ["pa"])
-        mm([[(T.pb[:, 128:160], PC[b], T.N1[:, b:64:2], 32) for b in range(2)],
-            [(T.pb[:, 160:192], SB[b], T.N1[:, b:64:2], 32) for b in range(2)]], ["N1"] + KC, ["pbC"], ["pb"])
-        cp("s", T.pcsc[:], T.pb[:, 128:192], 64, ["pbC"], ["pcsc"], ["pb"])
+        mm([[(T.pa[:, 288:320], PC[b], T.N1[:, b:64:2], 32) for b in range(2)],
+            [(T.pa[:, 320:352], SB[b], T.N1[:, b:64:2], 32) for b in range(2)]], ["N1"] + KC, ["pbC"], ["pa"])
+        cp("s", T.pcsc[:], T.pa[:, 288:352], 64, ["pbC"], ["pcsc"], ["pa"])
         gat("v", T.z[:], T.i64[:, 0:V], T.vu[:, 0:4], 64, ["i64", "vu", "lrow"], ["z"], T.lrow[:], A.add)
         aff("s", T.fs[:, 0:4], T.vF[:], -64.0, 0.5, 4, ["vF"], ["nlo"])
         tt(T.fs[:, 4:8], T.fs[:, 0:4], T.nn[:, 0:4], A.subtract, 4, ["nlo", "nn"], ["nhi"])
@@ -420,8 +425,13 @@ def build(T, topo, core, rank):
             s8 = slice(8 * c0, 8 * (c0 + nc))
             s16 = slice(16 * c0, 16 * (c0 + nc))
             pS, pD = T.pc0[:, 0, sc], T.pc1[:, 0, sc]
-            gat("v", T.m[:, e0:e1], Xw, T.pU[:, s8], 128 * nc, XK + ["pU" + H] + ["XpB%d" % j + H for j in range(8)],
-                ["m" + H], T.XpB[:, e0:e1], A.min)
+            np1 = CFG["p1"][h]
+            add("n", 0, None, (), ["m" + H])
+            for x in range(np1):
+                a, b = c0 + x * nc // np1, c0 + (x + 1) * nc // np1
+                gat("v", T.m[:, 128 * a:128 * b], Xw, T.pU[:, 8 * a:8 * b], 128 * (b - a),
+                    XK + ["m" + H] + ["pU" + H] + ["XpB%d" % j + H for j in range(8)], ["m" + H + "abcd"[x]], T.XpB[:, 128 * a:128 * b], A.min)
+            add("n", 0, None, ["m" + H + "abcd"[x] for x in range(np1)], ["m" + H])
             for a in range(c0, c0 + nc, CFG["xs"]):
                 n = min(CFG["xs"], c0 + nc - a)
                 gat(CFG["xe"][a // 4], T.Xs[:, 112 * a:112 * (a + n)], Xw, T.sU[:, 7 * a:7 * (a + n)], 112 * n, XK + ["sU" + H],
@@ -433,7 +443,7 @@ def build(T, topo, core, rank):
             ts(T.subU[:, c0:c0 + nc], T.sc1[:, 8 * c0 + 7:8 * (c0 + nc):8], -KA, 0.0, A.add, A.max, nc, ["sc1" + H], ["subU" + H])
             gat("s", T.Xsub[:, s16], Xw, T.subU[:, c0:c0 + nc], 16 * nc, XK + ["subU" + H], ["Xsub" + H])
             for k in range(c0 // 4, (c0 + nc) // 4):
-                pd, dk_ = T["pd%d" % (k % 2)], ["pd%d" % (k % 2)]
+                pd, dk_ = T["pd%d" % (k % NPD)], ["pd%d" % (k % NPD)]
                 mm([[(pd[:, :, 0:7, :], IDp, T.Xs[:, 448 * k:448 * k + 448], 448)]
                     + [(pd[:, :, i, :], IDn, T.Xsub[:, 64 * k:64 * k + 64], 64) for i in range(7)]],
                    ["Xs%d" % k, "Xsub" + H, "ID0", "ID1"], dk_, dk_)
@@ -444,7 +454,7 @@ def build(T, topo, core, rank):
             ts(T.pen[:, s8], pD, KD, -16.0, A.is_gt, A.mult, 8 * nc, ["D" + H], ["pen" + H], ["pc1"])
             per, w8 = 64 // nc, 8 * nc
             for r0 in range(0, 16, per):
-                pf, fk = T["pf%d" % (nf % 2)], ["pf%d" % (nf % 2)]
+                pf, fk = T["pf%d" % (nf % NPF)], ["pf%d" % (nf % NPF)]
                 rs = list(range(r0, min(16, r0 + per)))
                 fv = nf in CFG["fv"]
                 mm([[(pf[:, w8 * (r - r0):w8 * (r - r0 + 1)], IDp, T.m[:, e0 + r:e1:16], w8)][:0 if fv else 1]
@@ -484,44 +494,47 @@ def build(T, topo, core, rank):
                 return slice(a + c0, a + c0 + nc)
             sub = [(c0, nc // 2), (c0 + nc // 2, nc // 2)] if nc >= 16 else [(c0, nc)]
             so = T.SO
-            pn = T.pc0[:, 1, c0 // 8:(c0 + nc) // 8]
+            def px(k):
+                return T.pc0[:, 1, 4 * k + c0 // 8:4 * k + (c0 + nc) // 8]
+            pn = T.pc1[:, 1, c0 // 8:(c0 + nc) // 8]
             mm([[(pn, mat(T.BK, 1), T.dead[:, 8 * c0 + i:8 * (c0 + nc):8], nc) for i in range(8)]],
-               keys("dead", c0, nc) + ["BK1"], ["cnt" + U], ["pc0"], True, False)
+               keys("dead", c0, nc) + ["BK1"], ["cnt" + U, "psx"], ["pc1"], True, False)
             mm([[(pn, mat(T.BK, 0), T.pen[:, 8 * c0 + i:8 * (c0 + nc):8], nc) for i in range(8)]],
-               keys("pen", c0, nc) + ["BK0"], ["cnu" + U, "cnt" + U], ["pc0"], False, True)
-            ts(T.stT[:, cs(0)], pn, T.thr[:, 0:1], BIG, A.is_gt, A.mult, nc, ["cnt" + U, "thr"], ["stT" + U], ["pc0"])
+               keys("pen", c0, nc) + ["BK0"], ["cnu" + U, "cnt" + U], ["pc1"], False, True)
+            ts(T.stT[:, cs(0)], pn, T.thr[:, 0:1], BIG, A.is_gt, A.mult, nc, ["cnt" + U, "thr"], ["stT" + U], ["pc1"])
             for q in range(4):
                 rs = range(4 * q, 4 * q + 4)
                 kk = [x for r in rs for x in keys("SO%d_" % r, c0, nc)]
                 mm([[(T.pa[:, cs(128)], bview(T.Bw, r), so[:, 8 * c0 + 7:8 * (c0 + nc):8, r], nc) for r in rs]],
                    kk + ["Bw"], ["U" + U], ["pa"], q == 0, q == 3)
-                mm([[(T.pb[:, cs(32)], bview(T.B8, r), so[:, 8 * c0 + 7:8 * (c0 + nc):8, r], nc) for r in rs]],
-                   kk + ["B8"], ["sum" + U], ["pb"], q == 0, q == 3)
+                mm([[(px(1), bview(T.B8, r), so[:, 8 * c0 + 7:8 * (c0 + nc):8, r], nc) for r in rs]],
+                   kk + ["B8"], ["sum" + U], ["pc0"], q == 0, q == 3)
             cp("v", hI[:, cs(0)], T.pa[:, cs(128)], nc, ["U" + U], ["h0" + U], ["pa"])
             ts(hI[:, cs(32)], hI[:, cs(0)], 2047, None, A.bitwise_and, None, nc, ["h0" + U], ["h1" + U])
             ts(hI[:, cs(64)], hI[:, cs(32)], 32.0, None, A.add, None, nc, ["h1" + U], ["h2" + U])
             tt(hI[:, cs(0)], hI[:, cs(32)], hI[:, cs(64)], A.mult, nc, ["h1" + U, "h2" + U], ["h0" + U])
             ts(hI[:, cs(96)], hI[:, cs(0)], 5, 2047, A.arith_shift_right, A.bitwise_and, nc, ["h0" + U], ["h3" + U])
             cp("v", T.hU[:, cs(0)], hI[:, cs(96)], nc, ["h3" + U], ["hU" + U])
-            tt(sm[:, cs(128)], T.pb[:, cs(32)], T.stT[:, cs(0)], A.is_gt, nc, ["sum" + U, "stT" + U], ["sf" + U], ["pb"])
+            tt(sm[:, cs(128)], px(1), T.stT[:, cs(0)], A.is_gt, nc, ["sum" + U, "stT" + U], ["sf" + U], ["pc0"])
             aff("s", sm[:, cs(160)], sm[:, cs(128)], -BIG, BIG + KD, nc, ["sf" + U], ["thrK" + U])
             tt(sm[:, cs(192)], sm[:, cs(32)], sm[:, cs(160)], A.subtract, nc, ["base0", "thrK" + U], ["bm" + U])
-            tt(T.key[:, cs(0)], T.pb[:, cs(32)], sm[:, cs(192)], A.add, nc, ["sum" + U, "bm" + U], ["k0" + U], ["pb"])
-            for a, n in sub:
+            tt(T.key[:, cs(0)], px(1), sm[:, cs(192)], A.add, nc, ["sum" + U, "bm" + U], ["k0" + U], ["pc0"])
+            dks = [(c0, CFG["dk"]), (c0 + CFG["dk"], nc - CFG["dk"])]
+            for a, n in dks:
                 s16 = slice(16 * a, 16 * (a + n))
                 gat("v", T.dk[:, s16], Xw, T.hU[:, a:a + n], 16 * n, XK + ["hU" + U] + keys("pi", a, n), ["dk%d" % a],
                     W[:, 2560 + 16 * a:2560 + 16 * (a + n)], A.subtract)
                 act(T.ak[:, s16], T.dk[:, s16], F.Abs, 16 * n, ["dk%d" % a], ["ak%d" % a])
-            mm([[(T.pb[:, cs(224)], bview(T.B8, r), T.ak[:, 16 * c0 + r:16 * (c0 + nc):16], nc) for r in range(16)]],
-               ["ak%d" % a for a, n in sub] + ["B8"], ["KD" + U], ["pb"])
-            tt(T.ask[:, cs(0)], T.pb[:, cs(224)], sm[:, cs(160)], A.is_gt, nc, ["KD" + U, "thrK" + U], ["ask" + U], ["pb"])
+            mm([[(px(2), bview(T.B8, r), T.ak[:, 16 * c0 + r:16 * (c0 + nc):16], nc) for r in range(16)]],
+               ["ak%d" % a for a, n in dks] + ["B8"], ["KD" + U], ["pc0"])
+            tt(T.ask[:, cs(0)], px(2), sm[:, cs(160)], A.is_gt, nc, ["KD" + U, "thrK" + U], ["ask" + U], ["pc0"])
             ts(sm[:, cs(416)], T.ask[:, cs(0)], 512.0, None, A.mult, None, nc, ["ask" + U], ["a5" + U])
             scan(T.cum[:, cs(0)], T.one[:, 0:nc], T.ask[:, cs(0)], T.cum[:, c0 - 1:c0] if c0 else 56.0, A.add, nc,
                  ["ask" + U, "one"] + (["cum%d" % (u - 1)] if c0 else []), ["cum" + U])
             tt(sm[:, cs(448)], sm[:, cs(416)], T.nn[:, cs(0)], A.add, nc, ["a5" + U, "nn"], ["oa" + U])
-            mm([[(T.pb[:, cs(192)], mat(T.BK, 2), T.cum[:, cs(0)], nc), (T.pb[:, cs(192)], mat(T.BK, 3), T.ask[:, cs(0)], nc),
-                 (T.pb[:, cs(192)], N22, T.ask[:, cs(0)], nc)]], ["cum" + U, "ask" + U, "BK2", "BK3", "ID3"], ["pz" + U], ["pb"])
-            ts(sm[:, cs(480)], T.pb[:, cs(192)], 0.0, 512.0, A.is_le, A.mult, nc, ["pz" + U], ["b1" + U], ["pb"])
+            mm([[(px(3), mat(T.BK, 2), T.cum[:, cs(0)], nc), (px(3), mat(T.BK, 3), T.ask[:, cs(0)], nc),
+                 (px(3), N22, T.ask[:, cs(0)], nc)]], ["cum" + U, "ask" + U, "BK2", "BK3", "ID3"], ["pz" + U], ["pc0"])
+            ts(sm[:, cs(480)], px(3), 0.0, 512.0, A.is_le, A.mult, nc, ["pz" + U], ["b1" + U], ["pc0"])
             tt(sm[:, cs(384)], sm[:, cs(480)], sm[:, cs(448)], A.add, nc, ["b1" + U, "oa" + U], ["b2" + U])
             cp("v", T.bU[:, cs(0)], sm[:, cs(384)], nc, ["b2" + U], ["bU" + U])
             for x, (a, n) in enumerate(sub):
@@ -569,7 +582,7 @@ def build(T, topo, core, rank):
             + [(T.pa[:, 224 + b:288:2], toP[b], T.bp[:, 0:32], 32) for b in range(2)]
             + [(T.pa[:, 224 + b:288:2], toS[b], T.bp[:, 32:64], 32) for b in range(2)]], ["N1", "bp0", "bp1"] + KC, ["ppair"], ["pa"], True, False)
         mm([[(T.pa[:, 224 + b:288:2], toP[b], T.ad[:], 32) for b in range(2)]], ["ad"] + KC, ["ppair"], ["pa"], False, True)
-        cp("s", T.pair[:], T.pa[:, 224:288], 64, ["ppair"], ["pair"], ["pa"])
+        cp("v", T.pair[:], T.pa[:, 224:288], 64, ["ppair"], ["pair"], ["pa"])
         add("v", 60 + 64 * 3.5, lambda e: e.tensor_copy(T.ef[:, 0:V + 64].indirect(T.soff[:, 0:4]), T.pair[:]),
             ["pair", "soff", "ef0", "ef1", "efd"], ["ef0", "ef1", "efd"])
         kk = [k for k in lastw if k.startswith("av")] + PIK + allp("bU") + [OLD, XK[wk]]

@@ -4,21 +4,19 @@ from concourse.mybir import dt, AluOpType, AxisListType, ActivationFunctionType
 A = AluOpType
 F = ActivationFunctionType
 V, XW, RO = 1008, 2048, 5
+PAD = 16
 SC = 8192.0
 KA = 87.5 * SC
 KD = 20.0 * SC
 BIG = float(2 ** 30)
+UP = 393216.0
 
 CFG = {
-    "ch": (8, 8, 8, 8),
-    "bc": ("vvvvvvv", "vvvvvvg", "vvvvggg", "vvvgggg"),
-    "fb": (),
-    "tp": (32,),
-    "hd": (8, 24), "n2": "vs", "xp": "ssss", "fin": 12, "av": ("ssv", "ssv"), "tries": 7000, "seed": 2, "heat": 600.0, "xs": 4, "fv": (2, 4), "xe": "ssssssss",
-    "np": (2, 3), "dk": 22, "p1": (1, 2, 2, 2),
-    "off": {"cnt0": -1500.0, "cnu0": -1500.0, "sum0": -1000.0, "Y0": 3000.0, "dead0": 3000.0, "sc10": 3000.0, "subU0": 3000.0,
-            "Xsub0": 3000.0, "Y1": 2000.0, "dead1": 2000.0, "sc11": 2000.0, "subU1": 2000.0, "Xsub1": 2000.0, "Xs0": 2000.0, "Xs1": 2000.0,
-            "pd0": 1000.0, "pd1": 1000.0, "absd0": 2000.0, "absd1": 2000.0, "D0": 2000.0, "pen0": 2000.0},
+    "bc": ("vvvvvvv", "vvvvggg", "vvvvggg", "vvvgggg"),
+    "hd": (8, 24), "n2": "vs", "xp": "ssss", "fin": 12, "av": ("ssv", "ssv"), "xs": ((4, "s"),) * 8,
+    "lift": (1, 1, 1, 0), "per": ((6, 5, 5), (6, 5, 5), (6, 5, 5), (6, 5, 5)), "p1": (1, 2, 2, 2), "kd": "max", "dk": (32,), "sk": "ss", "pic": "gggg", "sh": "s", "de": "v",
+    "tries": 7000, "seed": 2, "heat": 600.0, "off": {"Y0": 3000.0, "dead0": 3000.0, "sc10": 3000.0, "subU0": 3000.0, "Xsub0": 3000.0,
+                                                    "Y1": 2000.0, "dead1": 2000.0, "sc11": 2000.0, "subU1": 2000.0, "Xsub1": 2000.0},
     "lat": 230.0, "pe": 0.55, "ga": 1.56, "so": 80.0,
 }
 
@@ -29,29 +27,30 @@ def _sb(n, d):
 
 F32, B16, F16, I32, U16 = "float32", "bfloat16", "float16", "int32", "uint16"
 SCRATCH = {
-    "ei": _sb(V, I32), "ef": _sb(V + 64, F32), "X": _sb(XW, B16),
+    "ei": _sb(V, I32), "ef": _sb(V + 64, F32), "X": _sb(PAD + XW, B16), "TW": _sb(1536, B16),
     "vi": _sb(4, I32), "wi": _sb(1, I32), "vu": _sb(4, U16), "vF": _sb(4, F32),
-    "N1": _sb(64, F16), "L": _sb(64, U16), "pcsc": _sb(64, F32), "XpB": _sb(4096, B16), "N2": _sb(512, F16),
+    "N1": _sb(64, F16), "L": _sb(64, U16), "XpB": _sb(4096, B16), "N2": _sb(512, F16),
     "pU": _sb(256, U16), "sU": _sb(224, U16), "sK": _sb(256, F32), "m": _sb(4096, B16), "Xs": _sb(3584, B16),
     "Y": _sb(256, F32), "dead": _sb(256, B16), "sc1": _sb(256, F32), "subU": _sb(32, U16), "Xsub": _sb(512, B16),
-    "absd": _sb(3584, B16), "pen": _sb(256, B16), "SO": _sb([256, 16], B16), "FS": _sb(1024, B16),
-    "hI": _sb(128, I32), "hU": _sb(32, U16), "dk": _sb(512, B16), "ak": _sb(512, B16),
-    "ask": _sb(32, B16), "cum": _sb(32, B16), "ad": _sb(32, F16), "bp": _sb(64, F16),
-    "sm": _sb(512, F32), "stT": _sb(32, B16), "aU": _sb(32, U16), "bU": _sb(32, U16),
-    "ga": _sb(512, B16), "gb": _sb(512, B16), "gc2": _sb(512, B16), "pair": _sb(64, F32),
-    "key": _sb(96, F32), "goI": _sb(8, I32), "goF": _sb(4, F32), "goH": _sb(16, F16),
-    "z": _sb(64, F32), "zj": _sb(544, F32), "fs": _sb(32, F32), "soff": _sb(4, U16), "aI": _sb(2, I32), "thr": _sb(2, F32),
+    "absd": _sb(3584, B16), "pen": _sb([32, 9], B16), "dd": _sb([4, 72], B16), "SO": _sb([256, 16], B16),
+    "hI": _sb(160, I32), "hU": _sb(32, U16), "rb": _sb(32, B16), "hH": _sb(96, F16), "dk": _sb(512, B16), "ak": _sb(512, B16),
+    "ask": _sb(64, B16), "cum": _sb(64, B16), "sm": _sb(128, F32), "nd": _sb(384, F32), "stT": _sb(32, B16), "bU": _sb(32, U16),
+    "gb": _sb(512, B16), "gc2": _sb(512, B16),
+    "key": _sb(64, F32), "goI": _sb(8, I32), "goH": _sb(16, F16),
+    "z": _sb(64, F32), "ne": _sb(256, B16), "so": _sb(256, B16), "zj": _sb(32, F32), "fs": _sb(16, F32), "soff": _sb(4, U16),
+    "aI": _sb(2, I32), "thr": _sb(2, F32),
     "val": _sb(128 * 5, B16), "ix": _sb(160, B16), "ci": _sb(8, I32), "cc": _sb(32, F32),
-    "PM": _sb(128 * 8, F16), "ID": _sb(128 * 4, B16), "ST": _sb(128 * 16, B16), "BK": _sb(128 * 7, B16),
-    "B8": _sb(144, B16), "Bw": _sb(144, B16), "G": _sb(160, F16), "rst": _sb(256, B16), "one": _sb(32, B16),
-    "nn": _sb(96, F32), "i64": _sb(V, F32), "lrow": _sb(64, F32),
-    "pa": ("psum", [128, 512], F32), "pf2": ("psum", [128, 512], F32),
+    "PM": _sb(128 * 9, F16), "ID": _sb(128 * 3, B16), "ST": _sb(128 * 16, B16), "BK": _sb(128 * 9, B16),
+    "B8": _sb(144, B16), "Bw": _sb(144, B16), "B2": _sb(144, B16), "Bm": _sb(144, B16), "G": _sb(160, F16),
+    "rst": _sb(256, B16), "stp": _sb(256, B16), "one": _sb(64, B16), "kc": _sb(128, B16),
+    "nn": _sb(16, F32), "nN": _sb(128, F32), "iv": _sb(V, F32),
+    "pa": ("psum", [128, 512], F32), "pf2": ("psum", [128, 72, 7], F32),
     "pc0": ("psum", [128, 2, 32, 8], F32), "pc1": ("psum", [128, 2, 32, 8], F32),
-    "pd0": ("psum", [128, 4, 8, 16], F32), "pd1": ("psum", [128, 4, 8, 16], F32),
-    "pf0": ("psum", [128, 512], F32), "pf1": ("psum", [128, 512], F32),
+    "pd0": ("psum", [128, 8, 8, 8], F32), "pd1": ("psum", [128, 8, 8, 8], F32),
+    "pf0": ("psum", [128, 72, 7], F32), "pf1": ("psum", [128, 72, 7], F32),
 }
 for _t in range(RO):
-    SCRATCH["W%d" % _t] = _sb(3584, B16)
+    SCRATCH["W%d" % _t] = _sb(PAD + XW, B16)
 
 
 def messages():
@@ -91,8 +90,8 @@ def helper_program(g, core, T, topo):
         for k, (t, a, b, _), dst in mine:
             g.wait_ge(T.sem["hop%d" % k], bits(topo.mask(T.cores[rank], core)))
             rid, pid = topo.addr(dst, core)
-            w = T["W%d" % t]
-            g.remote_dma(w[:, a:b], w[:, a:b], T.sem["arr%d" % t], T.sem["ls%d" % k], pid, rid, topo.mask(core, dst))
+            w = T["W%d" % t][:, PAD + a:PAD + b]
+            g.remote_dma(w, w, T.sem["arr%d" % t], T.sem["ls%d" % k], pid, rid, topo.mask(core, dst))
         for k, _, dst in mine:
             g.wait_ge(T.sem["ls%d" % k], bits(topo.mask(core, dst)))
 
@@ -177,7 +176,6 @@ def build(T, topo, core, rank):
     lastw, readers, bank, seen = {}, {}, {}, {}
     nd = [0]
     PE, GA, SO = CFG["pe"], CFG["ga"], CFG["so"]
-    NPD, NPF = CFG["np"]
 
     def add(eng, cost, fn, r=(), w=(), pk=(), lag=0.0, sem=None):
         i = len(ops)
@@ -235,8 +233,8 @@ def build(T, topo, core, rank):
         else:
             act(out, a, F.Identity, n, r, w, pk, bias=bias, scale=scale)
 
-    def scan(out, d0, d1, ini, op1, cost, r, w, pk=()):
-        add("v", max(64, cost), lambda e: e.tensor_tensor_scan(out, d0, d1, ini, A.mult, op1), r, w, pk)
+    def scan(out, d0, d1, ini, op0, op1, cost, r, w, pk=()):
+        add("v", max(64, cost), lambda e: e.tensor_tensor_scan(out, d0, d1, ini, op0, op1), r, w, pk)
 
     def gat(eng, out, win, off, n, r, w, in1=None, o=None):
         if in1 is not None:
@@ -260,15 +258,15 @@ def build(T, topo, core, rank):
         nd[0] += 1
         add(eng, 80, lambda e: e.dma_start(out, a), r, w, lag=2000 + nbytes / 200.0, sem=(s, 16))
 
-    def iota(out, pat, cm, n, w):
-        add("g", 160 + 2 * n, lambda e: e.iota(out, pat, 0, cm, allow_small_or_imprecise_dtypes=True), (), w)
+    def iota(out, pat, cm, n, w, base=0):
+        add("g", 160 + 2 * n, lambda e: e.iota(out, pat, base, cm, allow_small_or_imprecise_dtypes=True), (), w)
 
-    def fill(ap, x, w):
-        add("v", 64, lambda e: e.memset(ap, x), (), w)
+    def fill(ap, x, w, n=64):
+        add("v", vc(n, True), lambda e: e.memset(ap, x), (), w)
 
     XK = ["X0", "X1", "X2", "X3"]
-    Xw = T.X[:, 0:XW]
-    cc = T.cc
+    Xw = T.X[:, PAD:PAD + XW]
+    cc, TW = T.cc, T.TW
 
     def col(k):
         return cc[:, k:k + 1]
@@ -276,9 +274,12 @@ def build(T, topo, core, rank):
     def mat(buf, k):
         return buf[:, 128 * k:128 * k + 128]
 
+    def xcols(buf, a, b):
+        return buf[:, PAD + a:PAD + b]
+
     dma("s", T.vi[:], T.v0[:], 2048, (), ["vi"])
     dma("y", T.ei[:], T.e0[:], 516096, (), ["ei", "ldq"])
-    dma("y", T.X[:], T.x0[:], 2 * 524288, (), XK + ["ldq"])
+    dma("y", Xw, T.x0[:], 2 * 524288, (), XK + ["ldq"])
     dma("s", T.wi[:], T.wt[:], 512, (), ["wi"])
 
     add("g", 162, lambda e: e.iota(T.ci[:, 0:1], [[0, 1]], 0, 1), (), ["p"])
@@ -288,13 +289,16 @@ def build(T, topo, core, rank):
     iota(mat(T.val, 2), [[1, 128]], -1, 128, ["val2"])
     iota(mat(T.val, 3), [[16, 8], [0, 16]], -1, 128, ["val3"])
     iota(mat(T.val, 4), [[8, 16], [0, 8]], 0, 128, ["val4"])
-    iota(T.lrow[:], [[1, 64]], 0, 64, ["lrow"])
-    iota(T.i64[:], [[64, V]], 0, V, ["i64"])
+    iota(T.iv[:], [[1, V]], 0, V, ["iv"])
+    iota(T.kc[:, 96:128], [[48, 32]], 0, 32, ["c48"])
     for b in range(2):
         for k, (x, off) in enumerate(((0, 7), (0, 15), (1, 0), (1, 8))):
             ts(mat(T.PM, 2 * k + b), mat(T.val, x), 128.0 * b - off, None, A.is_equal, None, 128, ["val%d" % x], ["PM%d%d" % (k, b)], half=True)
     LP, LS, PC, SB = [[mat(T.PM, 2 * k + b) for b in range(2)] for k in range(4)]
     KL, KC = ["PM00", "PM01", "PM10", "PM11"], ["PM20", "PM21", "PM30", "PM31"]
+    toP, toS = [PC[0], SB[0]], [PC[1], SB[1]]
+    IH = mat(T.PM, 8)
+    ts(IH, mat(T.val, 2), 0.0, None, A.is_equal, None, 128, ["val2"], ["IH"], half=True)
     for k, mask in enumerate((112, 120, 15, 7, 96)):
         ts(T.ci[:, k + 1:k + 2], T.ci[:, 0:1], mask, None, A.bitwise_and, None, 1, ["p"], ["ci%d" % k])
     ts(T.ci[:, 6:7], T.ci[:, 0:1], 3, 3, A.arith_shift_right, A.bitwise_and, 1, ["p"], ["ci5"])
@@ -302,32 +306,45 @@ def build(T, topo, core, rank):
     aff("s", col(7), col(1), 1.0, 15.0, 1, ["cc"], ["c7"])
     aff("s", col(11), col(5), 1.0, 17.0, 1, ["cc"], ["c11"])
     aff("s", col(8), col(4), 2.0, col(11), 1, ["cc", "c11"], ["c8"])
-    aff("s", col(9), col(4), -1024.0, 8192.0 - KA + KD, 1, ["cc"], ["c9"])
+    aff("s", col(9), col(3), 3.0, 0.125 - 128.5 / 1024, 1, ["cc"], ["c9"])
+    aff("s", col(24), col(1), 1.0, 8.0, 1, ["cc"], ["c24"])
+    aff("s", col(25), col(4), -1024.0, 7168.0, 1, ["cc"], ["c25"])
     cp("v", col(10), T.wi[:], 1, ["wi"], ["c10"])
     ts(cc[:, 12:16], T.ix[:, 0:4], col(6), None, A.is_equal, None, 4, ["cc", "ix"], ["qm"])
     ts(cc[:, 16:24], T.ix[:, 0:8], col(4), None, A.is_equal, None, 8, ["cc", "ix"], ["jm"])
-    ts(T.B8[:], T.ix[:, 0:144], col(7), SC, A.is_equal, A.mult, 144, ["c7", "ix"], ["B8"], half=True)
-    ts(T.Bw[:], T.ix[:, 0:144], col(7), col(10), A.is_equal, A.mult, 144, ["c7", "c10", "ix"], ["Bw"], half=True)
+    for buf, x, k in ((T.B8, SC, "B8"), (T.Bw, col(10), "Bw"), (T.B2, 2.0 / 512, "B2"), (T.Bm, -1.0 / 512, "Bm")):
+        ts(buf[:], T.ix[:, 0:144], col(7), x, A.is_equal, A.mult, 144, ["c7", "c10", "ix"], [k], half=True)
     ts(T.G[:], T.ix[:], col(8), None, A.is_equal, None, 160, ["c8", "ix"], ["G"], half=True)
-    for k, x in enumerate((1.0, -1.0, 2.0 ** 22, -2.0 ** 22)):
+    for k, x in enumerate((1.0, -1.0, 2.0 ** 22)):
         ts(mat(T.ID, k), mat(T.val, 2), 0.0, x, A.is_equal, A.mult, 128, ["val2"], ["ID%d" % k], half=True)
-    IDp, IDn, I22, N22 = [mat(T.ID, k) for k in range(4)]
+    IDp, IDn, I22 = [mat(T.ID, k) for k in range(3)]
     for r in range(16):
         ts(mat(T.ST, r), mat(T.val, 3), float(-r), None, A.is_equal, None, 128, ["val3"], ["ST%d" % r], half=True)
     ts(mat(T.BK, 0), mat(T.val, 4), col(2), -1.0 / 16, A.is_equal, A.mult, 128, ["val4", "cc"], ["BK0"], half=True)
     ts(mat(T.BK, 1), mat(T.val, 4), col(2), -1.0, A.is_equal, A.mult, 128, ["val4", "cc"], ["BK1"], half=True)
-    ts(mat(T.BK, 5), mat(T.val, 3), col(0), col(1), A.add, A.is_equal, 128, ["val3", "cc"], ["BK5"], half=True)
-    aff("s", mat(T.BK, 2), mat(T.BK, 5), 4096.0, 0.0, 128, ["BK5"], ["BK2"])
-    ts(mat(T.BK, 6), mat(T.val, 2), 0.0, -4096.0, A.is_lt, A.mult, 128, ["val2"], ["BK6"], half=True)
-    tt(mat(T.BK, 3), mat(T.BK, 6), mat(T.BK, 5), A.mult, 128, ["BK6", "BK5"], ["BK3"])
-    fill(mat(T.BK, 4), 2.0 ** -33, ["BK4"])
+    fill(mat(T.BK, 2), 2.0 ** -33, ["BK2"])
+    for b in range(2):
+        for k, x in ((3, 1.0), (5, -1.0)):
+            ts(mat(T.BK, k + b), mat(T.val, 4), col(1 + 23 * b), x / 1024, A.is_equal, A.mult, 128, ["val4", "cc", "c24"], ["BK%d" % (k + b)], half=True)
+        add("g", 461, lambda e, b=b: e.affine_select(mat(T.BK, 7 + b), mat(T.BK, 5 + b), [[-1, 128]], A.is_gt, 0.0, 8 * b, 1),
+            ["BK%d" % (5 + b)], ["BK%d" % (7 + b)])
+        add("g", 461, lambda e, b=b: e.affine_select(mat(T.BK, 7 + b), mat(T.BK, 7 + b), [[-1, 128]], A.not_equal, 1.375, 8 * b, 1),
+            ["BK%d" % (7 + b)], ["BK%d" % (7 + b)])
     fill(T.one[:], 1.0, ["one"])
     fill(T.thr[:, 0:1], 14.0, ["thr"])
     fill(T.ef[:, V:V + 64], 0.0, ["efd"])
-    fill(T.rst[:], 1.0, ["rst1"])
-    aff("s", T.rst[:, 0:256:8], T.one[:], 0.0, 0.0, 32, ["one", "rst1"], ["rst"])
-    aff("s", T.nn[:, 0:32], T.ix[:, 0:32], 16.0, col(3), 32, ["ix", "cc"], ["nn"])
-    aff("s", T.nn[:, 32:36], T.nn[:, 0:4], 1.0, float(V), 4, ["nn"], ["dump"])
+    fill(T.rst[:], 1.0, ["rst1"], 256)
+    aff("s", T.rst[:, 0:256:8], T.one[:, 0:32], 0.0, 0.0, 32, ["one", "rst1"], ["rst"])
+    fill(T.stp[:], 2048.0, ["stp1"], 256)
+    aff("s", T.stp[:, 0:256:64], T.one[:, 0:4], 0.0, -2.0 ** 19, 4, ["one", "stp1"], ["stp"])
+    fill(T.pen[:, :, 0], -32.0, ["pz0"])
+    fill(T.kc[:, 0:32], UP, ["kU"])
+    fill(T.kc[:, 32:64], 16.0, ["k16"])
+    aff("s", T.kc[:, 64:96], T.one[:, 0:32], col(25), 0.0, 32, ["one", "c25"], ["kj"])
+    aff("s", T.nn[:, 0:4], T.ix[:, 0:4], 16.0, col(3), 4, ["ix", "cc"], ["nn"])
+    aff("s", T.nn[:, 4:8], T.nn[:, 0:4], 1.0, float(V), 4, ["nn"], ["dump"])
+    aff("s", T.nn[:, 8:12], T.nn[:, 0:4], 2048.0, -2048.0 * 63, 4, ["nn"], ["back"])
+    aff("s", T.nN[:, 0:64], T.ix[:, 0:64], 8.0, col(4), 64, ["ix", "cc"], ["nN"])
     cp("v", T.vu[:], T.vi[:], 4, ["vi"], ["vu"])
     cp("v", T.vF[:], T.vi[:], 4, ["vi"], ["vF"])
     for k in range(2):
@@ -344,7 +361,7 @@ def build(T, topo, core, rank):
             rs = T.sem["arr%d" % t] if via is None else T.sem["hop%d" % k]
 
             def fn(e, k=k, t=t, a=a, b=b, rs=rs, pid=pid, rid=rid, mask=mask):
-                e.remote_dma(T["W%d" % t][:, a:b], T.X[:, a:b], rs, T.sem["ls%d" % k], pid, rid, mask)
+                e.remote_dma(xcols(T["W%d" % t], a, b), xcols(T.X, a, b), rs, T.sem["ls%d" % k], pid, rid, mask)
                 return None
             add("g", 1000, fn, XK[a // 512:b // 512] + list(behind), ["sendq", "msg%d" % k], lag=(3000 + (b - a) * 4.0) * (2 - (t % 3 == 1)),
                 sem=("ls%d" % k, bits(mask)))
@@ -365,41 +382,39 @@ def build(T, topo, core, rank):
             c += n
         return out
 
-    CH, TP = pieces(CFG["ch"]), pieces(CFG["tp"])
+    CH = pieces((8, 8, 8, 8))
 
-    def keys(name, c0, nc):
+    def keys(name, c0=0, nc=32):
         return [name + str(h) for h, a, n in CH if a < c0 + nc and c0 < a + n]
 
+    def third(k, a, n):
+        return TW[:, 48 * a + k:48 * (a + n):3]
+
     send(-1, True)
-    sm, hI = T.sm, T.hI
+    sm, hI, hH, nb = T.sm, T.hI, T.hH, T.nd
     for t in range(RO):
         W = T["W%d" % t]
         wk = t % 4
         EK = ["ei"] if t == 0 else ["ef0", "ef1", "efd"]
         Ew = T.ei[:, 0:V] if t == 0 else T.ef[:, 0:V]
-        XR, OLD = "XR%d" % t, "old%d" % t
+        XR = "XR%d" % t
         seen.clear()
         add("x%d" % t, 0, None, ["msg%d" % k for k, x in enumerate(MSG) if x[0] == t], [XR], sem=("arr%d" % t, arrivals(t)))
-        dma("y", W[:, 2048:2560], T.X[:, 512 * wk:512 * wk + 512], 131072, [XK[wk]], [OLD])
         gat("v", T.N1[:], Ew, T.vu[:, 0:4], 64, EK + ["vu"], ["N1"])
         mm([[(T.pa[:, 32:64], LS[b], T.N1[:, b:64:2], 32) for b in range(2)],
             [(T.pa[:, 0:32], LP[b], T.N1[:, b:64:2], 32) for b in range(2)]], ["N1"] + KL, ["paL"], ["pa"])
         cp("v", T.L[:], T.pa[:, 0:64], 64, ["paL"], ["L"], ["pa"])
-        mm([[(T.pa[:, 288:320], PC[b], T.N1[:, b:64:2], 32) for b in range(2)],
-            [(T.pa[:, 320:352], SB[b], T.N1[:, b:64:2], 32) for b in range(2)]], ["N1"] + KC, ["pbC"], ["pa"])
-        cp("s", T.pcsc[:], T.pa[:, 288:352], 64, ["pbC"], ["pcsc"], ["pa"])
-        gat("v", T.z[:], T.i64[:, 0:V], T.vu[:, 0:4], 64, ["i64", "vu", "lrow"], ["z"], T.lrow[:], A.add)
-        aff("s", T.fs[:, 0:4], T.vF[:], -64.0, 0.5, 4, ["vF"], ["nlo"])
-        tt(T.fs[:, 4:8], T.fs[:, 0:4], T.nn[:, 0:4], A.subtract, 4, ["nlo", "nn"], ["nhi"])
-        for q in range(8):
-            act(T.zj[:, 64 * q:64 * q + 64], T.z[:], F.Sign, 90, ["z", "nlo", "nhi"], ["cn%d" % q], bias=T.fs[:, q:q + 1], accum_out=T.fs[:, 8 + q:9 + q])
-        tt(T.fs[:, 16:20], T.fs[:, 8:12], T.fs[:, 12:16], A.subtract, 4, ["cn%d" % q for q in range(8)], ["f1"])
-        aff("s", T.fs[:, 20:24], T.fs[:, 16:20], 1024.0, 0.0, 4, ["f1"], ["f2"])
-        tt(T.fs[:, 24:28], T.fs[:, 20:24], T.vF[:], A.add, 4, ["f2", "vF"], ["f3"])
-        tt(T.fs[:, 28:32], T.fs[:, 24:28], T.nn[:, 32:36], A.min, 4, ["f3", "dump"], ["f4"])
-        cp("v", T.soff[:], T.fs[:, 28:32], 4, ["f4"], ["soff"])
-        aff("s", sm[:, 0:32], T.pcsc[:, 32:64], col(16 + t), 0.0, 32, ["pcsc", "jm"], ["fb"])
-        aff("s", T.nn[:, 64:96], T.nn[:, 0:32], 1.0, 512.0 * wk, 32, ["nn"], ["nw"])
+        mm([[(T.pa[:, 320:352], SB[b], T.N1[:, b:64:2], 32) for b in range(2)]], ["N1"] + KC, ["pbC"], ["pa"])
+        aff("s", sm[:, 0:32], T.pa[:, 320:352], col(16 + t), 65536.0, 32, ["pbC", "jm"], ["fb"], pk=["pa"])
+        gat("v", T.z[:], T.iv[:, 0:V], T.vu[:, 0:4], 64, ["iv", "vu"], ["z"])
+        for q in range(4):
+            ts(T.ne[:, 64 * q:64 * q + 64], T.z[:], T.vF[:, q:q + 1], -2.0 ** 18, A.not_equal, A.mult, 64, ["z", "vF"], ["ne%d" % q])
+        tt(T.fs[:, 0:4], T.vF[:], T.nn[:, 8:12], A.add, 4, ["vF", "back"], ["f0"])
+        scan(T.so[:], T.stp[:], T.ne[:], 0.0, A.add, A.max, 128, ["stp"] + ["ne%d" % q for q in range(4)], ["so"])
+        tt(T.fs[:, 4:8], T.so[:, 63:256:64], T.fs[:, 0:4], A.add, 4, ["so", "f0"], ["f1"])
+        tt(T.fs[:, 8:12], T.fs[:, 4:8], T.nn[:, 4:8], A.min, 4, ["f1", "dump"], ["f2"])
+        cp("v", T.soff[:], T.fs[:, 8:12], 4, ["f2"], ["soff"])
+        aff("s", T.nN[:, 64:128], T.nN[:, 0:64], 1.0, 512.0 * wk, 64, ["nN"], ["nw"])
         nf = 0
         for h, c0, nc in CH:
             H = str(h)
@@ -407,17 +422,25 @@ def build(T, topo, core, rank):
             gat(CFG["xp"][h], T.XpB[:, e0:e1:8], Xw, T.L[:, c0:c0 + nc], 16 * nc, XK + ["L"], ["XpB0" + H])
             for j in range(1, 8):
                 cp(CFG["bc"][h][j - 1], T.XpB[:, e0 + j:e1:8], T.XpB[:, e0:e1:8], 16 * nc, ["XpB0" + H], ["XpB%d" % j + H], half=True)
-        send(t - 1, False, ["XpB%d%d" % (j, h) for h, _, _ in CH for j in range(1, 8) if CFG["bc"][h][j - 1] == "g"])
+        GK = ["XpB%d%d" % (j, h) for h, _, _ in CH for j in range(1, 8) if CFG["bc"][h][j - 1] == "g"]
+        send(t - 1, False, GK)
+        add("g", 205 + 1024, lambda e, wk=wk: e.affine_select(third(0, 0, 32), xcols(T.X, 512 * wk, 512 * wk + 512), [[0, 512]], A.is_ge, 0.0, 0, 0),
+            [XK[wk]] + GK, ["old"])
+        if t in (0, 4):
+            cp("g", T.X[:, 0:PAD], T.X[:, XW:XW + PAD], PAD, ["X3"] + GK, ["Xq"])
         for h, c0, nc in pieces(CFG["hd"]):
             H = str(h)
             sc, s8 = slice(c0, c0 + nc), slice(8 * c0, 8 * (c0 + nc))
             gat("v" if t == 0 else CFG["n2"][h], T.N2[:, 16 * c0:16 * (c0 + nc)], Ew, T.L[:, 32 + c0:32 + c0 + nc], 16 * nc, EK + ["L"], ["N2" + H])
             n2 = [T.N2[:, 16 * c0 + b:16 * (c0 + nc):2] for b in range(2)]
-            mm([[(T.pc1[:, 1, sc], SB[b], n2[b], 8 * nc) for b in range(2)]], ["N2" + H] + KC, ["ps" + H], ["pc1"])
-            mm([[(T.pf1[:, s8], PC[b], n2[b], 8 * nc) for b in range(2)]], ["N2" + H] + KC, ["pp" + H, "pf1"], ["pf1"])
+            pp = T.pd1[:, c0 // 8:(c0 + nc) // 8]
+            mm([[(pp, PC[b], n2[b], 8 * nc) for b in range(2)]], ["N2" + H] + KC, ["pp" + H, "pd1"], ["pd1"])
+            mm([[(T.pc1[:, 1, sc], SB[b], n2[b], 8 * nc) for b in range(2)]], ["N2" + H] + KC, ["ps" + H, "cnt"], ["pc1"])
+            cp("v", T.pU[:, s8], pp, 8 * nc, ["pp" + H, "pd1"], keys("pU", c0, nc), ["pd1"])
             cp("v", T.sU[:, 7 * c0:7 * (c0 + nc)], T.pc1[:, 1, sc, 0:7], 7 * nc, ["ps" + H], keys("sU", c0, nc), ["pc1"])
-            cp("v", T.pU[:, s8], T.pf1[:, s8], 8 * nc, ["pp" + H, "pf1"], keys("pU", c0, nc), ["pf1"])
-            act(T.sK[:, s8], T.pc1[:, 1, sc], F.Identity, 8 * nc, ["ps" + H], keys("sK", c0, nc), ["pc1"], bias=KA)
+            aff(CFG["sk"][h], T.sK[:, s8], T.pc1[:, 1, sc], 1.0, KA, 8 * nc, ["ps" + H], keys("sK", c0, nc), pk=["pc1"])
+        for x, a, n in pieces([y[0] for y in CFG["xs"]]):
+            gat(CFG["xs"][x][1], T.Xs[:, 112 * a:112 * (a + n)], Xw, T.sU[:, 7 * a:7 * (a + n)], 112 * n, XK + keys("sU", a, n), ["Xs%d" % x])
         for h, c0, nc in CH:
             H = str(h)
             e0, e1 = 128 * c0, 128 * (c0 + nc)
@@ -432,171 +455,160 @@ def build(T, topo, core, rank):
                 gat("v", T.m[:, 128 * a:128 * b], Xw, T.pU[:, 8 * a:8 * b], 128 * (b - a),
                     XK + ["m" + H] + ["pU" + H] + ["XpB%d" % j + H for j in range(8)], ["m" + H + "abcd"[x]], T.XpB[:, 128 * a:128 * b], A.min)
             add("n", 0, None, ["m" + H + "abcd"[x] for x in range(np1)], ["m" + H])
-            for a in range(c0, c0 + nc, CFG["xs"]):
-                n = min(CFG["xs"], c0 + nc - a)
-                gat(CFG["xe"][a // 4], T.Xs[:, 112 * a:112 * (a + n)], Xw, T.sU[:, 7 * a:7 * (a + n)], 112 * n, XK + ["sU" + H],
-                    ["Xs%d" % k for k in range(a // 4, (a + n) // 4)])
             mm([[(pS, bview(T.B8, r), T.m[:, e0 + r:e1:16], 8 * nc) for r in range(16)]], ["m" + H, "B8"], ["S" + H], ["pc0"])
             tt(T.Y[:, s8], T.sK[:, s8], pS, A.min, 8 * nc, ["sK" + H, "S" + H], ["Y" + H], ["pc0"])
             ts(T.dead[:, s8], pS, KA, None, A.is_lt, None, 8 * nc, ["S" + H], ["dead" + H], ["pc0"])
-            scan(T.sc1[:, s8], T.dead[:, s8], T.Y[:, s8], 0.0, A.max, 8 * nc, ["Y" + H, "dead" + H], ["sc1" + H])
+            scan(T.sc1[:, s8], T.dead[:, s8], T.Y[:, s8], 0.0, A.mult, A.max, 8 * nc, ["Y" + H, "dead" + H], ["sc1" + H])
             ts(T.subU[:, c0:c0 + nc], T.sc1[:, 8 * c0 + 7:8 * (c0 + nc):8], -KA, 0.0, A.add, A.max, nc, ["sc1" + H], ["subU" + H])
             gat("s", T.Xsub[:, s16], Xw, T.subU[:, c0:c0 + nc], 16 * nc, XK + ["subU" + H], ["Xsub" + H])
-            for k in range(c0 // 4, (c0 + nc) // 4):
-                pd, dk_ = T["pd%d" % (k % NPD)], ["pd%d" % (k % NPD)]
-                mm([[(pd[:, :, 0:7, :], IDp, T.Xs[:, 448 * k:448 * k + 448], 448)]
-                    + [(pd[:, :, i, :], IDn, T.Xsub[:, 64 * k:64 * k + 64], 64) for i in range(7)]],
-                   ["Xs%d" % k, "Xsub" + H, "ID0", "ID1"], dk_, dk_)
-                act(T.absd[:, 448 * k:448 * k + 448], pd[:, :, 0:7, :], F.Abs, 448, dk_, ["absd%d" % k], dk_)
-            mm([[(pD, I22, T.dead[:, s8], 8 * nc)]
-                + [(T.pc1[:, 0, sc, 0:7], bview(T.B8, r), T.absd[:, 112 * c0 + r:112 * (c0 + nc):16], 7 * nc) for r in range(16)]],
-               ["dead" + H, "ID2", "B8"] + ["absd%d" % k for k in range(c0 // 4, (c0 + nc) // 4)], ["D" + H], ["pc1"])
-            ts(T.pen[:, s8], pD, KD, -16.0, A.is_gt, A.mult, 8 * nc, ["D" + H], ["pen" + H], ["pc1"])
-            per, w8 = 64 // nc, 8 * nc
-            for r0 in range(0, 16, per):
-                pf, fk = T["pf%d" % (nf % NPF)], ["pf%d" % (nf % NPF)]
-                rs = list(range(r0, min(16, r0 + per)))
-                fv = nf in CFG["fv"]
-                mm([[(pf[:, w8 * (r - r0):w8 * (r - r0 + 1)], IDp, T.m[:, e0 + r:e1:16], w8)][:0 if fv else 1]
-                    + [(pf[:, w8 * (r - r0):w8 * (r - r0 + 1)], mat(T.ST, r), T.pen[:, s8], w8)] for r in rs],
-                   ["m" + H, "pen" + H, "ID0"] + ["ST%d" % r for r in rs], fk, fk)
-                if fv:
-                    for r in rs:
-                        a = w8 * (r - r0)
-                        b = 512 * (CFG["fv"].index(nf) % 2) + a
-                        tt(T.FS[:, b:b + w8], T.m[:, e0 + r:e1:16], pf[:, a:a + w8], A.add, w8, ["m" + H] + fk, ["FV%d" % b], fk)
-                        scan(T.SO[:, s8, r], T.rst[:, 0:w8], T.FS[:, b:b + w8], 0.0, A.max, w8 / 2, ["rst", "FV%d" % b], ["SO%d_" % r + H])
-                    nf += 1
-                    continue
-                via = nf in CFG["fb"]
-                if via:
-                    f0 = 512 * (CFG["fb"].index(nf) % 2)
-                    fkey = ["FS%d" % f0]
-                    cp("s", T.FS[:, f0:f0 + w8 * len(rs)], pf[:, 0:w8 * len(rs)], w8 * len(rs), fk, fkey, fk)
-                for r in rs:
-                    a = w8 * (r - r0)
-                    if via:
-                        scan(T.SO[:, s8, r], T.rst[:, 0:w8], T.FS[:, f0 + a:f0 + a + w8], 0.0, A.max, w8 / 2, ["rst"] + fkey, ["SO%d_" % r + H])
-                    else:
-                        scan(T.SO[:, s8, r], T.rst[:, 0:w8], pf[:, a:a + w8], 0.0, A.max, w8, ["rst"] + fk, ["SO%d_" % r + H], fk)
-                nf += 1
-            cp("s", W[:, 2560 + 16 * c0:2560 + 16 * (c0 + nc)], T.SO[:, 8 * c0 + 7:8 * (c0 + nc):8, :], 16 * nc,
-               ["SO%d_" % r + H for r in range(16)], ["pi" + H])
-        SCK = keys("sc1", 0, 32)
-        aff("s", sm[:, 32:64], T.sc1[:, 7:256:8], 1.0, col(9), 32, SCK + ["c9"], ["base0"])
-        act(sm[:, 64:96], T.sc1[:, 7:256:8], F.Relu, 32, SCK, ["subF"], bias=-KA)
-        tt(sm[:, 96:128], sm[:, 64:96], T.pcsc[:, 32:64], A.subtract, 32, ["subF", "pcsc"], ["ds"])
-        PIK = keys("pi", 0, 32)
-        for u, c0, nc in TP:
-            U = str(u)
-
-            def cs(a):
-                return slice(a + c0, a + c0 + nc)
-            sub = [(c0, nc // 2), (c0 + nc // 2, nc // 2)] if nc >= 16 else [(c0, nc)]
-            so = T.SO
-            def px(k):
-                return T.pc0[:, 1, 4 * k + c0 // 8:4 * k + (c0 + nc) // 8]
-            pn = T.pc1[:, 1, c0 // 8:(c0 + nc) // 8]
-            mm([[(pn, mat(T.BK, 1), T.dead[:, 8 * c0 + i:8 * (c0 + nc):8], nc) for i in range(8)]],
-               keys("dead", c0, nc) + ["BK1"], ["cnt" + U, "psx"], ["pc1"], True, False)
-            mm([[(pn, mat(T.BK, 0), T.pen[:, 8 * c0 + i:8 * (c0 + nc):8], nc) for i in range(8)]],
-               keys("pen", c0, nc) + ["BK0"], ["cnu" + U, "cnt" + U], ["pc1"], False, True)
-            ts(T.stT[:, cs(0)], pn, T.thr[:, 0:1], BIG, A.is_gt, A.mult, nc, ["cnt" + U, "thr"], ["stT" + U], ["pc1"])
-            for q in range(4):
-                rs = range(4 * q, 4 * q + 4)
-                kk = [x for r in rs for x in keys("SO%d_" % r, c0, nc)]
-                mm([[(T.pa[:, cs(128)], bview(T.Bw, r), so[:, 8 * c0 + 7:8 * (c0 + nc):8, r], nc) for r in rs]],
-                   kk + ["Bw"], ["U" + U], ["pa"], q == 0, q == 3)
-                mm([[(px(1), bview(T.B8, r), so[:, 8 * c0 + 7:8 * (c0 + nc):8, r], nc) for r in rs]],
-                   kk + ["B8"], ["sum" + U], ["pc0"], q == 0, q == 3)
-            cp("v", hI[:, cs(0)], T.pa[:, cs(128)], nc, ["U" + U], ["h0" + U], ["pa"])
-            ts(hI[:, cs(32)], hI[:, cs(0)], 2047, None, A.bitwise_and, None, nc, ["h0" + U], ["h1" + U])
-            ts(hI[:, cs(64)], hI[:, cs(32)], 32.0, None, A.add, None, nc, ["h1" + U], ["h2" + U])
-            tt(hI[:, cs(0)], hI[:, cs(32)], hI[:, cs(64)], A.mult, nc, ["h1" + U, "h2" + U], ["h0" + U])
-            ts(hI[:, cs(96)], hI[:, cs(0)], 5, 2047, A.arith_shift_right, A.bitwise_and, nc, ["h0" + U], ["h3" + U])
-            cp("v", T.hU[:, cs(0)], hI[:, cs(96)], nc, ["h3" + U], ["hU" + U])
-            tt(sm[:, cs(128)], px(1), T.stT[:, cs(0)], A.is_gt, nc, ["sum" + U, "stT" + U], ["sf" + U], ["pc0"])
-            aff("s", sm[:, cs(160)], sm[:, cs(128)], -BIG, BIG + KD, nc, ["sf" + U], ["thrK" + U])
-            tt(sm[:, cs(192)], sm[:, cs(32)], sm[:, cs(160)], A.subtract, nc, ["base0", "thrK" + U], ["bm" + U])
-            tt(T.key[:, cs(0)], px(1), sm[:, cs(192)], A.add, nc, ["sum" + U, "bm" + U], ["k0" + U], ["pc0"])
-            dks = [(c0, CFG["dk"]), (c0 + CFG["dk"], nc - CFG["dk"])]
-            for a, n in dks:
-                s16 = slice(16 * a, 16 * (a + n))
-                gat("v", T.dk[:, s16], Xw, T.hU[:, a:a + n], 16 * n, XK + ["hU" + U] + keys("pi", a, n), ["dk%d" % a],
-                    W[:, 2560 + 16 * a:2560 + 16 * (a + n)], A.subtract)
-                act(T.ak[:, s16], T.dk[:, s16], F.Abs, 16 * n, ["dk%d" % a], ["ak%d" % a])
-            mm([[(px(2), bview(T.B8, r), T.ak[:, 16 * c0 + r:16 * (c0 + nc):16], nc) for r in range(16)]],
-               ["ak%d" % a for a, n in dks] + ["B8"], ["KD" + U], ["pc0"])
-            tt(T.ask[:, cs(0)], px(2), sm[:, cs(160)], A.is_gt, nc, ["KD" + U, "thrK" + U], ["ask" + U], ["pc0"])
-            ts(sm[:, cs(416)], T.ask[:, cs(0)], 512.0, None, A.mult, None, nc, ["ask" + U], ["a5" + U])
-            scan(T.cum[:, cs(0)], T.one[:, 0:nc], T.ask[:, cs(0)], T.cum[:, c0 - 1:c0] if c0 else 56.0, A.add, nc,
-                 ["ask" + U, "one"] + (["cum%d" % (u - 1)] if c0 else []), ["cum" + U])
-            tt(sm[:, cs(448)], sm[:, cs(416)], T.nn[:, cs(0)], A.add, nc, ["a5" + U, "nn"], ["oa" + U])
-            mm([[(px(3), mat(T.BK, 2), T.cum[:, cs(0)], nc), (px(3), mat(T.BK, 3), T.ask[:, cs(0)], nc),
-                 (px(3), N22, T.ask[:, cs(0)], nc)]], ["cum" + U, "ask" + U, "BK2", "BK3", "ID3"], ["pz" + U], ["pc0"])
-            ts(sm[:, cs(480)], px(3), 0.0, 512.0, A.is_le, A.mult, nc, ["pz" + U], ["b1" + U], ["pc0"])
-            tt(sm[:, cs(384)], sm[:, cs(480)], sm[:, cs(448)], A.add, nc, ["b1" + U, "oa" + U], ["b2" + U])
-            cp("v", T.bU[:, cs(0)], sm[:, cs(384)], nc, ["b2" + U], ["bU" + U])
-            for x, (a, n) in enumerate(sub):
-                s16 = slice(16 * a, 16 * (a + n))
-                pi, av = W[:, 2560 + 16 * a:2560 + 16 * (a + n)], W[:, 3072 + 16 * a:3072 + 16 * (a + n)]
-                e1, e2, e3 = CFG["av"][x]
-                if e1 == "v":
-                    gat("v", T.gb[:, s16], W[:, 0:XW], T.hU[:, a:a + n], 16 * n, ["hU" + U, XR] + keys("pi", a, n), ["gb%d" % a], pi, A.add)
-                    aff(e2, T.gc2[:, s16], T.gb[:, s16], 0.5, 191.75, 16 * n, ["gb%d" % a], ["gc%d" % a], half=True)
+            xk = ["Xs%d" % x for x, a, n in pieces([y[0] for y in CFG["xs"]]) if a < c0 + nc and c0 < a + n]
+            for x in range(2):
+                pd, dk_ = T["pd%d" % x], ["pd%d" % x]
+                a0 = 112 * c0 + 448 * x
+                mm([[(pd[:, :, 0:7, :], IDp, T.Xs[:, 112 * c0 + x:112 * (c0 + nc):2], 448)]
+                    + [(pd[:, :, i, :], IDn, T.Xsub[:, 16 * c0 + x:16 * (c0 + nc):2], 64) for i in range(7)]],
+                   xk + ["Xsub" + H, "ID0", "ID1"], dk_, dk_)
+                act(T.absd[:, a0:a0 + 448], pd[:, :, 0:7, :], F.Abs, 448, dk_, ["absd%d" % x + H], dk_)
+                mm([[(pD, I22, T.dead[:, s8], 8 * nc)][:1 - x]
+                    + [(T.pc1[:, 0, sc, 0:7], bview(T.B8, 2 * r + x), T.absd[:, a0 + r:a0 + 448:8], 7 * nc) for r in range(8)]],
+                   ["dead" + H, "ID2", "B8", "absd%d" % x + H], ["D" + H], ["pc1"], x == 0, x == 1)
+            ts(T.pen[:, sc, 1:9], pD, KD, -16.0, A.is_gt, A.mult, 8 * nc, ["D" + H], ["pen" + H], ["pc1"])
+            lift = CFG["lift"][h]
+            w8 = (8 + lift) * nc
+            if lift:
+                tt(T.dd[:, h, 0:64], T.pen[:, sc, 0:8], T.pen[:, sc, 1:9], A.subtract, 64, ["pen" + H, "pz0"], ["dd" + H])
+                aff(CFG["de"], T.dd[:, h, 64:72], T.dead[:, 8 * c0 + 7:8 * (c0 + nc):8], -16.0, 0.0, 8, ["dead" + H], ["de" + H])
+            for _, r0, per in pieces(CFG["per"][h]):
+                pf, fk = T["pf%d" % (nf % 3)], ["pf%d" % (nf % 3)]
+                rs = list(range(r0, r0 + per))
+                if lift:
+                    mm([[(pf[:, :, r - r0], mat(T.ST, r), T.dd[:, h], w8)] for r in rs],
+                       ["dd" + H, "de" + H] + ["ST%d" % r for r in rs], fk, fk)
                 else:
-                    gat("s", T.gb[:, s16], W[:, 0:XW], T.hU[:, a:a + n], 16 * n, ["hU" + U, XR], ["gb%d" % a])
-                    pf, fk = T["pf%d" % x][:, 0:16 * n], ["pf%d" % x]
-                    mm([[(pf, IDp, pi, 16 * n), (pf, IDp, T.gb[:, s16], 16 * n)]], ["gb%d" % a, "ID0"] + keys("pi", a, n), fk, fk)
-                    aff(e2, T.gc2[:, s16], pf, 0.5, 191.75, 16 * n, fk, ["gc%d" % a], pk=fk)
-                aff(e3, av, T.gc2[:, s16], 1.0, -192.0, 16 * n, ["gc%d" % a], ["av%d" % a], half=True)
-
-        def allp(name):
-            return [name + str(u) for u, _, _ in TP]
-        if t + 1 < RO:
-            mm([[(T.pa[:, 64:96], mat(T.BK, 4), T.stT[:], 32)]], allp("stT") + ["BK4"], ["pA"], ["pa"])
-            act(T.zj[:, 512:544], T.pa[:, 64:96], F.Identity, 40, ["pA"], ["A0"], ["pa"], accum_out=T.thr[:, 1:2])
-            cp("v", T.aI[:, 0:1], T.thr[:, 1:2], 1, ["A0"], ["A1"])
-            ts(T.aI[:, 1:2], T.aI[:, 0:1], 7, None, A.bitwise_and, None, 1, ["A1"], ["A2"])
-            ts(T.thr[:, 0:1], T.aI[:, 1:2], 14.0, None, A.add, None, 1, ["A2"], ["thr"])
-        tt(T.key[:, 32:64], T.key[:, 0:32], sm[:, 0:32], A.max, 32, allp("k0") + ["fb"], ["k1"])
-        add("v", 64, lambda e: e.transpose(T.key[:, 64:96], T.key[:, 32:64]), ["k1"], ["k2"])
-        scan(T.key[:, 32:64], T.rst[:, 0:32], T.key[:, 64:96], 0.0, A.max, 32, ["k2", "rst"], ["k1"])
-        cp("v", T.goI[:, 0:4], T.key[:, 39:64:8], 4, ["k1"], ["g0"])
-        ts(T.goI[:, 4:8], T.goI[:, 0:4], 1023, None, A.bitwise_and, None, 4, ["g0"], ["g1"])
-        cp("v", T.goF[:], T.goI[:, 4:8], 4, ["g1"], ["g2"])
+                    mm([[(pf[:, 0:64, r - r0], IDp, T.m[:, e0 + r:e1:16], w8),
+                         (pf[:, 0:64, r - r0], mat(T.ST, r), T.pen[:, sc, 1:9], w8)] for r in rs],
+                       ["m" + H, "pen" + H, "ID0"] + ["ST%d" % r for r in rs], fk, fk)
+                for r in rs:
+                    if lift:
+                        scan(T.SO[:, s8, r], pf[:, 0:64, r - r0], T.m[:, e0 + r:e1:16], 0.0, A.add, A.max, 64, ["m" + H] + fk, ["SO%d_" % r + H], fk)
+                    else:
+                        scan(T.SO[:, s8, r], T.rst[:, 0:64], pf[:, 0:64, r - r0], 0.0, A.mult, A.max, 64, ["rst"] + fk, ["SO%d_" % r + H], fk)
+                if lift:
+                    end = T.SO[:, 8 * c0 + 7:8 * (c0 + nc):8, r0:r0 + per]
+                    kk = ["SO%d_" % r + H for r in rs]
+                    tt(end, end, pf[:, 64:72, 0:per], A.add, 8 * per, kk + fk, ["dn" + H] + kk, fk)
+                nf += 1
+            cp(CFG["pic"][h], third(2, c0, nc), T.SO[:, 8 * c0 + 7:8 * (c0 + nc):8, :], 16 * nc,
+               ["SO%d_" % r + H for r in range(16)], ["pi" + H], half=True)
+        PIK = keys("pi")
+        cp("g", W[:, 0:PAD], W[:, XW:XW + PAD], PAD, [XR] + keys("pi", 0, 24), ["Wq"])
+        if CFG["sh"] == "s":
+            act(hH[:, 32:64], T.sc1[:, 7:256:8], F.Relu, 32, keys("sc1"), ["subH"], bias=-KA)
+        else:
+            ts(hH[:, 32:64], T.sc1[:, 7:256:8], -KA, 0.0, A.add, A.max, 32, keys("sc1"), ["subH"])
+        pn, pk_, pu = T.pc1[:, 1, 0:4], T.pc0[:, 1, 0:4], T.pa[:, 128:160]
+        mm([[(pn, mat(T.BK, 1), T.dead[:, i:256:8], 32) for i in range(7)]], keys("dead") + ["BK1"], ["cnt"], ["pc1"], True, False)
+        mm([[(pn, mat(T.BK, 0), T.pen[:, :, 1 + i], 32) for i in range(7)]], keys("pen") + ["BK0"], ["cnu", "cnt"], ["pc1"], False, True)
+        ts(T.stT[:], pn, T.thr[:, 0:1], BIG, A.is_gt, A.mult, 32, ["cnt", "thr"], ["stT"], ["pc1"])
+        mm([[(pu, IDp, T.kc[:, 0:32], 32), (pu, IDp, T.kc[:, 32:64], 32)]], ["kU", "k16", "ID0"], ["U"], ["pa"], True, False)
+        mm([[(pk_, IDp, T.kc[:, 64:96], 32), (pk_, IH, hH[:, 32:64], 32)]], ["kj", "subH", "ID0", "IH"], ["key"], ["pc0"], True, False)
         for q in range(4):
-            aff("s", T.goH[:, q:16:4], T.goF[:], col(12 + q), 0.0, 4, ["g2", "qm"], ["gh%d" % q])
+            rs = range(4 * q, 4 * q + 4)
+            kk = [x for r in rs for x in keys("SO%d_" % r)]
+            mm([[(pu, bview(T.Bw, r), T.SO[:, 7:256:8, r], 32) for r in rs]], kk + ["Bw"], ["U"], ["pa"], False, q == 3)
+            mm([[(pk_, bview(T.B8, r), T.SO[:, 7:256:8, r], 32) for r in rs]], kk + ["B8"], ["key"], ["pc0"], False, q == 3)
+            if q == 1:
+                mm([[(pk_, IDn, T.stT[:], 32)]], ["stT", "ID1"], ["key"], ["pc0"], False, False)
+        ts(T.rb[:], pu, -1039.5, None, A.add, None, 32, ["U"], ["rb"], ["pa"])
+        tt(sm[:, 32:64], pu, T.rb[:], A.subtract, 32, ["U", "rb"], ["y"], ["pa"])
+        tt(hI[:, 0:32], sm[:, 32:64], sm[:, 32:64], A.mult, 32, ["y"], ["h0"])
+        ts(hI[:, 32:64], hI[:, 0:32], 5, 2047, A.arith_shift_right, A.bitwise_and, 32, ["h0"], ["h1"])
+        ts(T.hU[:], hI[:, 32:64], 8.0, None, A.add, None, 32, ["h1"], ["hU"])
+        ts(hI[:, 64:96], hI[:, 32:64], 2040.0, None, A.add, None, 32, ["h1"], ["h2"])
+        ts(hI[:, 96:128], hI[:, 64:96], 2047, None, A.bitwise_and, None, 32, ["h2"], ["h3"])
+        cp("v", hH[:, 0:32], hI[:, 96:128], 32, ["h3"], ["hH"])
+        ts(hH[:, 64:96], pk_, KA, None, A.is_gt, None, 32, ["key"], ["sf"], ["pc0"])
+        pq = T.pd0[:, 0]
+        XH = T.X[:, 0:PAD + XW]
+        dks = pieces(CFG["dk"])
+        mm([[(T.pd0[:, 0, :, b:8:2], toP[b], hH[:, 64:96], 32) for b in range(2)]], ["sf"] + KC, ["KD", "pd0"], ["pd0"], True, False)
+        if CFG["kd"] == "max":
+            mm([[(pq, bview(T.Bm, j), TW[:, 3 * j + 2:1536:24], 64) for j in range(8)]], PIK + ["Bm"], ["KD"], ["pd0"], False, False)
+            gat("s", T.ak[:], XH, T.hU[:], 512, XK + ["Xq", "hU"], ["ak"])
+        for x, a, n in dks:
+            s16 = slice(16 * a, 16 * (a + n))
+            gat("v", T.dk[:, s16], XH, T.hU[:, a:a + n], 16 * n, XK + ["Xq", "hU"] + keys("pi", a, n), ["dk%d" % x],
+                third(2, a, n), A.max if CFG["kd"] == "max" else A.subtract)
+            if CFG["kd"] == "relu":
+                ts(T.ak[:, s16], T.dk[:, s16], 0.0, None, A.max, None, 16 * n, ["dk%d" % x], ["ak%d" % x], half=True)
+        DK = ["dk%d" % x for x, _, _ in dks]
+        if CFG["kd"] == "max":
+            sets = ((T.B2, T.dk, DK), (T.Bm, T.ak, ["ak"]))
+        else:
+            sets = ((T.Bm, T.dk, DK), (T.B2, T.ak, ["ak%d" % x for x, _, _ in dks]))
+        for x, (bm, buf, kk) in enumerate(sets):
+            mm([[(pq, bview(bm, j), buf[:, j:512:8], 64) for j in range(8)]], kk + ["B2", "Bm"], ["KD"], ["pd0"], False, x == 1)
+        ts(T.ask[:], pq, 1.0 + 20.5 / 512, None, A.is_gt, None, 64, ["KD", "pd0"], ["ask"], ["pd0"])
+        pz = T.pf0[:, 0:32, 0]
+        scan(T.cum[:], T.one[:], T.ask[:], 0.0, A.mult, A.add, 32, ["ask", "one"], ["cum"])
+        mm([[(pz, IDp, T.kc[:, 96:128], 32)]], ["c48", "ID0"], ["pz", "pf0"], ["pf0"], True, False)
+        mm([[(pz, mat(T.BK, 7 + b), T.ask[:, b:64:2], 32) for b in range(2)]], ["ask", "BK7", "BK8"], ["pz"], ["pf0"], False, False)
+        mm([[(pz, mat(T.BK, 3 + b), T.cum[:, b:64:2], 32) for b in range(2)]], ["cum", "BK3", "BK4"], ["pz"], ["pf0"], False, True)
+        ts(T.bU[:], pz, col(9), None, A.add, None, 32, ["pz", "pf0", "c9"], ["bU"], ["pf0"])
+        for x, a, n in pieces((16, 16)):
+            s16 = slice(16 * a, 16 * (a + n))
+            e1, e2, e3 = CFG["av"][x]
+            wr = ["hU", XR, "Wq"]
+            if e1 == "v":
+                gat("v", T.gb[:, s16], W[:, 0:PAD + XW], T.hU[:, a:a + n], 16 * n, wr + keys("pi", a, n), ["gb%d" % a], third(2, a, n), A.add)
+                aff(e2, T.gc2[:, s16], T.gb[:, s16], 0.5, 191.75, 16 * n, ["gb%d" % a], ["gc%d" % a], half=True)
+            else:
+                gat("s", T.gb[:, s16], W[:, 0:PAD + XW], T.hU[:, a:a + n], 16 * n, wr, ["gb%d" % a])
+                pf, fk = T["pf%d" % (x + 1)][:, 0:64, 0:4], ["pf%d" % (x + 1)]
+                mm([[(pf, IDp, third(2, a, n), 16 * n), (pf, IDp, T.gb[:, s16], 16 * n)]], ["gb%d" % a, "ID0"] + keys("pi", a, n), fk, fk)
+                aff(e2, T.gc2[:, s16], pf, 0.5, 191.75, 16 * n, fk, ["gc%d" % a], pk=fk)
+            aff(e3, third(1, a, n), T.gc2[:, s16], 1.0, -192.0, 16 * n, ["gc%d" % a], ["av%d" % a], half=True)
+        tt(T.key[:, 0:32], pk_, sm[:, 0:32], A.max, 32, ["key", "fb"], ["k1"], ["pc0"])
+        add("v", 64, lambda e: e.transpose(T.key[:, 32:64], T.key[:, 0:32]), ["k1"], ["k2"])
+        scan(T.key[:, 0:32], T.rst[:, 0:32], T.key[:, 32:64], 0.0, A.mult, A.max, 32, ["k2", "rst"], ["k1"])
+        cp("v", T.goI[:, 0:4], T.key[:, 7:32:8], 4, ["k1"], ["g0"])
+        ts(T.goI[:, 4:8], T.goI[:, 0:4], 1023, None, A.bitwise_and, None, 4, ["g0"], ["g1"])
+        for q in range(4):
+            ts(T.goH[:, q:16:4], T.goI[:, 4:8], col(12 + q), None, A.mult, None, 4, ["g1", "qm"], ["gh%d" % q])
         mm([[(T.pa[:, 96:100], T.G[:, 17 - (16 * (x // 2) + x % 2):145 - (16 * (x // 2) + x % 2)], T.goH[:, 4 * x:4 * x + 4], 4) for x in range(4)]],
            ["G"] + ["gh%d" % q for q in range(4)], ["pgo"], ["pa"])
         if t + 1 < RO:
             cp("v", T.vu[:], T.pa[:, 96:100], 4, ["pgo"], ["vu"], ["pa"])
         cp("v", T.vF[:], T.pa[:, 96:100], 4, ["pgo"], ["vF"], ["pa"])
-        tt(sm[:, 224:256], hI[:, 96:128], T.pcsc[:, 0:32], A.subtract, 32, allp("h3") + ["pcsc"], ["dp"])
-        tt(T.bp[:, 0:32], sm[:, 224:256], sm[:, 128:160], A.mult, 32, ["dp"] + allp("sf"), ["bp0"])
-        tt(T.bp[:, 32:64], sm[:, 96:128], sm[:, 128:160], A.mult, 32, ["ds"] + allp("sf"), ["bp1"])
-        tt(sm[:, 352:384], T.nn[:, 64:96], hI[:, 96:128], A.subtract, 32, allp("h3") + ["nw"], ["dl"])
-        tt(T.ad[:], T.ask[:], sm[:, 352:384], A.mult, 32, allp("ask") + ["dl"], ["ad"])
-        toP, toS = [PC[0], SB[0]], [PC[1], SB[1]]
-        mm([[(T.pa[:, 224:288], PC[0], T.N1[:], 64), (T.pa[:, 224:288], SB[1], T.N1[:], 64)]
-            + [(T.pa[:, 224 + b:288:2], toP[b], T.bp[:, 0:32], 32) for b in range(2)]
-            + [(T.pa[:, 224 + b:288:2], toS[b], T.bp[:, 32:64], 32) for b in range(2)]], ["N1", "bp0", "bp1"] + KC, ["ppair"], ["pa"], True, False)
-        mm([[(T.pa[:, 224 + b:288:2], toP[b], T.ad[:], 32) for b in range(2)]], ["ad"] + KC, ["ppair"], ["pa"], False, True)
-        cp("v", T.pair[:], T.pa[:, 224:288], 64, ["ppair"], ["pair"], ["pa"])
-        add("v", 60 + 64 * 3.5, lambda e: e.tensor_copy(T.ef[:, 0:V + 64].indirect(T.soff[:, 0:4]), T.pair[:]),
-            ["pair", "soff", "ef0", "ef1", "efd"], ["ef0", "ef1", "efd"])
-        kk = [k for k in lastw if k.startswith("av")] + PIK + allp("bU") + [OLD, XK[wk]]
+        if t + 1 < RO:
+            mm([[(T.pf2[:, 0:32, 6], mat(T.BK, 2), T.stT[:], 32)]], ["stT", "BK2"], ["pA", "pf2"], ["pf2"])
+            act(T.zj[:], T.pf2[:, 0:32, 6], F.Identity, 40, ["pA", "pf2"], ["A0"], ["pf2"], accum_out=T.thr[:, 1:2])
+            cp("v", T.aI[:, 0:1], T.thr[:, 1:2], 1, ["A0"], ["A1"])
+            ts(T.aI[:, 1:2], T.aI[:, 0:1], 7, None, A.bitwise_and, None, 1, ["A1"], ["A2"])
+            ts(T.thr[:, 0:1], T.aI[:, 1:2], 14.0, None, A.add, None, 1, ["A2"], ["thr"])
+        ph, ps = T.pd1[:, 0], T.pd1[:, 1]
+        mm([[(T.pd1[:, 1, :, b:8:2], to[b], hH[:, 64:96], 32) for to in (toP, toS) for b in range(2)]], ["sf"] + KC, ["SF", "pd1"], ["pd1"])
+        mm([[(T.pd1[:, 0, :, b:8:2], to[b], hH[:, a:a + 32], 32) for to, a in ((toS, 32), (toP, 0)) for b in range(2)]],
+           ["hH", "subH"] + KC, ["HN", "pd1"], ["pd1"])
+        tt(nb[:, 0:64], ph, T.N1[:], A.subtract, 64, ["HN", "pd1", "N1"], ["df"], ["pd1"])
+        tt(nb[:, 64:128], T.nN[:, 64:128], ph, A.subtract, 64, ["HN", "pd1", "nw"], ["dl"], ["pd1"])
+        tt(nb[:, 128:192], ps, nb[:, 0:64], A.mult, 64, ["SF", "pd1", "df"], ["pr"], ["pd1"])
+        tt(nb[:, 192:256], nb[:, 128:192], T.N1[:], A.add, 64, ["pr", "N1"], ["base"])
+        tt(nb[:, 256:320], T.ask[:], nb[:, 64:128], A.mult, 64, ["ask", "dl"], ["ad"])
+        add("v", 60 + 64 * 3.5, lambda e: e.tensor_tensor(T.ef[:, 0:V + 64].indirect(T.soff[:, 0:4]), nb[:, 192:256], nb[:, 256:320], A.add),
+            ["base", "ad", "soff", "ef0", "ef1", "efd"], ["ef0", "ef1", "efd"])
+        kk = ["av0", "av16", "bU", "old", XK[wk]] + PIK
         add("n", 0, None, (), [XK[wk]])
         f = CFG["fin"]
-        gat("v", T.X[:, 512 * wk:512 * wk + 16 * f], W[:, 2048:3584], T.bU[:, 0:f], 16 * f, kk, ["Xa"])
-        gat("s", T.X[:, 512 * wk + 16 * f:512 * wk + 512], W[:, 2048:3584], T.bU[:, f:32], 512 - 16 * f, kk, ["Xb"])
+        gat("v", xcols(T.X, 512 * wk, 512 * wk + 16 * f), TW[:, 0:1536], T.bU[:, 0:f], 16 * f, kk, ["Xa"])
+        gat("s", xcols(T.X, 512 * wk + 16 * f, 512 * wk + 512), TW[:, 0:1536], T.bU[:, f:32], 512 - 16 * f, kk, ["Xb"])
         add("n", 0, None, ["Xa", "Xb"], [XK[wk]])
         send(t, True)
         if t == 3:
-            dma("y", T.yx[:, 512:2048], T.X[:, 512:2048], 393216, XK[1:], ["yx1"])
+            dma("y", T.yx[:, 512:2048], xcols(T.X, 512, 2048), 393216, XK[1:], ["yx1"])
     dma("y", T.yv[:], T.vF[:], 2048, ["vF"], ["yv"])
     dma("y", T.ye[:], T.ef[:, 0:V], 516096, ["ef0", "ef1"], ["ye"])
-    dma("s", T.yx[:, 0:512], T.X[:, 0:512], 131072, ["X0"], ["yx0"])
+    dma("s", T.yx[:, 0:512], xcols(T.X, 0, 512), 131072, ["X0"], ["yx0"])
     return ops
 
 

@@ -1,3 +1,4 @@
+import math
 import numpy as np
 from concourse.mybir import dt, AluOpType, AxisListType, ActivationFunctionType
 
@@ -9,15 +10,18 @@ SC = 8192.0
 KA = 87.5 * SC
 KD = 20.0 * SC
 BIG = float(2 ** 30)
+WHOLE = 12582912.0
 UP = 393216.0
 
 CFG = {
-    "bc": ("vvvvvvv", "vvvvggg", "vvvvggg", "vvvgggg"),
-    "hd": (8, 24), "n2": "vs", "xp": "ssss", "fin": 12, "av": ("ssv", "ssv"), "xs": ((4, "s"),) * 8,
-    "lift": (1, 1, 1, 0), "per": ((6, 5, 5), (6, 5, 5), (6, 5, 5), (6, 5, 5)), "p1": (1, 2, 2, 2), "kd": "max", "dk": (32,), "sk": "ss", "pic": "gggg", "sh": "s", "de": "v",
-    "tries": 7000, "seed": 2, "heat": 600.0, "off": {"Y0": 3000.0, "dead0": 3000.0, "sc10": 3000.0, "subU0": 3000.0, "Xsub0": 3000.0,
-                                                    "Y1": 2000.0, "dead1": 2000.0, "sc11": 2000.0, "subU1": 2000.0, "Xsub1": 2000.0},
-    "lat": 230.0, "pe": 0.55, "ga": 1.56, "so": 80.0,
+    "bc": ("vvvvvvg", "vvvvggg", "vvvgggg", "vvggggg"),
+    "hd": (8, 24), "n2": "vs", "xp": "ssss", "fin": 12, "av": ("srv", "srv"), "xs": ((4, "s"),) * 8,
+    "lift": (1, 1, 1, 0), "per": ((6, 5, 5), (6, 5, 5), (6, 5, 5), (6, 5, 5)), "p1": (1, 4, 3, 2), "kd": "max", "dk": (16, 16),
+    "sk": "ss", "pic": "gggg", "sh": "s", "de": "g", "xu": "ssss", "xg": (8, 8, 16),
+    "xb": "ssss", "cb": "pd1", "db": ("pd0", "pd1", "pa"), "sq": 3, "z": "s", "vf": "s",
+    "bc0": ("vvvvvvv", "vvvvvvv", "vvvvvgg", "vvggggg"), "upto": ("S0.1", "m1a.1", "Xs1.1"),
+    "tries": (5000, 6000, 500, 5000), "seed": 2, "heat": 300.0, "step": 500.0,
+    "lat": 240.0, "pe": 0.55, "so": 80.0, "paces": ((1.2, 1.56), (1.0, 1.3), (1.45, 1.9)),
 }
 
 
@@ -33,18 +37,18 @@ SCRATCH = {
     "pU": _sb(256, U16), "sU": _sb(224, U16), "sK": _sb(256, F32), "m": _sb(4096, B16), "Xs": _sb(3584, B16),
     "Y": _sb(256, F32), "dead": _sb(256, B16), "sc1": _sb(256, F32), "subU": _sb(32, U16), "Xsub": _sb(512, B16),
     "absd": _sb(3584, B16), "pen": _sb([32, 9], B16), "dd": _sb([4, 72], B16), "SO": _sb([256, 16], B16),
-    "hI": _sb(160, I32), "hU": _sb(32, U16), "rb": _sb(32, B16), "hH": _sb(96, F16), "dk": _sb(512, B16), "ak": _sb(512, B16),
+    "hI": _sb(64, I32), "hU": _sb(32, U16), "uU": _sb(32, U16), "uI": _sb(384, I32), "HL": _sb(128, U16), "XU": _sb(XW, B16), "rb": _sb(32, B16), "hH": _sb(128, F16), "dk": _sb(512, B16), "ak": _sb(512, B16),
     "ask": _sb(64, B16), "cum": _sb(64, B16), "sm": _sb(128, F32), "nd": _sb(384, F32), "stT": _sb(32, B16), "bU": _sb(32, U16),
     "gb": _sb(512, B16), "gc2": _sb(512, B16),
     "key": _sb(64, F32), "goI": _sb(8, I32), "goH": _sb(16, F16),
     "z": _sb(64, F32), "ne": _sb(256, B16), "so": _sb(256, B16), "zj": _sb(32, F32), "fs": _sb(16, F32), "soff": _sb(4, U16),
-    "aI": _sb(2, I32), "thr": _sb(2, F32),
+    "a8": _sb(1, B16), "thr": _sb(2, F32),
     "val": _sb(128 * 5, B16), "ix": _sb(160, B16), "ci": _sb(8, I32), "cc": _sb(32, F32),
-    "PM": _sb(128 * 9, F16), "ID": _sb(128 * 3, B16), "ST": _sb(128 * 16, B16), "BK": _sb(128 * 9, B16),
+    "PM": _sb(128 * 10, F16), "ID": _sb(128 * 4, B16), "low": _sb(256, B16), "ST": _sb(128 * 16, B16), "BK": _sb(128 * 9, B16),
     "B8": _sb(144, B16), "Bw": _sb(144, B16), "B2": _sb(144, B16), "Bm": _sb(144, B16), "G": _sb(160, F16),
     "rst": _sb(256, B16), "stp": _sb(256, B16), "one": _sb(64, B16), "kc": _sb(128, B16),
-    "nn": _sb(16, F32), "nN": _sb(128, F32), "iv": _sb(V, F32),
-    "pa": ("psum", [128, 512], F32), "pf2": ("psum", [128, 72, 7], F32),
+    "nn": _sb(16, F32), "nN": _sb(64, F32), "nH": _sb(64, F16), "iv": _sb(V, F32),
+    "pa": ("psum", [128, 8, 8, 8], F32), "pf2": ("psum", [128, 72, 7], F32),
     "pc0": ("psum", [128, 2, 32, 8], F32), "pc1": ("psum", [128, 2, 32, 8], F32),
     "pd0": ("psum", [128, 8, 8, 8], F32), "pd1": ("psum", [128, 8, 8, 8], F32),
     "pf0": ("psum", [128, 72, 7], F32), "pf1": ("psum", [128, 72, 7], F32),
@@ -96,88 +100,172 @@ def helper_program(g, core, T, topo):
             g.wait_ge(T.sem["ls%d" % k], bits(topo.mask(core, dst)))
 
 
-def plan_once(ops, succ, pr, look):
-    eng, cost, left = ops
-    n = len(eng)
-    left = list(left)
-    ready = {e: [] for e in eng}
-    for i in range(n):
-        if not left[i]:
-            ready[eng[i]].append(i)
-    est = [0.0] * n
-    at = [0.0] * n
-    free = {e: 0.0 for e in ready}
-    soon = {e: 0.0 for e in ready if ready[e]}
-    order = []
-    while soon:
-        e = min(soon, key=soon.get)
-        now, q = soon[e], ready[e]
-        i = q[0]
-        if len(q) > 1:
-            i = max([k for k in q if est[k] <= now], key=pr.get)
-            by = now + min(0.5 * cost[i], look[i])
-            i = max([k for k in q if est[k] <= by], key=pr.get)
-        q.remove(i)
-        at[i] = max(now, est[i])
-        f = free[e] = at[i] + cost[i]
-        order.append(i)
-        if q:
-            soon[e] = max(f, min([est[k] for k in q]))
-        else:
-            del soon[e]
-        for s, lag in succ[i]:
-            if f + lag > est[s]:
-                est[s] = f + lag
-            left[s] -= 1
-            if not left[s]:
-                x = eng[s]
-                ready[x].append(s)
-                soon[x] = min(soon.get(x, 1e18), max(est[s], free[x]))
-    return order, at
+def in_order(key, before, calls):
+    key = list(key)
+    for i in calls:
+        for d, _ in before[i]:
+            if key[d] >= key[i]:
+                key[i] = key[d] + 1e-3
+    return np.argsort(np.array(key), kind="stable").tolist()
+
+
+def place(seq, before, eng, cost, free):
+    end = [0.0] * len(seq)
+    starts, ends = {e: [] for e in set(eng)}, {e: [] for e in set(eng)}
+    for i in seq:
+        t = free[i]
+        for d, lag in before[i]:
+            if end[d] + lag > t:
+                t = end[d] + lag
+        c = cost[i]
+        if c:
+            s, f = starts[eng[i]], ends[eng[i]]
+            k = n = len(s)
+            while k and f[k - 1] > t:
+                k -= 1
+            while k < n and s[k] < t + c:
+                t = f[k]
+                k += 1
+            s.insert(k, t)
+            f.insert(k, t + c)
+        end[i] = t + c
+    return end
+
+
+def replay(seq, before, eng, cost):
+    end, free = [0.0] * len(seq), {e: 0.0 for e in set(eng)}
+    for i in seq:
+        t = free[eng[i]]
+        for d, lag in before[i]:
+            if end[d] + lag > t:
+                t = end[d] + lag
+        end[i] = t + cost[i]
+        if cost[i]:
+            free[eng[i]] = end[i]
+    return end
 
 
 def plan(ops):
-    n = len(ops)
-    succ = [[] for _ in ops]
+    part = middle(ops)
+    at = order_of(ops, part, None, *CFG["tries"][0:2])[1]
+    when = {(ops[i]["round"], ops[i]["kind"]): x for i, x in zip(part, at)}
+    span = when[3, "N1.1"] - when[2, "N1.1"]
+    key = [o["round"] * span + when.get((2, o["kind"]), when[2, "N1.1"] if o["round"] >= 0 else 3 * span) for o in ops]
+    for i in range(len(ops) - 1, -1, -1):
+        for d in ops[i]["dep"]:
+            if ops[d]["round"] < 0:
+                key[d] = min(key[d], key[i] - 2000.0)
+    best = order_of(ops, list(range(len(ops))), key, *CFG["tries"][2:4])
+    return best[2], best[0], best[3]
+
+
+def middle(ops):
+    take = [o["round"] in (1, 2) or (o["round"] == 3 and o["kind"] in CFG["upto"]) for o in ops]
+    for i in range(len(ops) - 1, -1, -1):
+        if take[i]:
+            for d in ops[i]["dep"]:
+                take[d] = take[d] or ops[d]["round"] == 3
+    return [i for i in range(len(ops)) if take[i]]
+
+
+def order_of(every, part, key, tries, swaps):
+    ops, n, first = [every[i] for i in part], len(part), part[0]
+    where = {x: i for i, x in enumerate(part)}
+    pred, succ = [[] for _ in ops], [[] for _ in ops]
     for i, o in enumerate(ops):
         for d, wait in o["dep"].items():
-            near = ops[d]["eng"] == o["eng"] and not wait
-            succ[d].append((i, 0.0 if near else ops[d]["lag"] + (0.0 if ops[d]["eng"] == "n" else CFG["lat"])))
-    pr = [0.0] * n
-    for i in range(n - 1, -1, -1):
-        pr[i] = ops[i]["cost"] + max([pr[s] + lag for s, lag in succ[i]] + [ops[i]["lag"]])
+            if d in where:
+                d = where[d]
+                near = ops[d]["eng"] == o["eng"] and not wait
+                lag = 0.0 if near else ops[d]["lag"] + (0.0 if ops[d]["eng"] == "n" else CFG["lat"])
+                pred[i].append((d, lag))
+                succ[d].append((i, lag))
+    eng, tail, zero = [o["eng"] for o in ops], [0.0 if first else o["lag"] for o in ops], [0.0] * n
+    costs = [[o["cost"] if o["sem"] else f * (o["cost"] + ga * o["picks"]) for o in ops] for f, ga in CFG["paces"]]
+    cost = costs[0]
+    up, down = list(range(n)), list(range(n - 1, -1, -1))
     names = sorted(set(o["kind"] for o in ops))
-    cls = [names.index(o["kind"]) for o in ops]
-    flat = ([o["eng"] for o in ops], [o["cost"] for o in ops], [len(o["dep"]) for o in ops])
+    cls = np.array([names.index(o["kind"]) for o in ops])
 
-    def run(off, look):
-        order, at = plan_once(flat, succ, {i: pr[i] + off[cls[i]] for i in range(n)}, [look[c] for c in cls])
-        return max(at[i] + o["cost"] + o["lag"] for i, o in enumerate(ops)), order, at
+    def run(key, both, bound=1e18):
+        end = place(in_order(key, pred, up), pred, eng, cost, zero)
+        if both:
+            back = place(in_order([-x for x in end], succ, down), succ, eng, cost, tail)
+            end = place(in_order([-x for x in back], pred, up), pred, eng, cost, zero)
+        if max(x + y for x, y in zip(end, tail)) > bound:
+            return [1e18]
+        at = [x - c for x, c in zip(end, cost)]
+        seq = in_order(at, pred, up)
+        spans = [max(x + y for x, y in zip(e, tail)) for e in [end] + [replay(seq, pred, eng, c) for c in costs[1:]]]
+        return sum(x / f for x, (f, _) in zip(spans, CFG["paces"])) / len(spans), at, seq, spans
+
+    def tight(got):
+        slack = -np.array(replay(got[2][::-1], succ, eng, cost)) - np.array(got[1])
+        return np.unique(cls[(slack < slack.min() + 400.0) & (np.array(cost) > 0)])
+    if key is None:
+        key = [0.0] * n
+        for i in down:
+            key[i] = min([key[s] - lag for s, lag in succ[i]] + [-tail[i]]) - cost[i]
     rng = np.random.default_rng(CFG["seed"])
-    off, look = [CFG["off"].get(x.split(".")[0], 0.0) for x in names], [250.0] * len(names)
-    best = cur = run(off, look)
-    for it in range(CFG["tries"]):
-        o2, l2 = list(off), list(look)
-        for _ in range(int(rng.integers(1, 9))):
-            k = int(rng.integers(0, len(names)))
-            o2[k] += float(rng.normal(0.0, 1500.0))
-            l2[k] = float(rng.choice([0.0, 150.0, 400.0, 900.0]))
-        got = run(o2, l2)
-        if got[0] <= cur[0] + CFG["heat"] * (1.0 - it / CFG["tries"]) * float(rng.random()):
-            cur, off, look = got, o2, l2
-            best = min(best, got)
-    for o, x in zip(ops, best[2]):
-        o["at"] = x
-    return best[1], best[0]
+    best = cur = run(key, first > 0)
+    crit = tight(cur)
+    for it in range(tries):
+        off = np.zeros(len(names))
+        m = int(rng.integers(1, 7))
+        k = np.where(rng.random(m) < 0.6, rng.choice(crit, m), rng.integers(0, len(names), m))
+        off[k] = rng.normal(0.0, CFG["step"], m) * rng.choice([1.0, 3.0])
+        got = run((np.array(cur[1]) + off[cls]).tolist(), rng.random() < 0.5, cur[3][0] + 3 * CFG["heat"])
+        if got[0] <= cur[0] + CFG["heat"] * (1.0 - it / tries) * float(rng.random()):
+            cur = got
+            crit = tight(cur)
+            if got[0] < best[0]:
+                best = got
+
+    def kept(key):
+        seq = in_order(key, pred, up)
+        ends = [replay(seq, pred, eng, c) for c in costs]
+        spans = [max(x + y for x, y in zip(e, tail)) for e in ends]
+        return sum(x / f for x, (f, _) in zip(spans, CFG["paces"])) / len(spans), [x - c for x, c in zip(ends[0], cost)], seq, spans, ends
+
+    def pairs(got):
+        prev, last, out = [-1] * n, {}, []
+        for i in got[2]:
+            prev[i] = last.get(eng[i], -1)
+            if cost[i]:
+                last[eng[i]] = i
+        for end, c in zip(got[4], costs):
+            i = int(np.argmax(np.array(end) + np.array(tail)))
+            while i >= 0:
+                by = [d for d, lag in pred[i] if end[d] + lag > end[i] - c[i] - 1e-6]
+                if not by and prev[i] >= 0:
+                    out.append((prev[i], i))
+                i = by[0] if by else prev[i]
+        return out
+    best = cur = kept(best[1])
+    pp = pairs(cur)
+    for it in range(swaps):
+        v, u = pp[int(rng.integers(0, len(pp)))]
+        far = 0.5 + float(rng.choice([0.0, 0.0, 150.0, 500.0, 1500.0])) * float(rng.random())
+        x, by = (u, cur[1][v] - cur[1][u] - far) if rng.random() < 0.5 else (v, cur[1][u] - cur[1][v] + far)
+        alike = cls == cls[x] if first or rng.random() < 0.5 else np.arange(n) == x
+        got = kept((np.array(cur[1]) + by * alike).tolist())
+        if got[0] <= cur[0] - 20.0 * (1.0 - it / swaps) * math.log(1.0 - rng.random()):
+            cur = got
+            pp = pairs(cur)
+            if got[0] < best[0]:
+                best = got
+    for o, x, c in zip(ops, best[1], cost):
+        o["at"], o["took"] = x, c
+    return best
 
 
 def build(T, topo, core, rank):
     ops = []
     lastw, readers, bank, seen = {}, {}, {}, {}
-    nd = [0]
-    PE, GA, SO = CFG["pe"], CFG["ga"], CFG["so"]
+    nd, now = [0], [-1]
+    PE, SO = CFG["pe"], CFG["so"]
 
-    def add(eng, cost, fn, r=(), w=(), pk=(), lag=0.0, sem=None):
+    def add(eng, cost, fn, r=(), w=(), pk=(), lag=0.0, sem=None, picks=0):
         i = len(ops)
         dep = {}
         w = list(w) + (["pe" + k for k in pk] if eng == "p" else [])
@@ -186,7 +274,7 @@ def build(T, topo, core, rank):
                 dep[lastw[k]] = True
         for k in w:
             for d in readers.get(k, []) + ([lastw[k]] if k in lastw else []):
-                dep[d] = dep.get(d, False) or not (eng == "p" or k in ("sendq", "ldq"))
+                dep[d] = dep.get(d, False) or not (eng == "p" or k in ("sendq", "ldq", "now", "later"))
         for k in pk:
             who, cur, prev = bank.get(k, (None, [], []))
             if who != eng:
@@ -201,7 +289,7 @@ def build(T, topo, core, rank):
             readers[k] = []
         dep.pop(i, None)
         seen[w[0]] = seen.get(w[0], 0) + 1
-        ops.append({"eng": eng, "cost": float(cost), "fn": fn, "dep": dep, "lag": float(lag), "sem": sem, "w": w,
+        ops.append({"eng": eng, "cost": float(cost), "fn": fn, "dep": dep, "lag": float(lag), "sem": sem, "w": w, "picks": picks, "round": now[0],
                     "kind": "%s.%d" % (w[0], seen[w[0]])})
 
     def vc(n, half=False):
@@ -238,11 +326,11 @@ def build(T, topo, core, rank):
 
     def gat(eng, out, win, off, n, r, w, in1=None, o=None):
         if in1 is not None:
-            add("v", 60 + GA * n, lambda e: e.tensor_tensor(out, win.indirect(off), in1, o), r, w)
+            add("v", 60, lambda e: e.tensor_tensor(out, win.indirect(off), in1, o), r, w, picks=n)
         elif eng == "v":
-            add("v", 60 + GA * n, lambda e: e.tensor_copy(out, win.indirect(off)), r, w)
+            add("v", 60, lambda e: e.tensor_copy(out, win.indirect(off)), r, w, picks=n)
         else:
-            add("s", 80 + GA * n, lambda e: e.activation(out, win.indirect(off), F.Copy), r, w)
+            add("s", 80, lambda e: e.activation(out, win.indirect(off), F.Copy), r, w, picks=n)
 
     def mm(groups, r, w, pk, first=True, last=True):
         def fn(e):
@@ -297,8 +385,9 @@ def build(T, topo, core, rank):
     LP, LS, PC, SB = [[mat(T.PM, 2 * k + b) for b in range(2)] for k in range(4)]
     KL, KC = ["PM00", "PM01", "PM10", "PM11"], ["PM20", "PM21", "PM30", "PM31"]
     toP, toS = [PC[0], SB[0]], [PC[1], SB[1]]
-    IH = mat(T.PM, 8)
+    IH, IHn = mat(T.PM, 8), mat(T.PM, 9)
     ts(IH, mat(T.val, 2), 0.0, None, A.is_equal, None, 128, ["val2"], ["IH"], half=True)
+    ts(IHn, mat(T.val, 2), 0.0, -1.0, A.is_equal, A.mult, 128, ["val2"], ["IHn"], half=True)
     for k, mask in enumerate((112, 120, 15, 7, 96)):
         ts(T.ci[:, k + 1:k + 2], T.ci[:, 0:1], mask, None, A.bitwise_and, None, 1, ["p"], ["ci%d" % k])
     ts(T.ci[:, 6:7], T.ci[:, 0:1], 3, 3, A.arith_shift_right, A.bitwise_and, 1, ["p"], ["ci5"])
@@ -315,12 +404,12 @@ def build(T, topo, core, rank):
     for buf, x, k in ((T.B8, SC, "B8"), (T.Bw, col(10), "Bw"), (T.B2, 2.0 / 512, "B2"), (T.Bm, -1.0 / 512, "Bm")):
         ts(buf[:], T.ix[:, 0:144], col(7), x, A.is_equal, A.mult, 144, ["c7", "c10", "ix"], [k], half=True)
     ts(T.G[:], T.ix[:], col(8), None, A.is_equal, None, 160, ["c8", "ix"], ["G"], half=True)
-    for k, x in enumerate((1.0, -1.0, 2.0 ** 22)):
+    for k, x in enumerate((1.0, -1.0, 2.0 ** 22, 0.5)):
         ts(mat(T.ID, k), mat(T.val, 2), 0.0, x, A.is_equal, A.mult, 128, ["val2"], ["ID%d" % k], half=True)
-    IDp, IDn, I22 = [mat(T.ID, k) for k in range(3)]
+    IDp, IDn, I22, IDh = [mat(T.ID, k) for k in range(4)]
+    fill(T.low[:], -0.5, ["low"], 256)
     for r in range(16):
-        ts(mat(T.ST, r), mat(T.val, 3), float(-r), None, A.is_equal, None, 128, ["val3"], ["ST%d" % r], half=True)
-    ts(mat(T.BK, 0), mat(T.val, 4), col(2), -1.0 / 16, A.is_equal, A.mult, 128, ["val4", "cc"], ["BK0"], half=True)
+        ts(mat(T.ST, r), mat(T.val, 3), float(-r), 16.0, A.is_equal, A.mult, 128, ["val3"], ["ST%d" % r], half=True)
     ts(mat(T.BK, 1), mat(T.val, 4), col(2), -1.0, A.is_equal, A.mult, 128, ["val4", "cc"], ["BK1"], half=True)
     fill(mat(T.BK, 2), 2.0 ** -33, ["BK2"])
     for b in range(2):
@@ -335,9 +424,15 @@ def build(T, topo, core, rank):
     fill(T.ef[:, V:V + 64], 0.0, ["efd"])
     fill(T.rst[:], 1.0, ["rst1"], 256)
     aff("s", T.rst[:, 0:256:8], T.one[:, 0:32], 0.0, 0.0, 32, ["one", "rst1"], ["rst"])
-    fill(T.stp[:], 2048.0, ["stp1"], 256)
-    aff("s", T.stp[:, 0:256:64], T.one[:, 0:4], 0.0, -2.0 ** 19, 4, ["one", "stp1"], ["stp"])
-    fill(T.pen[:, :, 0], -32.0, ["pz0"])
+    fill(T.stp[:], -2048.0, ["stp1"], 256)
+    aff("s", T.stp[:, 0:256:64], T.one[:, 0:4], 0.0, 2.0 ** 19, 4, ["one", "stp1"], ["stp"])
+    fill(T.pen[:, :, 0], -2.0, ["pz0"])
+    add("g", 160 + 256, lambda e: e.iota(T.uI[:, 0:128], [[16, 128]], 0, 1), (), ["u0"])
+    ts(T.uI[:, 128:256], T.uI[:, 0:128], col(1), None, A.subtract, None, 128, ["u0", "cc"], ["u1"])
+    ts(T.uI[:, 0:128], T.uI[:, 128:256], 32.0, None, A.add, None, 128, ["u1"], ["u0"])
+    tt(T.uI[:, 256:384], T.uI[:, 0:128], T.uI[:, 128:256], A.mult, 128, ["u0", "u1"], ["u2"])
+    ts(T.uI[:, 0:128], T.uI[:, 256:384], 5, 2047, A.arith_shift_right, A.bitwise_and, 128, ["u2"], ["u0"])
+    cp("v", T.HL[:], T.uI[:, 0:128], 128, ["u0"], ["HL"])
     fill(T.kc[:, 0:32], UP, ["kU"])
     fill(T.kc[:, 32:64], 16.0, ["k16"])
     aff("s", T.kc[:, 64:96], T.one[:, 0:32], col(25), 0.0, 32, ["one", "c25"], ["kj"])
@@ -363,7 +458,7 @@ def build(T, topo, core, rank):
             def fn(e, k=k, t=t, a=a, b=b, rs=rs, pid=pid, rid=rid, mask=mask):
                 e.remote_dma(xcols(T["W%d" % t], a, b), xcols(T.X, a, b), rs, T.sem["ls%d" % k], pid, rid, mask)
                 return None
-            add("g", 1000, fn, XK[a // 512:b // 512] + list(behind), ["sendq", "msg%d" % k], lag=(3000 + (b - a) * 4.0) * (2 - (t % 3 == 1)),
+            add("g", 1000 if k else 3000, fn, XK[a // 512:b // 512] + list(behind), ["now" if urgent else "later", "sendq", "msg%d" % k], lag=(3000 + (b - a) * 4.0) * (2 - (t % 3 == 1)),
                 sem=("ls%d" % k, bits(mask)))
 
     def arrivals(t):
@@ -399,39 +494,46 @@ def build(T, topo, core, rank):
         Ew = T.ei[:, 0:V] if t == 0 else T.ef[:, 0:V]
         XR = "XR%d" % t
         seen.clear()
+        now[0] = t
         add("x%d" % t, 0, None, ["msg%d" % k for k, x in enumerate(MSG) if x[0] == t], [XR], sem=("arr%d" % t, arrivals(t)))
         gat("v", T.N1[:], Ew, T.vu[:, 0:4], 64, EK + ["vu"], ["N1"])
-        mm([[(T.pa[:, 32:64], LS[b], T.N1[:, b:64:2], 32) for b in range(2)],
-            [(T.pa[:, 0:32], LP[b], T.N1[:, b:64:2], 32) for b in range(2)]], ["N1"] + KL, ["paL"], ["pa"])
-        cp("v", T.L[:], T.pa[:, 0:64], 64, ["paL"], ["L"], ["pa"])
-        mm([[(T.pa[:, 320:352], SB[b], T.N1[:, b:64:2], 32) for b in range(2)]], ["N1"] + KC, ["pbC"], ["pa"])
-        aff("s", sm[:, 0:32], T.pa[:, 320:352], col(16 + t), 65536.0, 32, ["pbC", "jm"], ["fb"], pk=["pa"])
-        gat("v", T.z[:], T.iv[:, 0:V], T.vu[:, 0:4], 64, ["iv", "vu"], ["z"])
+        mm([[(T.pa[:, 0, 4:8], LS[b], T.N1[:, b:64:2], 32) for b in range(2)],
+            [(T.pa[:, 0, 0:4], LP[b], T.N1[:, b:64:2], 32) for b in range(2)]], ["N1"] + KL, ["paL", "pa"], ["pa"])
+        cp("v", T.L[:], T.pa[:, 0], 64, ["paL", "pa"], ["L"], ["pa"])
+        mm([[(T.pf2[:, 0:32, 5], SB[b], T.N1[:, b:64:2], 32) for b in range(2)]], ["N1"] + KC, ["pbC", "pf2"], ["pf2"])
+        aff("s", sm[:, 0:32], T.pf2[:, 0:32, 5], col(16 + t), 65536.0, 32, ["pbC", "pf2", "jm"], ["fb"], pk=["pf2"])
+        gat(CFG["z"], T.z[:], T.iv[:, 0:V], T.vu[:, 0:4], 64, ["iv", "vu"], ["z"])
+        aff("s", T.fs[:, 12:16], T.vF[:], -2.0 ** 18, 0.0, 4, ["vF"], ["nv"])
         for q in range(4):
-            ts(T.ne[:, 64 * q:64 * q + 64], T.z[:], T.vF[:, q:q + 1], -2.0 ** 18, A.not_equal, A.mult, 64, ["z", "vF"], ["ne%d" % q])
+            act(T.ne[:, 64 * q:64 * q + 64], T.z[:], F.Abs, 64, ["z", "nv"], ["ne%d" % q], scale=2.0 ** 18, bias=T.fs[:, 12 + q:13 + q])
         tt(T.fs[:, 0:4], T.vF[:], T.nn[:, 8:12], A.add, 4, ["vF", "back"], ["f0"])
-        scan(T.so[:], T.stp[:], T.ne[:], 0.0, A.add, A.max, 128, ["stp"] + ["ne%d" % q for q in range(4)], ["so"])
-        tt(T.fs[:, 4:8], T.so[:, 63:256:64], T.fs[:, 0:4], A.add, 4, ["so", "f0"], ["f1"])
+        scan(T.so[:], T.stp[:], T.ne[:], 0.0, A.add, A.min, 128, ["stp"] + ["ne%d" % q for q in range(4)], ["so"])
+        tt(T.fs[:, 4:8], T.fs[:, 0:4], T.so[:, 63:256:64], A.subtract, 4, ["so", "f0"], ["f1"])
         tt(T.fs[:, 8:12], T.fs[:, 4:8], T.nn[:, 4:8], A.min, 4, ["f1", "dump"], ["f2"])
         cp("v", T.soff[:], T.fs[:, 8:12], 4, ["f2"], ["soff"])
-        aff("s", T.nN[:, 64:128], T.nN[:, 0:64], 1.0, 512.0 * wk, 64, ["nN"], ["nw"])
-        nf = 0
+        aff("s", T.nH[:], T.nN[:], 1.0, 512.0 * wk, 64, ["nN"], ["nw"])
+        nf, bc = 0, CFG["bc" if t else "bc0"]
+        for h, c0, nc in pieces(CFG["xg"]):
+            gat(CFG["xp"][h], T.XpB[:, 128 * c0:128 * (c0 + nc):8], Xw, T.L[:, c0:c0 + nc], 16 * nc, XK + ["L"], keys("XpB0", c0, nc))
         for h, c0, nc in CH:
             H = str(h)
             e0, e1 = 128 * c0, 128 * (c0 + nc)
-            gat(CFG["xp"][h], T.XpB[:, e0:e1:8], Xw, T.L[:, c0:c0 + nc], 16 * nc, XK + ["L"], ["XpB0" + H])
             for j in range(1, 8):
-                cp(CFG["bc"][h][j - 1], T.XpB[:, e0 + j:e1:8], T.XpB[:, e0:e1:8], 16 * nc, ["XpB0" + H], ["XpB%d" % j + H], half=True)
-        GK = ["XpB%d%d" % (j, h) for h, _, _ in CH for j in range(1, 8) if CFG["bc"][h][j - 1] == "g"]
+                cp(bc[h][j - 1], T.XpB[:, e0 + j:e1:8], T.XpB[:, e0:e1:8], 16 * nc, ["XpB0" + H], ["XpB%d" % j + H], half=True)
+        GK = ["XpB%d%d" % (j, h) for h, _, _ in CH for j in range(1, 8) if bc[h][j - 1] == "g"]
         send(t - 1, False, GK)
         add("g", 205 + 1024, lambda e, wk=wk: e.affine_select(third(0, 0, 32), xcols(T.X, 512 * wk, 512 * wk + 512), [[0, 512]], A.is_ge, 0.0, 0, 0),
             [XK[wk]] + GK, ["old"])
-        if t in (0, 4):
-            cp("g", T.X[:, 0:PAD], T.X[:, XW:XW + PAD], PAD, ["X3"] + GK, ["Xq"])
+        for x in range(4):
+            gat(CFG["xu"][x], T.XU[:, 512 * x:512 * x + 512], Xw, T.HL[:, 32 * x:32 * x + 32], 512, XK + ["HL"], ["XU%d" % x])
         for h, c0, nc in pieces(CFG["hd"]):
             H = str(h)
             sc, s8 = slice(c0, c0 + nc), slice(8 * c0, 8 * (c0 + nc))
-            gat("v" if t == 0 else CFG["n2"][h], T.N2[:, 16 * c0:16 * (c0 + nc)], Ew, T.L[:, 32 + c0:32 + c0 + nc], 16 * nc, EK + ["L"], ["N2" + H])
+            if t == 0 and h == 0:
+                gat("v", T.N2[:, 16 * c0:16 * (c0 + nc)], Ew, T.L[:, 32 + c0:32 + c0 + nc], 16 * nc, EK + ["L"], ["N2" + H])
+            else:
+                gat(CFG["n2"][h], T.N2[:, 16 * c0:16 * (c0 + nc)], T.ef[:, 0:V], T.L[:, 32 + c0:32 + c0 + nc], 16 * nc,
+                    ["ef0", "ef1", "efd", "L"], ["N2" + H])
             n2 = [T.N2[:, 16 * c0 + b:16 * (c0 + nc):2] for b in range(2)]
             pp = T.pd1[:, c0 // 8:(c0 + nc) // 8]
             mm([[(pp, PC[b], n2[b], 8 * nc) for b in range(2)]], ["N2" + H] + KC, ["pp" + H, "pd1"], ["pd1"])
@@ -460,24 +562,25 @@ def build(T, topo, core, rank):
             ts(T.dead[:, s8], pS, KA, None, A.is_lt, None, 8 * nc, ["S" + H], ["dead" + H], ["pc0"])
             scan(T.sc1[:, s8], T.dead[:, s8], T.Y[:, s8], 0.0, A.mult, A.max, 8 * nc, ["Y" + H, "dead" + H], ["sc1" + H])
             ts(T.subU[:, c0:c0 + nc], T.sc1[:, 8 * c0 + 7:8 * (c0 + nc):8], -KA, 0.0, A.add, A.max, nc, ["sc1" + H], ["subU" + H])
-            gat("s", T.Xsub[:, s16], Xw, T.subU[:, c0:c0 + nc], 16 * nc, XK + ["subU" + H], ["Xsub" + H])
+            gat(CFG["xb"][h], T.Xsub[:, s16], Xw, T.subU[:, c0:c0 + nc], 16 * nc, XK + ["subU" + H], ["Xsub" + H])
             xk = ["Xs%d" % x for x, a, n in pieces([y[0] for y in CFG["xs"]]) if a < c0 + nc and c0 < a + n]
             for x in range(2):
-                pd, dk_ = T["pd%d" % x], ["pd%d" % x]
+                dk_ = [CFG["db"][(2 * h + x) % len(CFG["db"])]]
+                pd = T[dk_[0]]
                 a0 = 112 * c0 + 448 * x
-                mm([[(pd[:, :, 0:7, :], IDp, T.Xs[:, 112 * c0 + x:112 * (c0 + nc):2], 448)]
-                    + [(pd[:, :, i, :], IDn, T.Xsub[:, 16 * c0 + x:16 * (c0 + nc):2], 64) for i in range(7)]],
-                   xk + ["Xsub" + H, "ID0", "ID1"], dk_, dk_)
+                mm([[(pd[:, :, 0:7, :], IDp, T.Xs[:, 112 * c0 + x:112 * (c0 + nc):2], 448)]], xk + ["ID0"], dk_, dk_, True, False)
+                mm([[(pd[:, :, i, :], IDn, T.Xsub[:, 16 * c0 + x:16 * (c0 + nc):2], 64) for i in range(7)]],
+                   ["Xsub" + H, "ID1"], dk_, dk_, False, True)
                 act(T.absd[:, a0:a0 + 448], pd[:, :, 0:7, :], F.Abs, 448, dk_, ["absd%d" % x + H], dk_)
                 mm([[(pD, I22, T.dead[:, s8], 8 * nc)][:1 - x]
                     + [(T.pc1[:, 0, sc, 0:7], bview(T.B8, 2 * r + x), T.absd[:, a0 + r:a0 + 448:8], 7 * nc) for r in range(8)]],
                    ["dead" + H, "ID2", "B8", "absd%d" % x + H], ["D" + H], ["pc1"], x == 0, x == 1)
-            ts(T.pen[:, sc, 1:9], pD, KD, -16.0, A.is_gt, A.mult, 8 * nc, ["D" + H], ["pen" + H], ["pc1"])
+            ts(T.pen[:, sc, 1:9], pD, KD, -1.0, A.is_gt, A.mult, 8 * nc, ["D" + H], ["pen" + H], ["pc1"])
             lift = CFG["lift"][h]
             w8 = (8 + lift) * nc
             if lift:
                 tt(T.dd[:, h, 0:64], T.pen[:, sc, 0:8], T.pen[:, sc, 1:9], A.subtract, 64, ["pen" + H, "pz0"], ["dd" + H])
-                aff(CFG["de"], T.dd[:, h, 64:72], T.dead[:, 8 * c0 + 7:8 * (c0 + nc):8], -16.0, 0.0, 8, ["dead" + H], ["de" + H])
+                cp(CFG["de"], T.dd[:, h, 64:72], T.dead[:, 8 * c0 + 7:8 * (c0 + nc):8], 8, ["dead" + H], ["de" + H])
             for _, r0, per in pieces(CFG["per"][h]):
                 pf, fk = T["pf%d" % (nf % 3)], ["pf%d" % (nf % 3)]
                 rs = list(range(r0, r0 + per))
@@ -496,7 +599,7 @@ def build(T, topo, core, rank):
                 if lift:
                     end = T.SO[:, 8 * c0 + 7:8 * (c0 + nc):8, r0:r0 + per]
                     kk = ["SO%d_" % r + H for r in rs]
-                    tt(end, end, pf[:, 64:72, 0:per], A.add, 8 * per, kk + fk, ["dn" + H] + kk, fk)
+                    tt(end, end, pf[:, 64:72, 0:per], A.subtract, 8 * per, kk + fk, ["dn" + H] + kk, fk)
                 nf += 1
             cp(CFG["pic"][h], third(2, c0, nc), T.SO[:, 8 * c0 + 7:8 * (c0 + nc):8, :], 16 * nc,
                ["SO%d_" % r + H for r in range(16)], ["pi" + H], half=True)
@@ -506,38 +609,40 @@ def build(T, topo, core, rank):
             act(hH[:, 32:64], T.sc1[:, 7:256:8], F.Relu, 32, keys("sc1"), ["subH"], bias=-KA)
         else:
             ts(hH[:, 32:64], T.sc1[:, 7:256:8], -KA, 0.0, A.add, A.max, 32, keys("sc1"), ["subH"])
-        pn, pk_, pu = T.pc1[:, 1, 0:4], T.pc0[:, 1, 0:4], T.pa[:, 128:160]
-        mm([[(pn, mat(T.BK, 1), T.dead[:, i:256:8], 32) for i in range(7)]], keys("dead") + ["BK1"], ["cnt"], ["pc1"], True, False)
-        mm([[(pn, mat(T.BK, 0), T.pen[:, :, 1 + i], 32) for i in range(7)]], keys("pen") + ["BK0"], ["cnu", "cnt"], ["pc1"], False, True)
-        ts(T.stT[:], pn, T.thr[:, 0:1], BIG, A.is_gt, A.mult, 32, ["cnt", "thr"], ["stT"], ["pc1"])
-        mm([[(pu, IDp, T.kc[:, 0:32], 32), (pu, IDp, T.kc[:, 32:64], 32)]], ["kU", "k16", "ID0"], ["U"], ["pa"], True, False)
+        cb = [CFG["cb"]]
+        pn, pk_, pu = T.pd1[:, 4, 0:4] if cb == ["pd1"] else T.pc1[:, 1, 0:4], T.pc0[:, 1, 0:4], T.pa[:, 2, 0:4]
+        mm([[(pn, mat(T.BK, 1), T.dead[:, i:256:8], 32) for i in range(7)]], keys("dead") + ["BK1"], ["cnt"] + cb, cb, True, False)
+        mm([[(pn, mat(T.BK, 1), T.pen[:, :, 1 + i], 32) for i in range(7)]], keys("pen") + ["BK1"], ["cnu", "cnt"], cb, False, True)
+        ts(T.stT[:], pn, T.thr[:, 0:1], BIG, A.is_gt, A.mult, 32, ["cnt", "thr"] + cb, ["stT"], cb)
+        mm([[(pu, IDp, T.kc[:, 0:32], 32), (pu, IDp, T.kc[:, 32:64], 32)]], ["kU", "k16", "ID0"], ["U", "pa"], ["pa"], True, False)
         mm([[(pk_, IDp, T.kc[:, 64:96], 32), (pk_, IH, hH[:, 32:64], 32)]], ["kj", "subH", "ID0", "IH"], ["key"], ["pc0"], True, False)
         for q in range(4):
             rs = range(4 * q, 4 * q + 4)
             kk = [x for r in rs for x in keys("SO%d_" % r)]
             mm([[(pu, bview(T.Bw, r), T.SO[:, 7:256:8, r], 32) for r in rs]], kk + ["Bw"], ["U"], ["pa"], False, q == 3)
-            mm([[(pk_, bview(T.B8, r), T.SO[:, 7:256:8, r], 32) for r in rs]], kk + ["B8"], ["key"], ["pc0"], False, q == 3)
-            if q == 1:
-                mm([[(pk_, IDn, T.stT[:], 32)]], ["stT", "ID1"], ["key"], ["pc0"], False, False)
-        ts(T.rb[:], pu, -1039.5, None, A.add, None, 32, ["U"], ["rb"], ["pa"])
-        tt(sm[:, 32:64], pu, T.rb[:], A.subtract, 32, ["U", "rb"], ["y"], ["pa"])
+            mm([[(pk_, bview(T.B8, r), T.SO[:, 7:256:8, r], 32) for r in rs]], kk + ["B8"], ["key"], ["pc0"], False, q == 3 and CFG["sq"] < 3)
+            if q == CFG["sq"]:
+                mm([[(pk_, IDn, T.stT[:], 32)]], ["stT", "ID1"], ["key"], ["pc0"], False, q == 3)
+        ts(T.rb[:], pu, -1039.5, None, A.add, None, 32, ["U", "pa"], ["rb"], ["pa"])
+        tt(sm[:, 32:64], pu, T.rb[:], A.subtract, 32, ["U", "pa", "rb"], ["y"], ["pa"])
+        ts(T.uU[:], sm[:, 32:64], -16.0, None, A.add, None, 32, ["y"], ["uU"])
         tt(hI[:, 0:32], sm[:, 32:64], sm[:, 32:64], A.mult, 32, ["y"], ["h0"])
         ts(hI[:, 32:64], hI[:, 0:32], 5, 2047, A.arith_shift_right, A.bitwise_and, 32, ["h0"], ["h1"])
         ts(T.hU[:], hI[:, 32:64], 8.0, None, A.add, None, 32, ["h1"], ["hU"])
-        ts(hI[:, 64:96], hI[:, 32:64], 2040.0, None, A.add, None, 32, ["h1"], ["h2"])
-        ts(hI[:, 96:128], hI[:, 64:96], 2047, None, A.bitwise_and, None, 32, ["h2"], ["h3"])
-        cp("v", hH[:, 0:32], hI[:, 96:128], 32, ["h3"], ["hH"])
+        ts(hH[:, 0:32], hI[:, 32:64], -8.0, None, A.add, None, 32, ["h1"], ["hH"])
+        ts(hH[:, 96:128], hI[:, 32:64], 8.0, 2048.0, A.is_lt, A.mult, 32, ["h1"], ["hW"])
         ts(hH[:, 64:96], pk_, KA, None, A.is_gt, None, 32, ["key"], ["sf"], ["pc0"])
         pq = T.pd0[:, 0]
-        XH = T.X[:, 0:PAD + XW]
+        XH, UK = T.XU[:, 0:XW], ["XU0", "XU1", "XU2", "XU3", "uU"]
         dks = pieces(CFG["dk"])
-        mm([[(T.pd0[:, 0, :, b:8:2], toP[b], hH[:, 64:96], 32) for b in range(2)]], ["sf"] + KC, ["KD", "pd0"], ["pd0"], True, False)
         if CFG["kd"] == "max":
-            mm([[(pq, bview(T.Bm, j), TW[:, 3 * j + 2:1536:24], 64) for j in range(8)]], PIK + ["Bm"], ["KD"], ["pd0"], False, False)
-            gat("s", T.ak[:], XH, T.hU[:], 512, XK + ["Xq", "hU"], ["ak"])
+            mm([[(pq, bview(T.Bm, j), TW[:, 3 * j + 2:1536:24], 64) for j in range(8)]], PIK + ["Bm"], ["KD", "pd0"], ["pd0"], True, False)
+        mm([[(T.pd0[:, 0, :, b:8:2], toP[b], hH[:, 64:96], 32) for b in range(2)]], ["sf"] + KC, ["KD", "pd0"], ["pd0"], CFG["kd"] != "max", False)
+        if CFG["kd"] == "max":
+            gat("s", T.ak[:], XH, T.uU[:], 512, UK, ["ak"])
         for x, a, n in dks:
             s16 = slice(16 * a, 16 * (a + n))
-            gat("v", T.dk[:, s16], XH, T.hU[:, a:a + n], 16 * n, XK + ["Xq", "hU"] + keys("pi", a, n), ["dk%d" % x],
+            gat("v", T.dk[:, s16], XH, T.uU[:, a:a + n], 16 * n, UK + keys("pi", a, n), ["dk%d" % x],
                 third(2, a, n), A.max if CFG["kd"] == "max" else A.subtract)
             if CFG["kd"] == "relu":
                 ts(T.ak[:, s16], T.dk[:, s16], 0.0, None, A.max, None, 16 * n, ["dk%d" % x], ["ak%d" % x], half=True)
@@ -565,7 +670,13 @@ def build(T, topo, core, rank):
             else:
                 gat("s", T.gb[:, s16], W[:, 0:PAD + XW], T.hU[:, a:a + n], 16 * n, wr, ["gb%d" % a])
                 pf, fk = T["pf%d" % (x + 1)][:, 0:64, 0:4], ["pf%d" % (x + 1)]
-                mm([[(pf, IDp, third(2, a, n), 16 * n), (pf, IDp, T.gb[:, s16], 16 * n)]], ["gb%d" % a, "ID0"] + keys("pi", a, n), fk, fk)
+                if e2 == "r":
+                    mm([[(pf, IDh, T.low[:], 16 * n), (pf, IDh, third(2, a, n), 16 * n)]], ["low", "ID3"] + keys("pi", a, n), fk, fk, True, False)
+                    mm([[(pf, IDh, T.gb[:, s16], 16 * n)]], ["gb%d" % a, "ID3"], fk, fk, False, True)
+                    ts(third(1, a, n), pf, WHOLE, -WHOLE, A.add, A.add, 16 * n, fk, ["av%d" % a], fk)
+                    continue
+                mm([[(pf, IDp, third(2, a, n), 16 * n)]], ["ID0"] + keys("pi", a, n), fk, fk, True, False)
+                mm([[(pf, IDp, T.gb[:, s16], 16 * n)]], ["gb%d" % a, "ID0"], fk, fk, False, True)
                 aff(e2, T.gc2[:, s16], pf, 0.5, 191.75, 16 * n, fk, ["gc%d" % a], pk=fk)
             aff(e3, third(1, a, n), T.gc2[:, s16], 1.0, -192.0, 16 * n, ["gc%d" % a], ["av%d" % a], half=True)
         tt(T.key[:, 0:32], pk_, sm[:, 0:32], A.max, 32, ["key", "fb"], ["k1"], ["pc0"])
@@ -575,27 +686,29 @@ def build(T, topo, core, rank):
         ts(T.goI[:, 4:8], T.goI[:, 0:4], 1023, None, A.bitwise_and, None, 4, ["g0"], ["g1"])
         for q in range(4):
             ts(T.goH[:, q:16:4], T.goI[:, 4:8], col(12 + q), None, A.mult, None, 4, ["g1", "qm"], ["gh%d" % q])
-        mm([[(T.pa[:, 96:100], T.G[:, 17 - (16 * (x // 2) + x % 2):145 - (16 * (x // 2) + x % 2)], T.goH[:, 4 * x:4 * x + 4], 4) for x in range(4)]],
-           ["G"] + ["gh%d" % q for q in range(4)], ["pgo"], ["pa"])
+        pg = T.pa[:, 3, 0, 0:4]
+        mm([[(pg, T.G[:, 17 - (16 * (x // 2) + x % 2):145 - (16 * (x // 2) + x % 2)], T.goH[:, 4 * x:4 * x + 4], 4) for x in range(4)]],
+           ["G"] + ["gh%d" % q for q in range(4)], ["pgo", "pa"], ["pa"])
         if t + 1 < RO:
-            cp("v", T.vu[:], T.pa[:, 96:100], 4, ["pgo"], ["vu"], ["pa"])
-        cp("v", T.vF[:], T.pa[:, 96:100], 4, ["pgo"], ["vF"], ["pa"])
+            cp("v", T.vu[:], pg, 4, ["pgo", "pa"], ["vu"], ["pa"])
+        cp(CFG["vf"], T.vF[:], pg, 4, ["pgo", "pa"], ["vF"], ["pa"])
         if t + 1 < RO:
             mm([[(T.pf2[:, 0:32, 6], mat(T.BK, 2), T.stT[:], 32)]], ["stT", "BK2"], ["pA", "pf2"], ["pf2"])
-            act(T.zj[:], T.pf2[:, 0:32, 6], F.Identity, 40, ["pA", "pf2"], ["A0"], ["pf2"], accum_out=T.thr[:, 1:2])
-            cp("v", T.aI[:, 0:1], T.thr[:, 1:2], 1, ["A0"], ["A1"])
-            ts(T.aI[:, 1:2], T.aI[:, 0:1], 7, None, A.bitwise_and, None, 1, ["A1"], ["A2"])
-            ts(T.thr[:, 0:1], T.aI[:, 1:2], 14.0, None, A.add, None, 1, ["A2"], ["thr"])
-        ph, ps = T.pd1[:, 0], T.pd1[:, 1]
-        mm([[(T.pd1[:, 1, :, b:8:2], to[b], hH[:, 64:96], 32) for to in (toP, toS) for b in range(2)]], ["sf"] + KC, ["SF", "pd1"], ["pd1"])
-        mm([[(T.pd1[:, 0, :, b:8:2], to[b], hH[:, a:a + 32], 32) for to, a in ((toS, 32), (toP, 0)) for b in range(2)]],
-           ["hH", "subH"] + KC, ["HN", "pd1"], ["pd1"])
-        tt(nb[:, 0:64], ph, T.N1[:], A.subtract, 64, ["HN", "pd1", "N1"], ["df"], ["pd1"])
-        tt(nb[:, 64:128], T.nN[:, 64:128], ph, A.subtract, 64, ["HN", "pd1", "nw"], ["dl"], ["pd1"])
-        tt(nb[:, 128:192], ps, nb[:, 0:64], A.mult, 64, ["SF", "pd1", "df"], ["pr"], ["pd1"])
-        tt(nb[:, 192:256], nb[:, 128:192], T.N1[:], A.add, 64, ["pr", "N1"], ["base"])
-        tt(nb[:, 256:320], T.ask[:], nb[:, 64:128], A.mult, 64, ["ask", "dl"], ["ad"])
-        add("v", 60 + 64 * 3.5, lambda e: e.tensor_tensor(T.ef[:, 0:V + 64].indirect(T.soff[:, 0:4]), nb[:, 192:256], nb[:, 256:320], A.add),
+            act(T.zj[:], T.pf2[:, 0:32, 6], F.Identity, 40, ["pA", "pf2"], ["A0"], ["pf2"], bias=1294.0 / 32, accum_out=T.thr[:, 1:2])
+            aff("s", T.a8[:], T.thr[:, 1:2], 1.0, -17.5, 1, ["A0"], ["A1"])
+            aff("s", T.thr[:, 0:1], T.a8[:], -1.0, T.thr[:, 1:2], 1, ["A0", "A1"], ["thr"])
+        def halves(k, to, x):
+            return [(T.pd1[:, k, :, b:8:2], to[b], x, 32) for b in range(2)]
+        mm([halves(1, toP, hH[:, 64:96]) + halves(1, toS, hH[:, 64:96])], ["sf"] + KC, ["SF", "pd1"], ["pd1"])
+        cp("s", nb[:, 64:128], T.pd1[:, 1], 64, ["SF", "pd1"], ["sfN"], ["pd1"])
+        mm([[(T.pd1[:, 3], IH, T.N1[:], 64)]], ["N1", "IH"], ["N1p", "pd1"], ["pd1"])
+        mm([[(T.pd1[:, 0], IHn, T.N1[:], 64)] + halves(0, toS, hH[:, 32:64]) + halves(0, toP, hH[:, 0:32]) + halves(0, toP, hH[:, 96:128]),
+            [(T.pd1[:, 2], IHn, T.nH[:], 64)] + halves(2, toP, hH[:, 0:32]) + halves(2, toP, hH[:, 96:128])],
+           ["hH", "hW", "subH", "nw", "N1", "IHn"] + KC, ["HN", "pd1"], ["pd1"])
+        tt(nb[:, 128:192], nb[:, 64:128], T.pd1[:, 0], A.mult, 64, ["HN", "pd1", "sfN"], ["pr"], ["pd1"])
+        tt(nb[:, 192:256], nb[:, 128:192], T.pd1[:, 3], A.add, 64, ["pr", "N1p", "pd1"], ["base"], ["pd1"])
+        tt(nb[:, 256:320], T.ask[:], T.pd1[:, 2], A.mult, 64, ["ask", "HN", "pd1"], ["ad"], ["pd1"])
+        add("v", 60 + 64 * 3.5, lambda e: e.tensor_tensor(T.ef[:, 0:V + 64].indirect(T.soff[:, 0:4]), nb[:, 192:256], nb[:, 256:320], A.subtract),
             ["base", "ad", "soff", "ef0", "ef1", "efd"], ["ef0", "ef1", "efd"])
         kk = ["av0", "av16", "bU", "old", XK[wk]] + PIK
         add("n", 0, None, (), [XK[wk]])

import math
import numpy as np
from concourse.mybir import dt, AluOpType, AxisListType, ActivationFunctionType

A = AluOpType
F = ActivationFunctionType
V, XW, RO = 1008, 2048, 5
PAD = 16
SC = 8192.0
KA = 87.5 * SC
KD = 20.0 * SC
BIG = float(2 ** 30)
WHOLE = 12582912.0
UP = 393216.0

CFG = {
    "bc": ("vvvvvvg", "vvvvggg", "vvvgggg", "vvggggg"),
    "hd": (8, 24), "n2": "vs", "xp": "ssss", "fin": 12, "av": ("srv", "srv"), "xs": ((4, "s"),) * 8,
    "lift": (1, 1, 1, 0), "per": ((6, 5, 5), (6, 5, 5), (6, 5, 5), (6, 5, 5)), "p1": (1, 4, 3, 2), "kd": "max", "dk": (16, 16),
    "sk": "ss", "pic": "gggg", "sh": "s", "de": "g", "xu": "ssss", "xg": (8, 8, 16),
    "xb": "ssss", "cb": "pd1", "db": ("pd0", "pd1", "pa"), "sq": 3, "z": "s", "vf": "s",
    "bc0": ("vvvvvvv", "vvvvvvv", "vvvvvgg", "vvggggg"), "upto": ("S0.1", "m1a.1", "Xs1.1"),
    "tries": (5000, 6000, 500, 5000), "seed": 2, "heat": 300.0, "step": 500.0,
    "lat": 240.0, "pe": 0.55, "so": 80.0, "paces": ((1.2, 1.56), (1.0, 1.3), (1.45, 1.9)),
}


def _sb(n, d):
    return ("sbuf", [128] + (n if isinstance(n, list) else [n]), d)


F32, B16, F16, I32, U16 = "float32", "bfloat16", "float16", "int32", "uint16"
SCRATCH = {
    "ei": _sb(V, I32), "ef": _sb(V + 64, F32), "X": _sb(PAD + XW, B16), "TW": _sb(1536, B16),
    "vi": _sb(4, I32), "wi": _sb(1, I32), "vu": _sb(4, U16), "vF": _sb(4, F32),
    "N1": _sb(64, F16), "L": _sb(64, U16), "XpB": _sb(4096, B16), "N2": _sb(512, F16),
    "pU": _sb(256, U16), "sU": _sb(224, U16), "sK": _sb(256, F32), "m": _sb(4096, B16), "Xs": _sb(3584, B16),
    "Y": _sb(256, F32), "dead": _sb(256, B16), "sc1": _sb(256, F32), "subU": _sb(32, U16), "Xsub": _sb(512, B16),
    "absd": _sb(3584, B16), "pen": _sb([32, 9], B16), "dd": _sb([4, 72], B16), "SO": _sb([256, 16], B16),
    "hI": _sb(64, I32), "hU": _sb(32, U16), "uU": _sb(32, U16), "uI": _sb(384, I32), "HL": _sb(128, U16), "XU": _sb(XW, B16), "rb": _sb(32, B16), "hH": _sb(128, F16), "dk": _sb(512, B16), "ak": _sb(512, B16),
    "ask": _sb(64, B16), "cum": _sb(64, B16), "sm": _sb(128, F32), "nd": _sb(384, F32), "stT": _sb(32, B16), "bU": _sb(32, U16),
    "gb": _sb(512, B16), "gc2": _sb(512, B16),
    "key": _sb(64, F32), "goI": _sb(8, I32), "goH": _sb(16, F16),
    "z": _sb(64, F32), "ne": _sb(256, B16), "so": _sb(256, B16), "zj": _sb(32, F32), "fs": _sb(16, F32), "soff": _sb(4, U16),
    "a8": _sb(1, B16), "thr": _sb(2, F32),
    "val": _sb(128 * 5, B16), "ix": _sb(160, B16), "ci": _sb(8, I32), "cc": _sb(32, F32),
    "PM": _sb(128 * 10, F16), "ID": _sb(128 * 4, B16), "low": _sb(256, B16), "ST": _sb(128 * 16, B16), "BK": _sb(128 * 9, B16),
    "B8": _sb(144, B16), "Bw": _sb(144, B16), "B2": _sb(144, B16), "Bm": _sb(144, B16), "G": _sb(160, F16),
    "rst": _sb(256, B16), "stp": _sb(256, B16), "one": _sb(64, B16), "kc": _sb(128, B16),
    "nn": _sb(16, F32), "nN": _sb(64, F32), "nH": _sb(64, F16), "iv": _sb(V, F32),
    "pa": ("psum", [128, 8, 8, 8], F32), "pf2": ("psum", [128, 72, 7], F32),
    "pc0": ("psum", [128, 2, 32, 8], F32), "pc1": ("psum", [128, 2, 32, 8], F32),
    "pd0": ("psum", [128, 8, 8, 8], F32), "pd1": ("psum", [128, 8, 8, 8], F32),
    "pf0": ("psum", [128, 72, 7], F32), "pf1": ("psum", [128, 72, 7], F32),
}
for _t in range(RO):
    SCRATCH["W%d" % _t] = _sb(PAD + XW, B16)


def messages():
    out = [(0, 1024 * w, 1024 * w + 1024, -1) for w in range(2)]
    out.append((1, 512, 2048, -1))
    for t in range(1, RO):
        out.append((t, 512 * t - 512, 512 * t, t - 1))
        if t + 1 < RO:
            out.append((t + 1, 0, 512 * t, t - 1))
            if t < 3:
                out.append((t + 1, 512 * t + 512, 2048, t - 1))
    return out


MSG = messages()
SEMAPHORES = (["cv", "cs", "cp", "cg"] + ["d%d" % k for k in range(16)] + ["arr%d" % t for t in range(RO)]
              + ["hop%d" % k for k in range(len(MSG))] + ["ls%d" % k for k in range(len(MSG))])


def bits(x):
    return bin(x).count("1")


def route(T, topo, rank, t):
    n = len(T.cores)
    src, dst = T.cores[rank], T.cores[(rank - 1 - t % (n - 1)) % n]
    if topo.may_write(src, dst):
        return dst, None
    can = [c for c in topo.cores_of(src) if T.rank_of(c) is None and topo.may_write(c, dst)]
    near = [c for c in can if topo.die(c) == topo.die(src)]
    return dst, (near or can)[0]


def helper_program(g, core, T, topo):
    for rank in range(len(T.cores)):
        mine = [(k, x, route(T, topo, rank, x[0])[0]) for k, x in enumerate(MSG) if route(T, topo, rank, x[0])[1] == core]
        for k, (t, a, b, _), dst in mine:
            g.wait_ge(T.sem["hop%d" % k], bits(topo.mask(T.cores[rank], core)))
            rid, pid = topo.addr(dst, core)
            w = T["W%d" % t][:, PAD + a:PAD + b]
            g.remote_dma(w, w, T.sem["arr%d" % t], T.sem["ls%d" % k], pid, rid, topo.mask(core, dst))
        for k, _, dst in mine:
            g.wait_ge(T.sem["ls%d" % k], bits(topo.mask(core, dst)))


def in_order(key, before, calls):
    key = list(key)
    for i in calls:
        for d, _ in before[i]:
            if key[d] >= key[i]:
                key[i] = key[d] + 1e-3
    return np.argsort(np.array(key), kind="stable").tolist()


def place(seq, before, eng, cost, free):
    end = [0.0] * len(seq)
    starts, ends = {e: [] for e in set(eng)}, {e: [] for e in set(eng)}
    for i in seq:
        t = free[i]
        for d, lag in before[i]:
            if end[d] + lag > t:
                t = end[d] + lag
        c = cost[i]
        if c:
            s, f = starts[eng[i]], ends[eng[i]]
            k = n = len(s)
            while k and f[k - 1] > t:
                k -= 1
            while k < n and s[k] < t + c:
                t = f[k]
                k += 1
            s.insert(k, t)
            f.insert(k, t + c)
        end[i] = t + c
    return end


def replay(seq, before, eng, cost):
    end, free = [0.0] * len(seq), {e: 0.0 for e in set(eng)}
    for i in seq:
        t = free[eng[i]]
        for d, lag in before[i]:
            if end[d] + lag > t:
                t = end[d] + lag
        end[i] = t + cost[i]
        if cost[i]:
            free[eng[i]] = end[i]
    return end


def plan(ops):
    part = middle(ops)
    at = order_of(ops, part, None, *CFG["tries"][0:2])[1]
    when = {(ops[i]["round"], ops[i]["kind"]): x for i, x in zip(part, at)}
    span = when[3, "N1.1"] - when[2, "N1.1"]
    key = [o["round"] * span + when.get((2, o["kind"]), when[2, "N1.1"] if o["round"] >= 0 else 3 * span) for o in ops]
    for i in range(len(ops) - 1, -1, -1):
        for d in ops[i]["dep"]:
            if ops[d]["round"] < 0:
                key[d] = min(key[d], key[i] - 2000.0)
    best = order_of(ops, list(range(len(ops))), key, *CFG["tries"][2:4])
    return best[2], best[0], best[3]


def middle(ops):
    take = [o["round"] in (1, 2) or (o["round"] == 3 and o["kind"] in CFG["upto"]) for o in ops]
    for i in range(len(ops) - 1, -1, -1):
        if take[i]:
            for d in ops[i]["dep"]:
                take[d] = take[d] or ops[d]["round"] == 3
    return [i for i in range(len(ops)) if take[i]]


def order_of(every, part, key, tries, swaps):
    ops, n, first = [every[i] for i in part], len(part), part[0]
    where = {x: i for i, x in enumerate(part)}
    pred, succ = [[] for _ in ops], [[] for _ in ops]
    for i, o in enumerate(ops):
        for d, wait in o["dep"].items():
            if d in where:
                d = where[d]
                near = ops[d]["eng"] == o["eng"] and not wait
                lag = 0.0 if near else ops[d]["lag"] + (0.0 if ops[d]["eng"] == "n" else CFG["lat"])
                pred[i].append((d, lag))
                succ[d].append((i, lag))
    eng, tail, zero = [o["eng"] for o in ops], [0.0 if first else o["lag"] for o in ops], [0.0] * n
    costs = [[o["cost"] if o["sem"] else f * (o["cost"] + ga * o["picks"]) for o in ops] for f, ga in CFG["paces"]]
    cost = costs[0]
    up, down = list(range(n)), list(range(n - 1, -1, -1))
    names = sorted(set(o["kind"] for o in ops))
    cls = np.array([names.index(o["kind"]) for o in ops])

    def run(key, both, bound=1e18):
        end = place(in_order(key, pred, up), pred, eng, cost, zero)
        if both:
            back = place(in_order([-x for x in end], succ, down), succ, eng, cost, tail)
            end = place(in_order([-x for x in back], pred, up), pred, eng, cost, zero)
        if max(x + y for x, y in zip(end, tail)) > bound:
            return [1e18]
        at = [x - c for x, c in zip(end, cost)]
        seq = in_order(at, pred, up)
        spans = [max(x + y for x, y in zip(e, tail)) for e in [end] + [replay(seq, pred, eng, c) for c in costs[1:]]]
        return sum(x / f for x, (f, _) in zip(spans, CFG["paces"])) / len(spans), at, seq, spans

    def tight(got):
        slack = -np.array(replay(got[2][::-1], succ, eng, cost)) - np.array(got[1])
        return np.unique(cls[(slack < slack.min() + 400.0) & (np.array(cost) > 0)])
    if key is None:
        key = [0.0] * n
        for i in down:
            key[i] = min([key[s] - lag for s, lag in succ[i]] + [-tail[i]]) - cost[i]
    rng = np.random.default_rng(CFG["seed"])
    best = cur = run(key, first > 0)
    crit = tight(cur)
    for it in range(tries):
        off = np.zeros(len(names))
        m = int(rng.integers(1, 7))
        k = np.where(rng.random(m) < 0.6, rng.choice(crit, m), rng.integers(0, len(names), m))
        off[k] = rng.normal(0.0, CFG["step"], m) * rng.choice([1.0, 3.0])
        got = run((np.array(cur[1]) + off[cls]).tolist(), rng.random() < 0.5, cur[3][0] + 3 * CFG["heat"])
        if got[0] <= cur[0] + CFG["heat"] * (1.0 - it / tries) * float(rng.random()):
            cur = got
            crit = tight(cur)
            if got[0] < best[0]:
                best = got

    def kept(key):
        seq = in_order(key, pred, up)
        ends = [replay(seq, pred, eng, c) for c in costs]
        spans = [max(x + y for x, y in zip(e, tail)) for e in ends]
        return sum(x / f for x, (f, _) in zip(spans, CFG["paces"])) / len(spans), [x - c for x, c in zip(ends[0], cost)], seq, spans, ends

    def pairs(got):
        prev, last, out = [-1] * n, {}, []
        for i in got[2]:
            prev[i] = last.get(eng[i], -1)
            if cost[i]:
                last[eng[i]] = i
        for end, c in zip(got[4], costs):
            i = int(np.argmax(np.array(end) + np.array(tail)))
            while i >= 0:
                by = [d for d, lag in pred[i] if end[d] + lag > end[i] - c[i] - 1e-6]
                if not by and prev[i] >= 0:
                    out.append((prev[i], i))
                i = by[0] if by else prev[i]
        return out
    best = cur = kept(best[1])
    pp = pairs(cur)
    for it in range(swaps):
        v, u = pp[int(rng.integers(0, len(pp)))]
        far = 0.5 + float(rng.choice([0.0, 0.0, 150.0, 500.0, 1500.0])) * float(rng.random())
        x, by = (u, cur[1][v] - cur[1][u] - far) if rng.random() < 0.5 else (v, cur[1][u] - cur[1][v] + far)
        alike = cls == cls[x] if first or rng.random() < 0.5 else np.arange(n) == x
        got = kept((np.array(cur[1]) + by * alike).tolist())
        if got[0] <= cur[0] - 20.0 * (1.0 - it / swaps) * math.log(1.0 - rng.random()):
            cur = got
            pp = pairs(cur)
            if got[0] < best[0]:
                best = got
    for o, x, c in zip(ops, best[1], cost):
        o["at"], o["took"] = x, c
    return best


def build(T, topo, core, rank):
    ops = []
    lastw, readers, bank, seen = {}, {}, {}, {}
    nd, now = [0], [-1]
    PE, SO = CFG["pe"], CFG["so"]

    def add(eng, cost, fn, r=(), w=(), pk=(), lag=0.0, sem=None, picks=0):
        i = len(ops)
        dep = {}
        w = list(w) + (["pe" + k for k in pk] if eng == "p" else [])
        for k in r:
            if k in lastw:
                dep[lastw[k]] = True
        for k in w:
            for d in readers.get(k, []) + ([lastw[k]] if k in lastw else []):
                dep[d] = dep.get(d, False) or not (eng == "p" or k in ("sendq", "ldq", "now", "later"))
        for k in pk:
            who, cur, prev = bank.get(k, (None, [], []))
            if who != eng:
                cur, prev = [], cur
            for d in prev:
                dep.setdefault(d, False)
            bank[k] = (eng, cur + [i], prev)
        for k in r:
            readers.setdefault(k, []).append(i)
        for k in w:
            lastw[k] = i
            readers[k] = []
        dep.pop(i, None)
        seen[w[0]] = seen.get(w[0], 0) + 1
        ops.append({"eng": eng, "cost": float(cost), "fn": fn, "dep": dep, "lag": float(lag), "sem": sem, "w": w, "picks": picks, "round": now[0],
                    "kind": "%s.%d" % (w[0], seen[w[0]])})

    def vc(n, half=False):
        return max(64.0, n * (0.5 if half else 1.0))

    def ts(out, a, s1, s2, o0, o1, n, r, w, pk=(), half=False):
        if o1 is None:
            add("v", vc(n, half), lambda e: e.tensor_scalar(out, a, s1, None, o0), r, w, pk)
        else:
            add("v", vc(n, half), lambda e: e.tensor_scalar(out, a, s1, s2, o0, o1), r, w, pk)

    def tt(out, a, b, o, n, r, w, pk=()):
        add("v", vc(n * (1 if pk else 2)), lambda e: e.tensor_tensor(out, a, b, o), r, w, pk)

    def act(out, a, f, n, r, w, pk=(), **kw):
        add("s", SO + vc(n), lambda e: e.activation(out, a, f, **kw), r, w, pk)

    def cp(eng, out, a, n, r, w, pk=(), half=False):
        if eng == "v":
            add("v", vc(n, half), lambda e: e.tensor_copy(out, a), r, w, pk)
        elif eng == "s":
            act(out, a, F.Copy, n, r, w, pk)
        else:
            add("g", 205 + 2 * n, lambda e: e.affine_select(out, a, [[0, n]], A.is_ge, 0.0, 0, 0), r, w, pk)

    def aff(eng, out, a, scale, bias, n, r, w, half=False, pk=()):
        if eng == "v":
            ts(out, a, scale, bias, A.mult, A.add, n, r, w, pk, half=half)
        else:
            act(out, a, F.Identity, n, r, w, pk, bias=bias, scale=scale)

    def scan(out, d0, d1, ini, op0, op1, cost, r, w, pk=()):
        add("v", max(64, cost), lambda e: e.tensor_tensor_scan(out, d0, d1, ini, op0, op1), r, w, pk)

    def gat(eng, out, win, off, n, r, w, in1=None, o=None):
        if in1 is not None:
            add("v", 60, lambda e: e.tensor_tensor(out, win.indirect(off), in1, o), r, w, picks=n)
        elif eng == "v":
            add("v", 60, lambda e: e.tensor_copy(out, win.indirect(off)), r, w, picks=n)
        else:
            add("s", 80, lambda e: e.activation(out, win.indirect(off), F.Copy), r, w, picks=n)

    def mm(groups, r, w, pk, first=True, last=True):
        def fn(e):
            ins = None
            for grp in groups:
                for k, (o, l, x, _) in enumerate(grp):
                    ins = e.matmul(o, l, x, first and k == 0, last and k == len(grp) - 1)
            return ins
        add("p", PE * sum(max(64, x[3]) for grp in groups for x in grp), fn, r, w, pk, lag=60)

    def dma(eng, out, a, nbytes, r, w):
        s = "d%d" % nd[0]
        nd[0] += 1
        add(eng, 80, lambda e: e.dma_start(out, a), r, w, lag=2000 + nbytes / 200.0, sem=(s, 16))

    def iota(out, pat, cm, n, w, base=0):
        add("g", 160 + 2 * n, lambda e: e.iota(out, pat, base, cm, allow_small_or_imprecise_dtypes=True), (), w)

    def fill(ap, x, w, n=64):
        add("v", vc(n, True), lambda e: e.memset(ap, x), (), w)

    XK = ["X0", "X1", "X2", "X3"]
    Xw = T.X[:, PAD:PAD + XW]
    cc, TW = T.cc, T.TW

    def col(k):
        return cc[:, k:k + 1]

    def mat(buf, k):
        return buf[:, 128 * k:128 * k + 128]

    def xcols(buf, a, b):
        return buf[:, PAD + a:PAD + b]

    dma("s", T.vi[:], T.v0[:], 2048, (), ["vi"])
    dma("y", T.ei[:], T.e0[:], 516096, (), ["ei", "ldq"])
    dma("y", Xw, T.x0[:], 2 * 524288, (), XK + ["ldq"])
    dma("s", T.wi[:], T.wt[:], 512, (), ["wi"])

    add("g", 162, lambda e: e.iota(T.ci[:, 0:1], [[0, 1]], 0, 1), (), ["p"])
    iota(mat(T.val, 0), [[16, 8], [-1, 8], [128, 2]], -1, 128, ["val0"])
    iota(mat(T.val, 1), [[16, 8], [128, 2], [1, 8]], -1, 128, ["val1"])
    iota(T.ix[:], [[1, 160]], 0, 160, ["ix"])
    iota(mat(T.val, 2), [[1, 128]], -1, 128, ["val2"])
    iota(mat(T.val, 3), [[16, 8], [0, 16]], -1, 128, ["val3"])
    iota(mat(T.val, 4), [[8, 16], [0, 8]], 0, 128, ["val4"])
    iota(T.iv[:], [[1, V]], 0, V, ["iv"])
    iota(T.kc[:, 96:128], [[48, 32]], 0, 32, ["c48"])
    for b in range(2):
        for k, (x, off) in enumerate(((0, 7), (0, 15), (1, 0), (1, 8))):
            ts(mat(T.PM, 2 * k + b), mat(T.val, x), 128.0 * b - off, None, A.is_equal, None, 128, ["val%d" % x], ["PM%d%d" % (k, b)], half=True)
    LP, LS, PC, SB = [[mat(T.PM, 2 * k + b) for b in range(2)] for k in range(4)]
    KL, KC = ["PM00", "PM01", "PM10", "PM11"], ["PM20", "PM21", "PM30", "PM31"]
    toP, toS = [PC[0], SB[0]], [PC[1], SB[1]]
    IH, IHn = mat(T.PM, 8), mat(T.PM, 9)
    ts(IH, mat(T.val, 2), 0.0, None, A.is_equal, None, 128, ["val2"], ["IH"], half=True)
    ts(IHn, mat(T.val, 2), 0.0, -1.0, A.is_equal, A.mult, 128, ["val2"], ["IHn"], half=True)
    for k, mask in enumerate((112, 120, 15, 7, 96)):
        ts(T.ci[:, k + 1:k + 2], T.ci[:, 0:1], mask, None, A.bitwise_and, None, 1, ["p"], ["ci%d" % k])
    ts(T.ci[:, 6:7], T.ci[:, 0:1], 3, 3, A.arith_shift_right, A.bitwise_and, 1, ["p"], ["ci5"])
    cp("v", cc[:, 0:7], T.ci[:, 0:7], 7, ["p"] + ["ci%d" % k for k in range(6)], ["cc"])
    aff("s", col(7), col(1), 1.0, 15.0, 1, ["cc"], ["c7"])
    aff("s", col(11), col(5), 1.0, 17.0, 1, ["cc"], ["c11"])
    aff("s", col(8), col(4), 2.0, col(11), 1, ["cc", "c11"], ["c8"])
    aff("s", col(9), col(3), 3.0, 0.125 - 128.5 / 1024, 1, ["cc"], ["c9"])
    aff("s", col(24), col(1), 1.0, 8.0, 1, ["cc"], ["c24"])
    aff("s", col(25), col(4), -1024.0, 7168.0, 1, ["cc"], ["c25"])
    cp("v", col(10), T.wi[:], 1, ["wi"], ["c10"])
    ts(cc[:, 12:16], T.ix[:, 0:4], col(6), None, A.is_equal, None, 4, ["cc", "ix"], ["qm"])
    ts(cc[:, 16:24], T.ix[:, 0:8], col(4), None, A.is_equal, None, 8, ["cc", "ix"], ["jm"])
    for buf, x, k in ((T.B8, SC, "B8"), (T.Bw, col(10), "Bw"), (T.B2, 2.0 / 512, "B2"), (T.Bm, -1.0 / 512, "Bm")):
        ts(buf[:], T.ix[:, 0:144], col(7), x, A.is_equal, A.mult, 144, ["c7", "c10", "ix"], [k], half=True)
    ts(T.G[:], T.ix[:], col(8), None, A.is_equal, None, 160, ["c8", "ix"], ["G"], half=True)
    for k, x in enumerate((1.0, -1.0, 2.0 ** 22, 0.5)):
        ts(mat(T.ID, k), mat(T.val, 2), 0.0, x, A.is_equal, A.mult, 128, ["val2"], ["ID%d" % k], half=True)
    IDp, IDn, I22, IDh = [mat(T.ID, k) for k in range(4)]
    fill(T.low[:], -0.5, ["low"], 256)
    for r in range(16):
        ts(mat(T.ST, r), mat(T.val, 3), float(-r), 16.0, A.is_equal, A.mult, 128, ["val3"], ["ST%d" % r], half=True)
    ts(mat(T.BK, 1), mat(T.val, 4), col(2), -1.0, A.is_equal, A.mult, 128, ["val4", "cc"], ["BK1"], half=True)
    fill(mat(T.BK, 2), 2.0 ** -33, ["BK2"])
    for b in range(2):
        for k, x in ((3, 1.0), (5, -1.0)):
            ts(mat(T.BK, k + b), mat(T.val, 4), col(1 + 23 * b), x / 1024, A.is_equal, A.mult, 128, ["val4", "cc", "c24"], ["BK%d" % (k + b)], half=True)
        add("g", 461, lambda e, b=b: e.affine_select(mat(T.BK, 7 + b), mat(T.BK, 5 + b), [[-1, 128]], A.is_gt, 0.0, 8 * b, 1),
            ["BK%d" % (5 + b)], ["BK%d" % (7 + b)])
        add("g", 461, lambda e, b=b: e.affine_select(mat(T.BK, 7 + b), mat(T.BK, 7 + b), [[-1, 128]], A.not_equal, 1.375, 8 * b, 1),
            ["BK%d" % (7 + b)], ["BK%d" % (7 + b)])
    fill(T.one[:], 1.0, ["one"])
    fill(T.thr[:, 0:1], 14.0, ["thr"])
    fill(T.ef[:, V:V + 64], 0.0, ["efd"])
    fill(T.rst[:], 1.0, ["rst1"], 256)
    aff("s", T.rst[:, 0:256:8], T.one[:, 0:32], 0.0, 0.0, 32, ["one", "rst1"], ["rst"])
    fill(T.stp[:], -2048.0, ["stp1"], 256)
    aff("s", T.stp[:, 0:256:64], T.one[:, 0:4], 0.0, 2.0 ** 19, 4, ["one", "stp1"], ["stp"])
    fill(T.pen[:, :, 0], -2.0, ["pz0"])
    add("g", 160 + 256, lambda e: e.iota(T.uI[:, 0:128], [[16, 128]], 0, 1), (), ["u0"])
    ts(T.uI[:, 128:256], T.uI[:, 0:128], col(1), None, A.subtract, None, 128, ["u0", "cc"], ["u1"])
    ts(T.uI[:, 0:128], T.uI[:, 128:256], 32.0, None, A.add, None, 128, ["u1"], ["u0"])
    tt(T.uI[:, 256:384], T.uI[:, 0:128], T.uI[:, 128:256], A.mult, 128, ["u0", "u1"], ["u2"])
    ts(T.uI[:, 0:128], T.uI[:, 256:384], 5, 2047, A.arith_shift_right, A.bitwise_and, 128, ["u2"], ["u0"])
    cp("v", T.HL[:], T.uI[:, 0:128], 128, ["u0"], ["HL"])
    fill(T.kc[:, 0:32], UP, ["kU"])
    fill(T.kc[:, 32:64], 16.0, ["k16"])
    aff("s", T.kc[:, 64:96], T.one[:, 0:32], col(25), 0.0, 32, ["one", "c25"], ["kj"])
    aff("s", T.nn[:, 0:4], T.ix[:, 0:4], 16.0, col(3), 4, ["ix", "cc"], ["nn"])
    aff("s", T.nn[:, 4:8], T.nn[:, 0:4], 1.0, float(V), 4, ["nn"], ["dump"])
    aff("s", T.nn[:, 8:12], T.nn[:, 0:4], 2048.0, -2048.0 * 63, 4, ["nn"], ["back"])
    aff("s", T.nN[:, 0:64], T.ix[:, 0:64], 8.0, col(4), 64, ["ix", "cc"], ["nN"])
    cp("v", T.vu[:], T.vi[:], 4, ["vi"], ["vu"])
    cp("v", T.vF[:], T.vi[:], 4, ["vi"], ["vF"])
    for k in range(2):
        cp("v", T.ef[:, 504 * k:504 * k + 504], T.ei[:, 504 * k:504 * k + 504], 504, ["ei"], ["ef%d" % k])

    def send(after, urgent, behind=()):
        for k, (t, a, b, aft) in enumerate(MSG):
            if aft != after or (t == after + 1) != urgent:
                continue
            dst, via = route(T, topo, rank, t)
            to = dst if via is None else via
            rid, pid = topo.addr(to, core)
            mask = topo.mask(core, to)
            rs = T.sem["arr%d" % t] if via is None else T.sem["hop%d" % k]

            def fn(e, k=k, t=t, a=a, b=b, rs=rs, pid=pid, rid=rid, mask=mask):
                e.remote_dma(xcols(T["W%d" % t], a, b), xcols(T.X, a, b), rs, T.sem["ls%d" % k], pid, rid, mask)
                return None
            add("g", 1000 if k else 3000, fn, XK[a // 512:b // 512] + list(behind), ["now" if urgent else "later", "sendq", "msg%d" % k], lag=(3000 + (b - a) * 4.0) * (2 - (t % 3 == 1)),
                sem=("ls%d" % k, bits(mask)))

    def arrivals(t):
        n = len(T.cores)
        src = (rank + 1 + t % (n - 1)) % n
        via = route(T, topo, src, t)[1]
        return bits(topo.mask(T.cores[src] if via is None else via, core)) * sum(1 for x in MSG if x[0] == t)

    def bview(buf, r):
        return buf[:, 15 - r:143 - r]

    def pieces(sizes):
        out, c = [], 0
        for k, n in enumerate(sizes):
            out.append((k, c, n))
            c += n
        return out

    CH = pieces((8, 8, 8, 8))

    def keys(name, c0=0, nc=32):
        return [name + str(h) for h, a, n in CH if a < c0 + nc and c0 < a + n]

    def third(k, a, n):
        return TW[:, 48 * a + k:48 * (a + n):3]

    send(-1, True)
    sm, hI, hH, nb = T.sm, T.hI, T.hH, T.nd
    for t in range(RO):
        W = T["W%d" % t]
        wk = t % 4
        EK = ["ei"] if t == 0 else ["ef0", "ef1", "efd"]
        Ew = T.ei[:, 0:V] if t == 0 else T.ef[:, 0:V]
        XR = "XR%d" % t
        seen.clear()
        now[0] = t
        add("x%d" % t, 0, None, ["msg%d" % k for k, x in enumerate(MSG) if x[0] == t], [XR], sem=("arr%d" % t, arrivals(t)))
        gat("v", T.N1[:], Ew, T.vu[:, 0:4], 64, EK + ["vu"], ["N1"])
        mm([[(T.pa[:, 0, 4:8], LS[b], T.N1[:, b:64:2], 32) for b in range(2)],
            [(T.pa[:, 0, 0:4], LP[b], T.N1[:, b:64:2], 32) for b in range(2)]], ["N1"] + KL, ["paL", "pa"], ["pa"])
        cp("v", T.L[:], T.pa[:, 0], 64, ["paL", "pa"], ["L"], ["pa"])
        mm([[(T.pf2[:, 0:32, 5], SB[b], T.N1[:, b:64:2], 32) for b in range(2)]], ["N1"] + KC, ["pbC", "pf2"], ["pf2"])
        aff("s", sm[:, 0:32], T.pf2[:, 0:32, 5], col(16 + t), 65536.0, 32, ["pbC", "pf2", "jm"], ["fb"], pk=["pf2"])
        gat(CFG["z"], T.z[:], T.iv[:, 0:V], T.vu[:, 0:4], 64, ["iv", "vu"], ["z"])
        aff("s", T.fs[:, 12:16], T.vF[:], -2.0 ** 18, 0.0, 4, ["vF"], ["nv"])
        for q in range(4):
            act(T.ne[:, 64 * q:64 * q + 64], T.z[:], F.Abs, 64, ["z", "nv"], ["ne%d" % q], scale=2.0 ** 18, bias=T.fs[:, 12 + q:13 + q])
        tt(T.fs[:, 0:4], T.vF[:], T.nn[:, 8:12], A.add, 4, ["vF", "back"], ["f0"])
        scan(T.so[:], T.stp[:], T.ne[:], 0.0, A.add, A.min, 128, ["stp"] + ["ne%d" % q for q in range(4)], ["so"])
        tt(T.fs[:, 4:8], T.fs[:, 0:4], T.so[:, 63:256:64], A.subtract, 4, ["so", "f0"], ["f1"])
        tt(T.fs[:, 8:12], T.fs[:, 4:8], T.nn[:, 4:8], A.min, 4, ["f1", "dump"], ["f2"])
        cp("v", T.soff[:], T.fs[:, 8:12], 4, ["f2"], ["soff"])
        aff("s", T.nH[:], T.nN[:], 1.0, 512.0 * wk, 64, ["nN"], ["nw"])
        nf, bc = 0, CFG["bc" if t else "bc0"]
        for h, c0, nc in pieces(CFG["xg"]):
            gat(CFG["xp"][h], T.XpB[:, 128 * c0:128 * (c0 + nc):8], Xw, T.L[:, c0:c0 + nc], 16 * nc, XK + ["L"], keys("XpB0", c0, nc))
        for h, c0, nc in CH:
            H = str(h)
            e0, e1 = 128 * c0, 128 * (c0 + nc)
            for j in range(1, 8):
                cp(bc[h][j - 1], T.XpB[:, e0 + j:e1:8], T.XpB[:, e0:e1:8], 16 * nc, ["XpB0" + H], ["XpB%d" % j + H], half=True)
        GK = ["XpB%d%d" % (j, h) for h, _, _ in CH for j in range(1, 8) if bc[h][j - 1] == "g"]
        send(t - 1, False, GK)
        add("g", 205 + 1024, lambda e, wk=wk: e.affine_select(third(0, 0, 32), xcols(T.X, 512 * wk, 512 * wk + 512), [[0, 512]], A.is_ge, 0.0, 0, 0),
            [XK[wk]] + GK, ["old"])
        for x in range(4):
            gat(CFG["xu"][x], T.XU[:, 512 * x:512 * x + 512], Xw, T.HL[:, 32 * x:32 * x + 32], 512, XK + ["HL"], ["XU%d" % x])
        for h, c0, nc in pieces(CFG["hd"]):
            H = str(h)
            sc, s8 = slice(c0, c0 + nc), slice(8 * c0, 8 * (c0 + nc))
            if t == 0 and h == 0:
                gat("v", T.N2[:, 16 * c0:16 * (c0 + nc)], Ew, T.L[:, 32 + c0:32 + c0 + nc], 16 * nc, EK + ["L"], ["N2" + H])
            else:
                gat(CFG["n2"][h], T.N2[:, 16 * c0:16 * (c0 + nc)], T.ef[:, 0:V], T.L[:, 32 + c0:32 + c0 + nc], 16 * nc,
                    ["ef0", "ef1", "efd", "L"], ["N2" + H])
            n2 = [T.N2[:, 16 * c0 + b:16 * (c0 + nc):2] for b in range(2)]
            pp = T.pd1[:, c0 // 8:(c0 + nc) // 8]
            mm([[(pp, PC[b], n2[b], 8 * nc) for b in range(2)]], ["N2" + H] + KC, ["pp" + H, "pd1"], ["pd1"])
            mm([[(T.pc1[:, 1, sc], SB[b], n2[b], 8 * nc) for b in range(2)]], ["N2" + H] + KC, ["ps" + H, "cnt"], ["pc1"])
            cp("v", T.pU[:, s8], pp, 8 * nc, ["pp" + H, "pd1"], keys("pU", c0, nc), ["pd1"])
            cp("v", T.sU[:, 7 * c0:7 * (c0 + nc)], T.pc1[:, 1, sc, 0:7], 7 * nc, ["ps" + H], keys("sU", c0, nc), ["pc1"])
            aff(CFG["sk"][h], T.sK[:, s8], T.pc1[:, 1, sc], 1.0, KA, 8 * nc, ["ps" + H], keys("sK", c0, nc), pk=["pc1"])
        for x, a, n in pieces([y[0] for y in CFG["xs"]]):
            gat(CFG["xs"][x][1], T.Xs[:, 112 * a:112 * (a + n)], Xw, T.sU[:, 7 * a:7 * (a + n)], 112 * n, XK + keys("sU", a, n), ["Xs%d" % x])
        for h, c0, nc in CH:
            H = str(h)
            e0, e1 = 128 * c0, 128 * (c0 + nc)
            sc = slice(c0, c0 + nc)
            s8 = slice(8 * c0, 8 * (c0 + nc))
            s16 = slice(16 * c0, 16 * (c0 + nc))
            pS, pD = T.pc0[:, 0, sc], T.pc1[:, 0, sc]
            np1 = CFG["p1"][h]
            add("n", 0, None, (), ["m" + H])
            for x in range(np1):
                a, b = c0 + x * nc // np1, c0 + (x + 1) * nc // np1
                gat("v", T.m[:, 128 * a:128 * b], Xw, T.pU[:, 8 * a:8 * b], 128 * (b - a),
                    XK + ["m" + H] + ["pU" + H] + ["XpB%d" % j + H for j in range(8)], ["m" + H + "abcd"[x]], T.XpB[:, 128 * a:128 * b], A.min)
            add("n", 0, None, ["m" + H + "abcd"[x] for x in range(np1)], ["m" + H])
            mm([[(pS, bview(T.B8, r), T.m[:, e0 + r:e1:16], 8 * nc) for r in range(16)]], ["m" + H, "B8"], ["S" + H], ["pc0"])
            tt(T.Y[:, s8], T.sK[:, s8], pS, A.min, 8 * nc, ["sK" + H, "S" + H], ["Y" + H], ["pc0"])
            ts(T.dead[:, s8], pS, KA, None, A.is_lt, None, 8 * nc, ["S" + H], ["dead" + H], ["pc0"])
            scan(T.sc1[:, s8], T.dead[:, s8], T.Y[:, s8], 0.0, A.mult, A.max, 8 * nc, ["Y" + H, "dead" + H], ["sc1" + H])
            ts(T.subU[:, c0:c0 + nc], T.sc1[:, 8 * c0 + 7:8 * (c0 + nc):8], -KA, 0.0, A.add, A.max, nc, ["sc1" + H], ["subU" + H])
            gat(CFG["xb"][h], T.Xsub[:, s16], Xw, T.subU[:, c0:c0 + nc], 16 * nc, XK + ["subU" + H], ["Xsub" + H])
            xk = ["Xs%d" % x for x, a, n in pieces([y[0] for y in CFG["xs"]]) if a < c0 + nc and c0 < a + n]
            for x in range(2):
                dk_ = [CFG["db"][(2 * h + x) % len(CFG["db"])]]
                pd = T[dk_[0]]
                a0 = 112 * c0 + 448 * x
                mm([[(pd[:, :, 0:7, :], IDp, T.Xs[:, 112 * c0 + x:112 * (c0 + nc):2], 448)]], xk + ["ID0"], dk_, dk_, True, False)
                mm([[(pd[:, :, i, :], IDn, T.Xsub[:, 16 * c0 + x:16 * (c0 + nc):2], 64) for i in range(7)]],
                   ["Xsub" + H, "ID1"], dk_, dk_, False, True)
                act(T.absd[:, a0:a0 + 448], pd[:, :, 0:7, :], F.Abs, 448, dk_, ["absd%d" % x + H], dk_)
                mm([[(pD, I22, T.dead[:, s8], 8 * nc)][:1 - x]
                    + [(T.pc1[:, 0, sc, 0:7], bview(T.B8, 2 * r + x), T.absd[:, a0 + r:a0 + 448:8], 7 * nc) for r in range(8)]],
                   ["dead" + H, "ID2", "B8", "absd%d" % x + H], ["D" + H], ["pc1"], x == 0, x == 1)
            ts(T.pen[:, sc, 1:9], pD, KD, -1.0, A.is_gt, A.mult, 8 * nc, ["D" + H], ["pen" + H], ["pc1"])
            lift = CFG["lift"][h]
            w8 = (8 + lift) * nc
            if lift:
                tt(T.dd[:, h, 0:64], T.pen[:, sc, 0:8], T.pen[:, sc, 1:9], A.subtract, 64, ["pen" + H, "pz0"], ["dd" + H])
                cp(CFG["de"], T.dd[:, h, 64:72], T.dead[:, 8 * c0 + 7:8 * (c0 + nc):8], 8, ["dead" + H], ["de" + H])
            for _, r0, per in pieces(CFG["per"][h]):
                pf, fk = T["pf%d" % (nf % 3)], ["pf%d" % (nf % 3)]
                rs = list(range(r0, r0 + per))
                if lift:
                    mm([[(pf[:, :, r - r0], mat(T.ST, r), T.dd[:, h], w8)] for r in rs],
                       ["dd" + H, "de" + H] + ["ST%d" % r for r in rs], fk, fk)
                else:
                    mm([[(pf[:, 0:64, r - r0], IDp, T.m[:, e0 + r:e1:16], w8),
                         (pf[:, 0:64, r - r0], mat(T.ST, r), T.pen[:, sc, 1:9], w8)] for r in rs],
                       ["m" + H, "pen" + H, "ID0"] + ["ST%d" % r for r in rs], fk, fk)
                for r in rs:
                    if lift:
                        scan(T.SO[:, s8, r], pf[:, 0:64, r - r0], T.m[:, e0 + r:e1:16], 0.0, A.add, A.max, 64, ["m" + H] + fk, ["SO%d_" % r + H], fk)
                    else:
                        scan(T.SO[:, s8, r], T.rst[:, 0:64], pf[:, 0:64, r - r0], 0.0, A.mult, A.max, 64, ["rst"] + fk, ["SO%d_" % r + H], fk)
                if lift:
                    end = T.SO[:, 8 * c0 + 7:8 * (c0 + nc):8, r0:r0 + per]
                    kk = ["SO%d_" % r + H for r in rs]
                    tt(end, end, pf[:, 64:72, 0:per], A.subtract, 8 * per, kk + fk, ["dn" + H] + kk, fk)
                nf += 1
            cp(CFG["pic"][h], third(2, c0, nc), T.SO[:, 8 * c0 + 7:8 * (c0 + nc):8, :], 16 * nc,
               ["SO%d_" % r + H for r in range(16)], ["pi" + H], half=True)
        PIK = keys("pi")
        cp("g", W[:, 0:PAD], W[:, XW:XW + PAD], PAD, [XR] + keys("pi", 0, 24), ["Wq"])
        if CFG["sh"] == "s":
            act(hH[:, 32:64], T.sc1[:, 7:256:8], F.Relu, 32, keys("sc1"), ["subH"], bias=-KA)
        else:
            ts(hH[:, 32:64], T.sc1[:, 7:256:8], -KA, 0.0, A.add, A.max, 32, keys("sc1"), ["subH"])
        cb = [CFG["cb"]]
        pn, pk_, pu = T.pd1[:, 4, 0:4] if cb == ["pd1"] else T.pc1[:, 1, 0:4], T.pc0[:, 1, 0:4], T.pa[:, 2, 0:4]
        mm([[(pn, mat(T.BK, 1), T.dead[:, i:256:8], 32) for i in range(7)]], keys("dead") + ["BK1"], ["cnt"] + cb, cb, True, False)
        mm([[(pn, mat(T.BK, 1), T.pen[:, :, 1 + i], 32) for i in range(7)]], keys("pen") + ["BK1"], ["cnu", "cnt"], cb, False, True)
        ts(T.stT[:], pn, T.thr[:, 0:1], BIG, A.is_gt, A.mult, 32, ["cnt", "thr"] + cb, ["stT"], cb)
        mm([[(pu, IDp, T.kc[:, 0:32], 32), (pu, IDp, T.kc[:, 32:64], 32)]], ["kU", "k16", "ID0"], ["U", "pa"], ["pa"], True, False)
        mm([[(pk_, IDp, T.kc[:, 64:96], 32), (pk_, IH, hH[:, 32:64], 32)]], ["kj", "subH", "ID0", "IH"], ["key"], ["pc0"], True, False)
        for q in range(4):
            rs = range(4 * q, 4 * q + 4)
            kk = [x for r in rs for x in keys("SO%d_" % r)]
            mm([[(pu, bview(T.Bw, r), T.SO[:, 7:256:8, r], 32) for r in rs]], kk + ["Bw"], ["U"], ["pa"], False, q == 3)
            mm([[(pk_, bview(T.B8, r), T.SO[:, 7:256:8, r], 32) for r in rs]], kk + ["B8"], ["key"], ["pc0"], False, q == 3 and CFG["sq"] < 3)
            if q == CFG["sq"]:
                mm([[(pk_, IDn, T.stT[:], 32)]], ["stT", "ID1"], ["key"], ["pc0"], False, q == 3)
        ts(T.rb[:], pu, -1039.5, None, A.add, None, 32, ["U", "pa"], ["rb"], ["pa"])
        tt(sm[:, 32:64], pu, T.rb[:], A.subtract, 32, ["U", "pa", "rb"], ["y"], ["pa"])
        ts(T.uU[:], sm[:, 32:64], -16.0, None, A.add, None, 32, ["y"], ["uU"])
        tt(hI[:, 0:32], sm[:, 32:64], sm[:, 32:64], A.mult, 32, ["y"], ["h0"])
        ts(hI[:, 32:64], hI[:, 0:32], 5, 2047, A.arith_shift_right, A.bitwise_and, 32, ["h0"], ["h1"])
        ts(T.hU[:], hI[:, 32:64], 8.0, None, A.add, None, 32, ["h1"], ["hU"])
        ts(hH[:, 0:32], hI[:, 32:64], -8.0, None, A.add, None, 32, ["h1"], ["hH"])
        ts(hH[:, 96:128], hI[:, 32:64], 8.0, 2048.0, A.is_lt, A.mult, 32, ["h1"], ["hW"])
        ts(hH[:, 64:96], pk_, KA, None, A.is_gt, None, 32, ["key"], ["sf"], ["pc0"])
        pq = T.pd0[:, 0]
        XH, UK = T.XU[:, 0:XW], ["XU0", "XU1", "XU2", "XU3", "uU"]
        dks = pieces(CFG["dk"])
        if CFG["kd"] == "max":
            mm([[(pq, bview(T.Bm, j), TW[:, 3 * j + 2:1536:24], 64) for j in range(8)]], PIK + ["Bm"], ["KD", "pd0"], ["pd0"], True, False)
        mm([[(T.pd0[:, 0, :, b:8:2], toP[b], hH[:, 64:96], 32) for b in range(2)]], ["sf"] + KC, ["KD", "pd0"], ["pd0"], CFG["kd"] != "max", False)
        if CFG["kd"] == "max":
            gat("s", T.ak[:], XH, T.uU[:], 512, UK, ["ak"])
        for x, a, n in dks:
            s16 = slice(16 * a, 16 * (a + n))
            gat("v", T.dk[:, s16], XH, T.uU[:, a:a + n], 16 * n, UK + keys("pi", a, n), ["dk%d" % x],
                third(2, a, n), A.max if CFG["kd"] == "max" else A.subtract)
            if CFG["kd"] == "relu":
                ts(T.ak[:, s16], T.dk[:, s16], 0.0, None, A.max, None, 16 * n, ["dk%d" % x], ["ak%d" % x], half=True)
        DK = ["dk%d" % x for x, _, _ in dks]
        if CFG["kd"] == "max":
            sets = ((T.B2, T.dk, DK), (T.Bm, T.ak, ["ak"]))
        else:
            sets = ((T.Bm, T.dk, DK), (T.B2, T.ak, ["ak%d" % x for x, _, _ in dks]))
        for x, (bm, buf, kk) in enumerate(sets):
            mm([[(pq, bview(bm, j), buf[:, j:512:8], 64) for j in range(8)]], kk + ["B2", "Bm"], ["KD"], ["pd0"], False, x == 1)
        ts(T.ask[:], pq, 1.0 + 20.5 / 512, None, A.is_gt, None, 64, ["KD", "pd0"], ["ask"], ["pd0"])
        pz = T.pf0[:, 0:32, 0]
        scan(T.cum[:], T.one[:], T.ask[:], 0.0, A.mult, A.add, 32, ["ask", "one"], ["cum"])
        mm([[(pz, IDp, T.kc[:, 96:128], 32)]], ["c48", "ID0"], ["pz", "pf0"], ["pf0"], True, False)
        mm([[(pz, mat(T.BK, 7 + b), T.ask[:, b:64:2], 32) for b in range(2)]], ["ask", "BK7", "BK8"], ["pz"], ["pf0"], False, False)
        mm([[(pz, mat(T.BK, 3 + b), T.cum[:, b:64:2], 32) for b in range(2)]], ["cum", "BK3", "BK4"], ["pz"], ["pf0"], False, True)
        ts(T.bU[:], pz, col(9), None, A.add, None, 32, ["pz", "pf0", "c9"], ["bU"], ["pf0"])
        for x, a, n in pieces((16, 16)):
            s16 = slice(16 * a, 16 * (a + n))
            e1, e2, e3 = CFG["av"][x]
            wr = ["hU", XR, "Wq"]
            if e1 == "v":
                gat("v", T.gb[:, s16], W[:, 0:PAD + XW], T.hU[:, a:a + n], 16 * n, wr + keys("pi", a, n), ["gb%d" % a], third(2, a, n), A.add)
                aff(e2, T.gc2[:, s16], T.gb[:, s16], 0.5, 191.75, 16 * n, ["gb%d" % a], ["gc%d" % a], half=True)
            else:
                gat("s", T.gb[:, s16], W[:, 0:PAD + XW], T.hU[:, a:a + n], 16 * n, wr, ["gb%d" % a])
                pf, fk = T["pf%d" % (x + 1)][:, 0:64, 0:4], ["pf%d" % (x + 1)]
                if e2 == "r":
                    mm([[(pf, IDh, T.low[:], 16 * n), (pf, IDh, third(2, a, n), 16 * n)]], ["low", "ID3"] + keys("pi", a, n), fk, fk, True, False)
                    mm([[(pf, IDh, T.gb[:, s16], 16 * n)]], ["gb%d" % a, "ID3"], fk, fk, False, True)
                    ts(third(1, a, n), pf, WHOLE, -WHOLE, A.add, A.add, 16 * n, fk, ["av%d" % a], fk)
                    continue
                mm([[(pf, IDp, third(2, a, n), 16 * n)]], ["ID0"] + keys("pi", a, n), fk, fk, True, False)
                mm([[(pf, IDp, T.gb[:, s16], 16 * n)]], ["gb%d" % a, "ID0"], fk, fk, False, True)
                aff(e2, T.gc2[:, s16], pf, 0.5, 191.75, 16 * n, fk, ["gc%d" % a], pk=fk)
            aff(e3, third(1, a, n), T.gc2[:, s16], 1.0, -192.0, 16 * n, ["gc%d" % a], ["av%d" % a], half=True)
        tt(T.key[:, 0:32], pk_, sm[:, 0:32], A.max, 32, ["key", "fb"], ["k1"], ["pc0"])
        add("v", 64, lambda e: e.transpose(T.key[:, 32:64], T.key[:, 0:32]), ["k1"], ["k2"])
        scan(T.key[:, 0:32], T.rst[:, 0:32], T.key[:, 32:64], 0.0, A.mult, A.max, 32, ["k2", "rst"], ["k1"])
        cp("v", T.goI[:, 0:4], T.key[:, 7:32:8], 4, ["k1"], ["g0"])
        ts(T.goI[:, 4:8], T.goI[:, 0:4], 1023, None, A.bitwise_and, None, 4, ["g0"], ["g1"])
        for q in range(4):
            ts(T.goH[:, q:16:4], T.goI[:, 4:8], col(12 + q), None, A.mult, None, 4, ["g1", "qm"], ["gh%d" % q])
        pg = T.pa[:, 3, 0, 0:4]
        mm([[(pg, T.G[:, 17 - (16 * (x // 2) + x % 2):145 - (16 * (x // 2) + x % 2)], T.goH[:, 4 * x:4 * x + 4], 4) for x in range(4)]],
           ["G"] + ["gh%d" % q for q in range(4)], ["pgo", "pa"], ["pa"])
        if t + 1 < RO:
            cp("v", T.vu[:], pg, 4, ["pgo", "pa"], ["vu"], ["pa"])
        cp(CFG["vf"], T.vF[:], pg, 4, ["pgo", "pa"], ["vF"], ["pa"])
        if t + 1 < RO:
            mm([[(T.pf2[:, 0:32, 6], mat(T.BK, 2), T.stT[:], 32)]], ["stT", "BK2"], ["pA", "pf2"], ["pf2"])
            act(T.zj[:], T.pf2[:, 0:32, 6], F.Identity, 40, ["pA", "pf2"], ["A0"], ["pf2"], bias=1294.0 / 32, accum_out=T.thr[:, 1:2])
            aff("s", T.a8[:], T.thr[:, 1:2], 1.0, -17.5, 1, ["A0"], ["A1"])
            aff("s", T.thr[:, 0:1], T.a8[:], -1.0, T.thr[:, 1:2], 1, ["A0", "A1"], ["thr"])
        def halves(k, to, x):
            return [(T.pd1[:, k, :, b:8:2], to[b], x, 32) for b in range(2)]
        mm([halves(1, toP, hH[:, 64:96]) + halves(1, toS, hH[:, 64:96])], ["sf"] + KC, ["SF", "pd1"], ["pd1"])
        cp("s", nb[:, 64:128], T.pd1[:, 1], 64, ["SF", "pd1"], ["sfN"], ["pd1"])
        mm([[(T.pd1[:, 3], IH, T.N1[:], 64)]], ["N1", "IH"], ["N1p", "pd1"], ["pd1"])
        mm([[(T.pd1[:, 0], IHn, T.N1[:], 64)] + halves(0, toS, hH[:, 32:64]) + halves(0, toP, hH[:, 0:32]) + halves(0, toP, hH[:, 96:128]),
            [(T.pd1[:, 2], IHn, T.nH[:], 64)] + halves(2, toP, hH[:, 0:32]) + halves(2, toP, hH[:, 96:128])],
           ["hH", "hW", "subH", "nw", "N1", "IHn"] + KC, ["HN", "pd1"], ["pd1"])
        tt(nb[:, 128:192], nb[:, 64:128], T.pd1[:, 0], A.mult, 64, ["HN", "pd1", "sfN"], ["pr"], ["pd1"])
        tt(nb[:, 192:256], nb[:, 128:192], T.pd1[:, 3], A.add, 64, ["pr", "N1p", "pd1"], ["base"], ["pd1"])
        tt(nb[:, 256:320], T.ask[:], T.pd1[:, 2], A.mult, 64, ["ask", "HN", "pd1"], ["ad"], ["pd1"])
        add("v", 60 + 64 * 3.5, lambda e: e.tensor_tensor(T.ef[:, 0:V + 64].indirect(T.soff[:, 0:4]), nb[:, 192:256], nb[:, 256:320], A.subtract),
            ["base", "ad", "soff", "ef0", "ef1", "efd"], ["ef0", "ef1", "efd"])
        kk = ["av0", "av16", "bU", "old", XK[wk]] + PIK
        add("n", 0, None, (), [XK[wk]])
        f = CFG["fin"]
        gat("v", xcols(T.X, 512 * wk, 512 * wk + 16 * f), TW[:, 0:1536], T.bU[:, 0:f], 16 * f, kk, ["Xa"])
        gat("s", xcols(T.X, 512 * wk + 16 * f, 512 * wk + 512), TW[:, 0:1536], T.bU[:, f:32], 512 - 16 * f, kk, ["Xb"])
        add("n", 0, None, ["Xa", "Xb"], [XK[wk]])
        send(t, True)
        if t == 3:
            dma("y", T.yx[:, 512:2048], xcols(T.X, 512, 2048), 393216, XK[1:], ["yx1"])
    dma("y", T.yv[:], T.vF[:], 2048, ["vF"], ["yv"])
    dma("y", T.ye[:], T.ef[:, 0:V], 516096, ["ef0", "ef1"], ["ye"])
    dma("s", T.yx[:, 0:512], xcols(T.X, 0, 512), 131072, ["X0"], ["yx0"])
    return ops


PLAN = {}


def rank_program(g, core, T, topo):
    rank = T.rank_of(core)
    if rank is None:
        helper_program(g, core, T, topo)
        return
    ops = build(T, topo, core, rank)
    if "order" not in PLAN:
        PLAN["order"] = plan(ops)[0]
    eng = {"v": g.vector, "s": g.scalar, "p": g.tensor, "g": g, "y": g.sync}
    cnt = {"v": 0, "s": 0, "p": 0, "g": 0}
    seen = {e: {} for e in eng}
    done = {}

    def needs(o, e, need):
        for d, raw in o["dep"].items():
            p = ops[d]
            if p["eng"] == "n":
                needs({"dep": {x: True for x in p["dep"]}, "sem": o["sem"]}, e, need)
            elif p["eng"] == e and p["sem"] is None and (not raw or e == "p"):
                continue
            elif p["eng"] == e and not raw and ("sendq" in o.get("w", ()) or "ldq" in o.get("w", ())):
                continue
            else:
                s, n = done[d]
                need[s] = max(need.get(s, 0), n)
        return need

    for i in PLAN["order"]:
        o = ops[i]
        e = o["eng"]
        if o["fn"] is not None:
            for s, n in needs(o, e, {}).items():
                if seen[e].get(s, 0) < n:
                    eng[e].wait_ge(T.sem[s], n)
                    seen[e][s] = n
            ins = o["fn"](eng[e])
            if o["sem"] is None:
                cnt[e] += 1
                ins.then_inc(T.sem["c" + e], 1)
            elif ins is not None:
                ins.then_inc(T.sem[o["sem"][0]], o["sem"][1])
        if e != "n":
            done[i] = o["sem"] if o["sem"] is not None else ("c" + e, cnt[e])
    last = {"c" + e: n for e, n in cnt.items()}
    for o in ops:
        if o["sem"] is not None:
            last[o["sem"][0]] = o["sem"][1]
    for s, n in last.items():
        if n and not any(seen[e].get(s, 0) >= n for e in eng):
            g.sync.wait_ge(T.sem[s], n)
